import numpy as np
import ml_dtypes


def mxq(x, axis, fmt="e4m3"):
    dtype, down = {"e4m3": (ml_dtypes.float8_e4m3fn, 7), "e5m2": (ml_dtypes.float8_e5m2, 14)}[fmt]
    v = np.moveaxis(np.asarray(x, np.float32).astype(ml_dtypes.bfloat16).astype(np.float64), axis, -1)
    blocks = v.reshape(v.shape[:-1] + (-1, 32))
    amax = np.abs(blocks).max(-1, keepdims=True)
    byte = np.maximum(np.where(amax > 0, np.frexp(amax)[1] - 1 + 127, 0) - down, 1)
    scale = np.exp2(byte - 127.0)
    codes = (blocks / scale).astype(np.float32).astype(dtype).astype(np.float64)
    return np.moveaxis((codes * scale).reshape(v.shape), -1, axis)


WIDE = False


def mx_kscale(k):
    if not WIDE:
        return np.ones(k)
    levels = np.array([10, -10, 5, -5, 0])
    if k % 512:
        return np.exp2(np.random.permutation(np.resize(levels, k // 32))).repeat(32)
    a = np.empty((k // 512, 16))
    for p in range(k // 512):
        a[p, :8] = np.random.permutation(np.resize(levels, 8))
        for g in range(8):
            far = levels[np.abs(levels - a[p, g]) >= 10]
            a[p, g + 8] = far[np.random.randint(len(far))]
    return np.exp2(a.ravel()).repeat(32)


def f64(x):
    return np.asarray(x).astype(np.float64)


def striped(idx):
    return np.tile(idx.reshape(-1, 16).T, (8, 1)).astype(np.uint16)


def unstriped(offs):
    return offs[:16].T.reshape(-1).astype(np.int64)


E2M1 = np.array([0.0, 0.5, 1.0, 1.5, 2.0, 3.0, 4.0, 6.0, -0.0, -0.5, -1.0, -1.5, -2.0, -3.0, -4.0, -6.0])


def pack_weight(w, fmt):
    k, n = w.shape
    w = f64(np.asarray(w, np.float32).astype(ml_dtypes.bfloat16)).reshape(k // 32, 32, n)
    amax = np.abs(w).max(1)
    if fmt == "e4m3":
        byte = np.frexp(amax)[1] - 1 + 127 - 7
    else:
        mant, ex = np.frexp(amax / 6.0)
        byte = np.where(mant > 0.5, ex, ex - 1) + 127
    byte = np.clip(np.where(amax > 0, byte, 1), 1, 254)
    scaled = (w * np.exp2(127.0 - byte)[:, None, :]).reshape(k, n).astype(np.float32)
    by_word = np.ascontiguousarray(scaled.reshape(k // 512, 128, 4, n).transpose(0, 1, 3, 2))
    if fmt == "e4m3":
        words = by_word.astype(ml_dtypes.float8_e4m3fn).view(np.uint8)
    else:
        c = by_word.astype(ml_dtypes.float4_e2m1fn).view(np.uint8) & 0xF
        words = (c[..., 0::2] | (c[..., 1::2] << 4)).reshape(k // 512, 128, 2 * n)
    return np.ascontiguousarray(words), np.ascontiguousarray(byte.astype(np.uint8).reshape(k // 512, 16, n))


def unpack_weight(words, scales, fmt):
    g, _, n = scales.shape
    words = np.ascontiguousarray(words).reshape(g, 128, n, -1)
    if fmt == "e4m3":
        vals = words.view(ml_dtypes.float8_e4m3fn).astype(np.float64)
    else:
        nib = np.empty((g, 128, n, 4), np.uint8)
        nib[..., 0::2] = words & 0xF
        nib[..., 1::2] = words >> 4
        vals = E2M1[nib]
    vals = vals * np.repeat(np.exp2(scales.astype(np.float64) - 127.0), 8, axis=1)[..., None]
    return vals.transpose(0, 1, 3, 2).reshape(g * 512, n)


def gelu(v):
    return 0.5 * v * (1.0 + np.tanh(np.sqrt(2.0 / np.pi) * (v + 0.044715 * v**3)))


K, T, S, P, H = 1536, 2048, 1024, 512, 1024


def setup_inputs():
    n = np.random.standard_normal
    s = mx_kscale(K)[:, None]
    u = mx_kscale(H)[:, None]
    tab_words, tab_scales = pack_weight(n((K, T)) * s, "e4m3")
    w1_words, w1_scales = pack_weight(n((K, H)) / np.sqrt(K) / s, "e2m1")
    return {
        "tab_words": tab_words,
        "tab_scales": tab_scales,
        "offs": striped(np.random.permutation(T)[:S]),
        "pos1": striped(np.random.permutation(S)[:P]),
        "pos2": striped(np.random.permutation(S)[:P]),
        "w1_words": w1_words,
        "w1_scales": w1_scales,
        "gain": (np.random.uniform(0.5, 2.0, H) * u[:, 0]).astype(np.float32),
        "w2": (0.6 * n((H, H)) / np.sqrt(H) / u).astype(np.float32),
    }


def reference(tab_words, tab_scales, offs, pos1, pos2, w1_words, w1_scales, gain, w2):
    v = unpack_weight(tab_words, tab_scales, "e4m3")[:, unstriped(offs)]
    w1 = unpack_weight(w1_words, w1_scales, "e2m1")
    h = w1.T @ v
    ref = h[:, unstriped(pos1)]
    rot = h[:, unstriped(pos2)]
    z = np.tanh(ref) * f64(gain)[:, None]
    y = mxq(f64(w2), 0, "e4m3").T @ mxq(z, 0, "e4m3")
    out = rot * np.cos(y) + ref * y
    return out

@@ -1,0 +1,299 @@
+import math
+from contextlib import ExitStack
+
+import concourse.mybir as mybir
+from concourse.masks import make_identity
+
+F32 = mybir.dt.float32
+BF16 = mybir.dt.bfloat16
+I32 = mybir.dt.int32
+U32 = mybir.dt.uint32
+U16 = mybir.dt.uint16
+U8 = mybir.dt.uint8
+FP8X4 = mybir.dt.float8_e4m3fn_x4
+FP4X4 = mybir.dt.float4_e2m1fn_x4
+ALU = mybir.AluOpType
+ACT = mybir.ActivationFunctionType
+
+K, T, S, M, H = 1536, 2048, 1024, 512, 1024
+P = 128
+PASSES = K // 512
+GROUPS = H // 512
+SLOTS = 4
+TILES = GROUPS * SLOTS
+BANK = 512
+HALVES = S // BANK
+
+FLOPS = 2 * K * H * S + 2 * H * H * M
+
+EVAC_ON_VECTOR = ((0, 1), (2, 1), (4, 1), (6, 1))
+PRE = 2
+
+
+def tile_list_quilt_block_turn_kernel(tc, tab_words, tab_scales, offs, pos1, pos2, w1_words, w1_scales, gain, w2, out):
+    nc = tc.nc
+    with ExitStack() as ctx:
+        keep = ctx.enter_context(tc.tile_pool(name="keep", bufs=1))
+        ring = ctx.enter_context(tc.tile_pool(name="ring", bufs=2))
+        ring3 = ctx.enter_context(tc.tile_pool(name="ring3", bufs=3))
+        psum = ctx.enter_context(tc.psum_pool(name="psum", bufs=8))
+
+        offs_sb = keep.tile([P, S // 16], U16, name="offs_sb")
+        pos1_sb = keep.tile([P, M // 16], U16, name="pos1_sb")
+        pos2_sb = keep.tile([P, M // 16], U16, name="pos2_sb")
+        nc.sync.dma_start(offs_sb[:], offs)
+        nc.sync.dma_start(pos1_sb[:], pos1)
+        nc.sync.dma_start(pos2_sb[:], pos2)
+
+        tab_scale = keep.tile([P, T], U8, name="tab_scale", align_bytes=64)
+        w1_scale_raw = keep.tile([P, PASSES * H // 4], I32, name="w1_scale_raw")
+        moved_scale = [keep.tile([P, S], U8, name="moved_scale%d" % a, align_bytes=64) for a in range(1, PASSES)]
+        gain_rows = keep.tile([P, GROUPS * P], F32, name="gain_rows")
+        ident = keep.tile([P, P], F32, name="ident")
+        nc.gpsimd.memset(tab_scale[:].bitcast(I32), 0)
+        nc.vector.memset(w1_scale_raw[:], 0)
+        nc.vector.memset(gain_rows[:], 0.0)
+        for plane in moved_scale:
+            nc.vector.memset(plane[:].bitcast(I32), 0)
+
+        w1_raw = keep.tile([P, PASSES, H // 2], I32, name="w1_raw")
+        nc.sync.dma_start(w1_raw[:], w1_words.bitcast(I32).rearrange("a p c -> p a c"))
+        tab_first = keep.tile([P, T], I32, name="tab_first", tag="staging")
+        tab_rest = keep.tile([P, PASSES - 1, T], I32, name="tab_rest")
+        tab_view = tab_words.rearrange("a p t i -> p a (t i)").bitcast(I32)
+        nc.sync.dma_start(tab_first[:], tab_view[:, 0, :])
+        nc.sync.dma_start(tab_rest[:], tab_view[:, 1:PASSES, :])
+        tab_sb = [tab_first[:]] + [tab_rest[:, a, :] for a in range(PASSES - 1)]
+        for quad in range(4):
+            nc.scalar.dma_start(
+                tab_scale[32 * quad : 32 * quad + 4 * PASSES, :].bitcast(I32),
+                tab_scales[:, 4 * quad : 4 * quad + 4, :].bitcast(I32),
+            )
+        for quad in range(4):
+            nc.gpsimd.dma_start(
+                w1_scale_raw[32 * quad : 32 * quad + 4, :].rearrange("r (a c) -> r a c", a=PASSES),
+                w1_scales[:, 4 * quad : 4 * quad + 4, :].bitcast(I32).rearrange("a r c -> r a c"),
+            )
+        nc.scalar.dma_start(
+            gain_rows[0:SLOTS, :].rearrange("t (g i) -> t g i", i=8), gain.rearrange("(g t i) -> t g i", t=SLOTS, i=8)
+        )
+        make_identity(nc, ident[:])
+        warm = keep.tile([P, 1], F32, name="warm")
+        nc.scalar.activation(warm[:], ident[:, 0:1], ACT.Silu)
+
+        w1_sb = keep.tile([P, PASSES * 2 * H], U8, name="w1_sb", align_bytes=64)
+        w1_scale = keep.tile([P, PASSES * H], U8, name="w1_scale", align_bytes=64)
+        nc.vector.tensor_copy(
+            w1_sb[:].bitcast(I32).rearrange("p (g t q i) -> p g t q i", t=SLOTS, q=16, i=4),
+            w1_raw[:].rearrange("p a (b q t i) -> p (a b) t q i", t=SLOTS, q=16, i=4),
+        )
+
+        picked_scale = keep.tile([P, S], U8, name="picked_scale", align_bytes=64)
+        nc.vector.tensor_copy(picked_scale[:], tab_scale[:].indirect(offs_sb[:]))
+        for a in range(1, PASSES):
+            nc.scalar.dma_start(
+                moved_scale[a - 1][0:100, :].bitcast(I32), picked_scale[4 * a : 4 * a + 100, :].bitcast(I32)
+            )
+        v_scale = [picked_scale] + moved_scale
+
+        def order_w1():
+            nc.vector.tensor_copy(
+                w1_scale[:].bitcast(I32).rearrange("p (g t q i) -> p g t q i", t=SLOTS, q=16, i=2),
+                w1_scale_raw[:].rearrange("p (g q t i) -> p g t q i", t=SLOTS, q=16, i=2),
+            )
+
+        gain_bank = psum.tile([P, BANK], F32, name="bank")
+        for b in range(GROUPS):
+            nc.tensor.transpose(gain_bank[:, b * P : (b + 1) * P], gain_rows[:, b * P : (b + 1) * P], ident[:])
+        gain_sb = keep.tile([P, TILES], F32, name="gain_sb")
+        nc.scalar.copy(
+            gain_sb[:].rearrange("p (b t) -> p b t", t=SLOTS),
+            gain_bank[:, 0 : GROUPS * P].rearrange("p (b c) -> p b c", b=GROUPS)[:, :, 0:SLOTS],
+        )
+
+        v_words = {}
+        h_bank = {}
+
+        def pick_words(a, half):
+            v_words[a, half] = keep.tile([P, BANK], U32, name="v%d_%d" % (a, half), align_bytes=64)
+            cols = slice(half * BANK // 16, (half + 1) * BANK // 16)
+            nc.vector.tensor_copy(v_words[a, half][:], tab_sb[a].bitcast(U32).indirect(offs_sb[:, cols]))
+
+        def first_product(j, half, a):
+            if a == 0:
+                h_bank[j, half] = psum.tile([P, BANK], F32, name="bank")
+            col = a * H + j * P
+            nc.tensor.matmul_mx(
+                out=h_bank[j, half][:],
+                lhsT=w1_sb[:, 2 * col : 2 * (col + P)].bitcast(FP4X4),
+                lhsT_scale=w1_scale[:, col : col + P],
+                rhs=v_words[a, half][:].bitcast(FP8X4),
+                rhs_scale=v_scale[a][:, half * BANK : (half + 1) * BANK],
+                start=(a == 0),
+                stop=(a == PASSES - 1),
+            )
+
+        pick_words(0, 0)
+        order_w1()
+        pick_words(0, 1)
+        w2_view = w2.rearrange("(b q t i) n -> b t q i n", b=GROUPS, t=SLOTS, i=8)
+        w2_all = keep.tile([P, GROUPS, SLOTS, H], F32, name="w2_all", tag="staging")
+        w2_raw = [w2_all[:, b] for b in range(GROUPS)]
+        for b in range(GROUPS):
+            for t in range(SLOTS):
+                nc.sync.dma_start(w2_raw[b][:, t, :], w2_view[b, t])
+
+        for a in range(PASSES):
+            for half in range(HALVES):
+                if a > 0:
+                    pick_words(a, half)
+                for j in range(SLOTS):
+                    first_product(j, half, a)
+
+        h_sb = [keep.tile([P, S], F32, name="h%d" % j) for j in range(TILES)]
+        ref = [keep.tile([P, M], F32, name="ref%d" % j) for j in range(TILES)]
+        rot = [keep.tile([P, M], F32, name="rot%d" % j) for j in range(PRE)]
+        z_codes = [keep.tile([P, M], U32, name="z_codes%d" % b, align_bytes=64) for b in range(GROUPS)]
+        z_scale = [keep.tile([P, M], U8, name="z_scale%d" % b, align_bytes=64) for b in range(GROUPS)]
+        z_planes = [keep.tile([P, SLOTS, M], BF16, name="z_planes%d" % b) for b in range(GROUPS)]
+        z_woven = [keep.tile([P, M, SLOTS], BF16, name="z_woven%d" % b, align_bytes=64) for b in range(GROUPS)]
+
+        def evacuate(j, half):
+            dst = h_sb[j][:, half * BANK : (half + 1) * BANK]
+            if (j, half) in EVAC_ON_VECTOR:
+                nc.vector.tensor_copy(dst, h_bank[j, half][:])
+            else:
+                nc.scalar.copy(dst, h_bank[j, half][:])
+
+        def pick_ref(j):
+            nc.vector.tensor_copy(ref[j][:], h_sb[j][:].indirect(pos1_sb[:]))
+
+        def bound(j):
+            b, t = divmod(j, SLOTS)
+            th = ring.tile([P, M], F32, name="th")
+            nc.scalar.activation(th[:], ref[j][:], ACT.Tanh)
+            nc.scalar.activation(z_planes[b][:, t, :], th[:], ACT.Copy, scale=gain_sb[:, j : j + 1])
+
+        def weave_z(b):
+            nc.vector.tensor_copy(
+                z_woven[b][:].rearrange("p (c i) t -> p c t i", i=4),
+                z_planes[b][:].rearrange("p t (c i) -> p c t i", i=4),
+            )
+
+        def quantize_z(b):
+            nc.vector.quantize_mx(
+                out=z_codes[b][:].bitcast(FP8X4), scales=z_scale[b][:], in_=z_woven[b][:].rearrange("p m t -> p (m t)")
+            )
+
+        w2_codes = {}
+        w2_scale = {}
+        w2_woven = {}
+
+        def weave_w2(j):
+            bn, tn = divmod(j, SLOTS)
+            w2_woven[j] = ring3.tile([P, GROUPS, P, SLOTS], BF16, name="w2_woven", align_bytes=64)
+            for b in range(GROUPS):
+                src = w2_raw[b].rearrange("p s (g q t i) -> p g t q s i", g=GROUPS, t=SLOTS, i=8)[:, bn, tn]
+                nc.scalar.copy(w2_woven[j][:, b].rearrange("p (q i) s -> p q s i", i=8), src)
+
+        def quantize_w2(j):
+            w2_codes[j] = keep.tile([P, GROUPS * P], U32, name="w2_codes%d" % j, align_bytes=64)
+            w2_scale[j] = keep.tile([P, GROUPS * P], U8, name="w2_scale%d" % j, align_bytes=64)
+            nc.vector.quantize_mx(
+                out=w2_codes[j][:].bitcast(FP8X4),
+                scales=w2_scale[j][:],
+                in_=w2_woven[j][:].rearrange("p b n s -> p (b n s)"),
+            )
+
+        evacuate(0, 0)
+        evacuate(1, 0)
+        for j in range(TILES):
+            if j >= SLOTS:
+                for half in range(HALVES):
+                    for a in range(PASSES):
+                        first_product(j, half, a)
+            if j >= 2:
+                evacuate(j, 0)
+            evacuate(j, 1)
+            if j >= 1:
+                bound(j - 1)
+            pick_ref(j)
+            if j == SLOTS + 1:
+                weave_z(0)
+            if j == SLOTS + 2:
+                quantize_z(0)
+                weave_w2(0)
+        bound(TILES - 1)
+        quantize_w2(0)
+        weave_z(1)
+        nc.vector.tensor_copy(rot[0][:], h_sb[0][:].indirect(pos2_sb[:]))
+        quantize_z(1)
+        for j in range(1, PRE):
+            nc.vector.tensor_copy(rot[j][:], h_sb[j][:].indirect(pos2_sb[:]))
+
+        out_view = out.rearrange("(b q t i) m -> b t q i m", b=GROUPS, t=SLOTS, i=8)
+        y_bank = {}
+        turns = {}
+        whole = {}
+        cosine = {}
+        lean = {}
+        turned = {}
+
+        def second_product(j):
+            y_bank[j] = psum.tile([P, BANK], F32, name="bank")
+            for b in range(GROUPS):
+                nc.tensor.matmul_mx(
+                    out=y_bank[j][:],
+                    lhsT=w2_codes[j][:, b * P : (b + 1) * P].bitcast(FP8X4),
+                    lhsT_scale=w2_scale[j][:, b * P : (b + 1) * P],
+                    rhs=z_codes[b][:].bitcast(FP8X4),
+                    rhs_scale=z_scale[b][:],
+                    start=(b == 0),
+                    stop=(b == GROUPS - 1),
+                )
+
+        def count_turns(j):
+            turns[j] = ring3.tile([P, M], F32, name="turns")
+            whole[j] = ring.tile([P, M], I32, name="whole")
+            nc.scalar.activation(turns[j][:], y_bank[j][:], ACT.Abs, scale=1.0 / (2.0 * math.pi))
+            nc.scalar.activation(whole[j][:].bitcast(U32), turns[j][:], ACT.Copy, bias=-0.25)
+
+        def reduce_angle(j):
+            part = ring.tile([P, M], F32, name="part")
+            nc.vector.scalar_tensor_tensor(part[:], whole[j][:], 0.25, turns[j][:], ALU.add, ALU.subtract)
+            cosine[j] = ring3.tile([P, M], F32, name="cosine")
+            nc.scalar.activation(cosine[j][:], part[:], ACT.Sin, scale=2.0 * math.pi)
+
+        def lean_ref(j):
+            lean[j] = ring3.tile([P, M], F32, name="lean")
+            nc.vector.tensor_tensor(lean[j][:], y_bank[j][:], ref[j][:], ALU.mult)
+
+        def turn_rot(j):
+            turned[j] = ring.tile([P, M], F32, name="turned")
+            if j < PRE:
+                nc.vector.tensor_tensor(turned[j][:], rot[j][:], cosine[j][:], ALU.mult)
+            else:
+                nc.vector.tensor_tensor(turned[j][:], h_sb[j][:].indirect(pos2_sb[:]), cosine[j][:], ALU.mult)
+
+        def finish(j):
+            res = ring3.tile([P, M], F32, name="res")
+            nc.vector.tensor_tensor(res[:], turned[j][:], lean[j][:], ALU.add)
+            b, t = divmod(j, SLOTS)
+            nc.sync.dma_start(out_view[b, t], res[:])
+
+        for step in range(TILES + 2):
+            if step < TILES:
+                second_product(step)
+                count_turns(step)
+            if step + 1 < TILES:
+                weave_w2(step + 1)
+            if step >= 2:
+                turn_rot(step - 2)
+            if step < TILES:
+                reduce_angle(step)
+            if step + 1 < TILES:
+                quantize_w2(step + 1)
+            if 1 <= step <= TILES:
+                lean_ref(step - 1)
+            if step >= 2:
+                finish(step - 2)

@@ -26,8 +26,9 @@ HALVES = S // BANK
 
 FLOPS = 2 * K * H * S + 2 * H * H * M
 
-EVAC_ON_VECTOR = ((0, 1), (2, 1), (4, 1), (6, 1))
-PRE = 2
+EVAC_ON_VECTOR = ((0, 1),)
+PRE = 1
+CUTS = 2
 
 
 def tile_list_quilt_block_turn_kernel(tc, tab_words, tab_scales, offs, pos1, pos2, w1_words, w1_scales, gain, w2, out):
@@ -56,21 +57,18 @@ def tile_list_quilt_block_turn_kernel(tc, tab_words, tab_scales, offs, pos1, pos
         for plane in moved_scale:
             nc.vector.memset(plane[:].bitcast(I32), 0)
 
-        w1_raw = keep.tile([P, PASSES, H // 2], I32, name="w1_raw")
+        w1_raw = keep.tile([P, PASSES, H // 2], I32, name="w1_raw", tag="staging_b")
         nc.sync.dma_start(w1_raw[:], w1_words.bitcast(I32).rearrange("a p c -> p a c"))
         tab_first = keep.tile([P, T], I32, name="tab_first", tag="staging")
-        tab_rest = keep.tile([P, PASSES - 1, T], I32, name="tab_rest")
         tab_view = tab_words.rearrange("a p t i -> p a (t i)").bitcast(I32)
         nc.sync.dma_start(tab_first[:], tab_view[:, 0, :])
-        nc.sync.dma_start(tab_rest[:], tab_view[:, 1:PASSES, :])
-        tab_sb = [tab_first[:]] + [tab_rest[:, a, :] for a in range(PASSES - 1)]
         for quad in range(4):
             nc.scalar.dma_start(
                 tab_scale[32 * quad : 32 * quad + 4 * PASSES, :].bitcast(I32),
                 tab_scales[:, 4 * quad : 4 * quad + 4, :].bitcast(I32),
             )
         for quad in range(4):
-            nc.gpsimd.dma_start(
+            nc.scalar.dma_start(
                 w1_scale_raw[32 * quad : 32 * quad + 4, :].rearrange("r (a c) -> r a c", a=PASSES),
                 w1_scales[:, 4 * quad : 4 * quad + 4, :].bitcast(I32).rearrange("a r c -> r a c"),
             )
@@ -87,6 +85,11 @@ def tile_list_quilt_block_turn_kernel(tc, tab_words, tab_scales, offs, pos1, pos
             w1_sb[:].bitcast(I32).rearrange("p (g t q i) -> p g t q i", t=SLOTS, q=16, i=4),
             w1_raw[:].rearrange("p a (b q t i) -> p (a b) t q i", t=SLOTS, q=16, i=4),
         )
+
+        tab_rest = keep.tile([P, PASSES - 1, T], I32, name="tab_rest", tag="staging_b")
+        for a in range(1, PASSES):
+            nc.sync.dma_start(tab_rest[:, a - 1, :], tab_view[:, a, :])
+        tab_sb = [tab_first[:]] + [tab_rest[:, a, :] for a in range(PASSES - 1)]
 
         picked_scale = keep.tile([P, S], U8, name="picked_scale", align_bytes=64)
         nc.vector.tensor_copy(picked_scale[:], tab_scale[:].indirect(offs_sb[:]))
@@ -136,6 +139,12 @@ def tile_list_quilt_block_turn_kernel(tc, tab_words, tab_scales, offs, pos1, pos
         pick_words(0, 0)
         order_w1()
         pick_words(0, 1)
+        for a, half in ((0, 0), (0, 1), (1, 0), (2, 0), (1, 1), (2, 1)):
+            if a > 0:
+                pick_words(a, half)
+            for j in range(SLOTS):
+                first_product(j, half, a)
+
         w2_view = w2.rearrange("(b q t i) n -> b t q i n", b=GROUPS, t=SLOTS, i=8)
         w2_all = keep.tile([P, GROUPS, SLOTS, H], F32, name="w2_all", tag="staging")
         w2_raw = [w2_all[:, b] for b in range(GROUPS)]
@@ -143,20 +152,12 @@ def tile_list_quilt_block_turn_kernel(tc, tab_words, tab_scales, offs, pos1, pos
             for t in range(SLOTS):
                 nc.sync.dma_start(w2_raw[b][:, t, :], w2_view[b, t])
 
-        for a in range(PASSES):
-            for half in range(HALVES):
-                if a > 0:
-                    pick_words(a, half)
-                for j in range(SLOTS):
-                    first_product(j, half, a)
-
         h_sb = [keep.tile([P, S], F32, name="h%d" % j) for j in range(TILES)]
-        ref = [keep.tile([P, M], F32, name="ref%d" % j) for j in range(TILES)]
+        ref_group = [keep.tile([P, SLOTS, M], F32, name="ref%d" % b) for b in range(GROUPS)]
+        ref = [ref_group[j // SLOTS][:, j % SLOTS, :] for j in range(TILES)]
         rot = [keep.tile([P, M], F32, name="rot%d" % j) for j in range(PRE)]
         z_codes = [keep.tile([P, M], U32, name="z_codes%d" % b, align_bytes=64) for b in range(GROUPS)]
         z_scale = [keep.tile([P, M], U8, name="z_scale%d" % b, align_bytes=64) for b in range(GROUPS)]
-        z_planes = [keep.tile([P, SLOTS, M], BF16, name="z_planes%d" % b) for b in range(GROUPS)]
-        z_woven = [keep.tile([P, M, SLOTS], BF16, name="z_woven%d" % b, align_bytes=64) for b in range(GROUPS)]
 
         def evacuate(j, half):
             dst = h_sb[j][:, half * BANK : (half + 1) * BANK]
@@ -165,24 +166,35 @@ def tile_list_quilt_block_turn_kernel(tc, tab_words, tab_scales, offs, pos1, pos
             else:
                 nc.scalar.copy(dst, h_bank[j, half][:])
 
-        def pick_ref(j):
-            nc.vector.tensor_copy(ref[j][:], h_sb[j][:].indirect(pos1_sb[:]))
+        CW = M // CUTS
+        bounded = {}
+        z_woven = {}
 
-        def bound(j):
-            b, t = divmod(j, SLOTS)
-            th = ring.tile([P, M], F32, name="th")
-            nc.scalar.activation(th[:], ref[j][:], ACT.Tanh)
-            nc.scalar.activation(z_planes[b][:, t, :], th[:], ACT.Copy, scale=gain_sb[:, j : j + 1])
+        def pick_ref(j, lo, hi):
+            nc.vector.tensor_copy(ref[j][:, lo * CW : hi * CW], h_sb[j][:].indirect(pos1_sb[:, lo * CW // 16 : hi * CW // 16]))
 
-        def weave_z(b):
-            nc.vector.tensor_copy(
-                z_woven[b][:].rearrange("p (c i) t -> p c t i", i=4),
-                z_planes[b][:].rearrange("p t (c i) -> p c t i", i=4),
+        def bound(b, cut):
+            bounded[b, cut] = ring3.tile([P, CW, SLOTS], F32, name="bounded")
+            nc.scalar.activation(
+                bounded[b, cut][:],
+                ref_group[b][:, :, cut * CW : (cut + 1) * CW].rearrange("p t m -> p m t"),
+                ACT.Tanh,
             )
 
-        def quantize_z(b):
+        def weigh(b, cut):
+            z_woven[b, cut] = ring3.tile([P, CW, SLOTS], BF16, name="z_woven", align_bytes=64)
+            nc.vector.tensor_tensor(
+                z_woven[b, cut][:],
+                bounded[b, cut][:],
+                gain_sb[:, b * SLOTS : (b + 1) * SLOTS].unsqueeze(1).to_broadcast([P, CW, SLOTS]),
+                ALU.mult,
+            )
+
+        def quantize_z(b, cut):
             nc.vector.quantize_mx(
-                out=z_codes[b][:].bitcast(FP8X4), scales=z_scale[b][:], in_=z_woven[b][:].rearrange("p m t -> p (m t)")
+                out=z_codes[b][:, cut * CW : (cut + 1) * CW].bitcast(FP8X4),
+                scales=z_scale[b][:, cut * CW : (cut + 1) * CW],
+                in_=z_woven[b, cut][:].rearrange("p m t -> p (m t)"),
             )
 
         w2_codes = {}
@@ -192,9 +204,8 @@ def tile_list_quilt_block_turn_kernel(tc, tab_words, tab_scales, offs, pos1, pos
         def weave_w2(j):
             bn, tn = divmod(j, SLOTS)
             w2_woven[j] = ring3.tile([P, GROUPS, P, SLOTS], BF16, name="w2_woven", align_bytes=64)
-            for b in range(GROUPS):
-                src = w2_raw[b].rearrange("p s (g q t i) -> p g t q s i", g=GROUPS, t=SLOTS, i=8)[:, bn, tn]
-                nc.scalar.copy(w2_woven[j][:, b].rearrange("p (q i) s -> p q s i", i=8), src)
+            src = w2_all[:].rearrange("p b s (g q t i) -> p g t b q i s", g=GROUPS, t=SLOTS, i=8)[:, bn, tn]
+            nc.scalar.copy(w2_woven[j][:].rearrange("p b (q i) s -> p b q i s", i=8), src)
 
         def quantize_w2(j):
             w2_codes[j] = keep.tile([P, GROUPS * P], U32, name="w2_codes%d" % j, align_bytes=64)
@@ -205,30 +216,44 @@ def tile_list_quilt_block_turn_kernel(tc, tab_words, tab_scales, offs, pos1, pos
                 in_=w2_woven[j][:].rearrange("p b n s -> p (b n s)"),
             )
 
-        evacuate(0, 0)
-        evacuate(1, 0)
-        for j in range(TILES):
-            if j >= SLOTS:
-                for half in range(HALVES):
-                    for a in range(PASSES):
-                        first_product(j, half, a)
-            if j >= 2:
-                evacuate(j, 0)
+        def second_group_products(j):
+            for half in range(HALVES):
+                for a in range(PASSES):
+                    first_product(j, half, a)
+
+        for j in range(SLOTS):
+            evacuate(j, 0)
+        for j in range(SLOTS):
             evacuate(j, 1)
-            if j >= 1:
-                bound(j - 1)
-            pick_ref(j)
-            if j == SLOTS + 1:
-                weave_z(0)
-            if j == SLOTS + 2:
-                quantize_z(0)
-                weave_w2(0)
-        bound(TILES - 1)
+            pick_ref(j, 0, 2)
+        for j in range(SLOTS, TILES):
+            second_group_products(j)
+        for j in (4, 5):
+            evacuate(j, 0)
+            evacuate(j, 1)
+            pick_ref(j, 0, 2)
+        bound(0, 0)
+        evacuate(6, 0)
+        evacuate(6, 1)
+        pick_ref(6, 0, 2)
+        evacuate(7, 0)
+        evacuate(7, 1)
+        pick_ref(7, 0, 1)
+        bound(0, 1)
+        weigh(0, 0)
+        bound(1, 0)
+        pick_ref(7, 1, 2)
+        weave_w2(0)
+        weigh(0, 1)
+        bound(1, 1)
+        quantize_z(0, 0)
+        weigh(1, 0)
+        quantize_z(0, 1)
         quantize_w2(0)
-        weave_z(1)
-        nc.vector.tensor_copy(rot[0][:], h_sb[0][:].indirect(pos2_sb[:]))
-        quantize_z(1)
-        for j in range(1, PRE):
+        weigh(1, 1)
+        quantize_z(1, 0)
+        quantize_z(1, 1)
+        for j in range(PRE):
             nc.vector.tensor_copy(rot[j][:], h_sb[j][:].indirect(pos2_sb[:]))
 
         out_view = out.rearrange("(b q t i) m -> b t q i m", b=GROUPS, t=SLOTS, i=8)
@@ -266,7 +291,7 @@ def tile_list_quilt_block_turn_kernel(tc, tab_words, tab_scales, offs, pos1, pos
 
         def lean_ref(j):
             lean[j] = ring3.tile([P, M], F32, name="lean")
-            nc.vector.tensor_tensor(lean[j][:], y_bank[j][:], ref[j][:], ALU.mult)
+            nc.vector.tensor_tensor(lean[j][:], y_bank[j][:], ref[j], ALU.mult)
 
         def turn_rot(j):
             turned[j] = ring.tile([P, M], F32, name="turned")

@@ -42,115 +42,122 @@ def tile_list_quilt_block_turn_kernel(tc, tab_words, tab_scales, offs, pos1, pos
         offs_sb = keep.tile([P, S // 16], U16, name="offs_sb")
         pos1_sb = keep.tile([P, M // 16], U16, name="pos1_sb")
         pos2_sb = keep.tile([P, M // 16], U16, name="pos2_sb")
-        nc.sync.dma_start(offs_sb[:], offs)
-        nc.sync.dma_start(pos1_sb[:], pos1)
-        nc.sync.dma_start(pos2_sb[:], pos2)
-
         tab_scale = keep.tile([P, T], U8, name="tab_scale", align_bytes=64)
         w1_scale_raw = keep.tile([P, PASSES * H // 4], I32, name="w1_scale_raw")
-        moved_scale = [keep.tile([P, S], U8, name="moved_scale%d" % a, align_bytes=64) for a in range(1, PASSES)]
+        moved_scale = {}
+        for half in range(HALVES):
+            for a in range(1, PASSES):
+                moved_scale[a, half] = keep.tile([P, BANK], U8, name="moved_scale%d_%d" % (a, half), align_bytes=64)
         gain_rows = keep.tile([P, GROUPS * P], F32, name="gain_rows")
         ident = keep.tile([P, P], F32, name="ident")
         nc.gpsimd.memset(tab_scale[:].bitcast(I32), 0)
         nc.vector.memset(w1_scale_raw[:], 0)
-        nc.vector.memset(gain_rows[:], 0.0)
-        for plane in moved_scale:
-            nc.vector.memset(plane[:].bitcast(I32), 0)
+        for plane in moved_scale.values():
+            nc.vector.memset(plane[96:P, :].bitcast(I32), 0)
+        nc.vector.memset(gain_rows[0 : P - SLOTS, :], 0.0)
 
-        w1_raw = keep.tile([P, PASSES, H // 2], I32, name="w1_raw", tag="staging_b")
-        nc.sync.dma_start(w1_raw[:], w1_words.bitcast(I32).rearrange("a p c -> p a c"))
-        tab_first = keep.tile([P, T], I32, name="tab_first", tag="staging")
         tab_view = tab_words.rearrange("a p t i -> p a (t i)").bitcast(I32)
-        nc.sync.dma_start(tab_first[:], tab_view[:, 0, :])
+        w1_view = w1_words.bitcast(I32).rearrange("a p c -> p a c")
+        tab_sb = [keep.tile([P, T], I32, name="tab%d" % a) for a in range(PASSES)]
+        w1_raw_first = keep.tile([P, 1, H // 2], I32, name="w1_raw_first")
+        w1_raw_rest = keep.tile([P, PASSES - 1, H // 2], I32, name="w1_raw_rest", tag="staging")
+        nc.sync.dma_start(offs_sb[:], offs)
+        nc.sync.dma_start(tab_sb[0][:], tab_view[:, 0, :])
         for quad in range(4):
             nc.scalar.dma_start(
                 tab_scale[32 * quad : 32 * quad + 4 * PASSES, :].bitcast(I32),
                 tab_scales[:, 4 * quad : 4 * quad + 4, :].bitcast(I32),
             )
+        nc.sync.dma_start(w1_raw_first[:], w1_view[:, 0:1, :])
         for quad in range(4):
-            nc.scalar.dma_start(
+            nc.sync.dma_start(
                 w1_scale_raw[32 * quad : 32 * quad + 4, :].rearrange("r (a c) -> r a c", a=PASSES),
                 w1_scales[:, 4 * quad : 4 * quad + 4, :].bitcast(I32).rearrange("a r c -> r a c"),
             )
-        nc.scalar.dma_start(
-            gain_rows[0:SLOTS, :].rearrange("t (g i) -> t g i", i=8), gain.rearrange("(g t i) -> t g i", t=SLOTS, i=8)
+        nc.sync.dma_start(tab_sb[1][:], tab_view[:, 1, :])
+        nc.sync.dma_start(w1_raw_rest[:], w1_view[:, 1:PASSES, :])
+        nc.sync.dma_start(tab_sb[2][:], tab_view[:, 2, :])
+        nc.sync.dma_start(pos1_sb[:], pos1)
+        nc.sync.dma_start(pos2_sb[:], pos2)
+        nc.sync.dma_start(
+            gain_rows[P - SLOTS : P, :].rearrange("t (g i) -> t g i", i=8),
+            gain.rearrange("(g t i) -> t g i", t=SLOTS, i=8),
         )
         make_identity(nc, ident[:])
         warm = keep.tile([P, 1], F32, name="warm")
-        nc.scalar.activation(warm[:], ident[:, 0:1], ACT.Silu)
+        nc.scalar.activation(warm[0:64, :], gain_rows[0:64, 0:1], ACT.Silu)
 
-        w1_sb = keep.tile([P, PASSES * 2 * H], U8, name="w1_sb", align_bytes=64)
-        w1_scale = keep.tile([P, PASSES * H], U8, name="w1_scale", align_bytes=64)
-        nc.vector.tensor_copy(
-            w1_sb[:].bitcast(I32).rearrange("p (g t q i) -> p g t q i", t=SLOTS, q=16, i=4),
-            w1_raw[:].rearrange("p a (b q t i) -> p (a b) t q i", t=SLOTS, q=16, i=4),
-        )
+        w1_codes = {}
+        w1_scale = {}
 
-        tab_rest = keep.tile([P, PASSES - 1, T], I32, name="tab_rest", tag="staging_b")
-        for a in range(1, PASSES):
-            nc.sync.dma_start(tab_rest[:, a - 1, :], tab_view[:, a, :])
-        tab_sb = [tab_first[:]] + [tab_rest[:, a, :] for a in range(PASSES - 1)]
-
-        picked_scale = keep.tile([P, S], U8, name="picked_scale", align_bytes=64)
-        nc.vector.tensor_copy(picked_scale[:], tab_scale[:].indirect(offs_sb[:]))
-        for a in range(1, PASSES):
-            nc.scalar.dma_start(
-                moved_scale[a - 1][0:100, :].bitcast(I32), picked_scale[4 * a : 4 * a + 100, :].bitcast(I32)
-            )
-        v_scale = [picked_scale] + moved_scale
-
-        def order_w1():
+        def order_w1(raw, lo, hi):
+            codes = keep.tile([P, (hi - lo) * 2 * H], U8, name="w1_codes%d" % lo, align_bytes=64)
+            scale = keep.tile([P, (hi - lo) * H], U8, name="w1_scale%d" % lo, align_bytes=64)
             nc.vector.tensor_copy(
-                w1_scale[:].bitcast(I32).rearrange("p (g t q i) -> p g t q i", t=SLOTS, q=16, i=2),
-                w1_scale_raw[:].rearrange("p (g q t i) -> p g t q i", t=SLOTS, q=16, i=2),
+                codes[:].bitcast(I32).rearrange("p (g t q i) -> p g t q i", t=SLOTS, q=16, i=4),
+                raw[:].rearrange("p a (b q t i) -> p (a b) t q i", t=SLOTS, q=16, i=4),
             )
-
-        gain_bank = psum.tile([P, BANK], F32, name="bank")
-        for b in range(GROUPS):
-            nc.tensor.transpose(gain_bank[:, b * P : (b + 1) * P], gain_rows[:, b * P : (b + 1) * P], ident[:])
-        gain_sb = keep.tile([P, TILES], F32, name="gain_sb")
-        nc.scalar.copy(
-            gain_sb[:].rearrange("p (b t) -> p b t", t=SLOTS),
-            gain_bank[:, 0 : GROUPS * P].rearrange("p (b c) -> p b c", b=GROUPS)[:, :, 0:SLOTS],
-        )
+            nc.vector.tensor_copy(
+                scale[:].bitcast(I32).rearrange("p (g t q i) -> p g t q i", t=SLOTS, q=16, i=2),
+                w1_scale_raw[:, lo * H // 4 : hi * H // 4].rearrange("p (g q t i) -> p g t q i", t=SLOTS, q=16, i=2),
+            )
+            for a in range(lo, hi):
+                w1_codes[a] = codes[:, (a - lo) * 2 * H : (a - lo + 1) * 2 * H]
+                w1_scale[a] = scale[:, (a - lo) * H : (a - lo + 1) * H]
 
         v_words = {}
+        v_scale = {}
         h_bank = {}
 
+        def list_half(half):
+            return offs_sb[:, half * BANK // 16 : (half + 1) * BANK // 16]
+
+        def pick_scales(half):
+            picked = keep.tile([P, BANK], U8, name="picked_scale%d" % half, align_bytes=64)
+            nc.vector.tensor_copy(picked[:], tab_scale[:].indirect(list_half(half)))
+            v_scale[0, half] = picked
+            for a in range(1, PASSES):
+                v_scale[a, half] = moved_scale[a, half]
+                nc.scalar.dma_start(
+                    moved_scale[a, half][0:100, :].bitcast(I32), picked[4 * a : 4 * a + 100, :].bitcast(I32)
+                )
+
         def pick_words(a, half):
-            v_words[a, half] = keep.tile([P, BANK], U32, name="v%d_%d" % (a, half), align_bytes=64)
-            cols = slice(half * BANK // 16, (half + 1) * BANK // 16)
-            nc.vector.tensor_copy(v_words[a, half][:], tab_sb[a].bitcast(U32).indirect(offs_sb[:, cols]))
+            tag = "v%d" % a if a < PASSES - 1 else "v%d_%d" % (a, half)
+            v_words[a, half] = keep.tile([P, BANK], U32, name="v%d_%d" % (a, half), tag=tag, align_bytes=64)
+            nc.vector.tensor_copy(v_words[a, half][:], tab_sb[a][:].bitcast(U32).indirect(list_half(half)))
 
         def first_product(j, half, a):
             if a == 0:
                 h_bank[j, half] = psum.tile([P, BANK], F32, name="bank")
-            col = a * H + j * P
             nc.tensor.matmul_mx(
                 out=h_bank[j, half][:],
-                lhsT=w1_sb[:, 2 * col : 2 * (col + P)].bitcast(FP4X4),
-                lhsT_scale=w1_scale[:, col : col + P],
+                lhsT=w1_codes[a][:, 2 * j * P : 2 * (j + 1) * P].bitcast(FP4X4),
+                lhsT_scale=w1_scale[a][:, j * P : (j + 1) * P],
                 rhs=v_words[a, half][:].bitcast(FP8X4),
-                rhs_scale=v_scale[a][:, half * BANK : (half + 1) * BANK],
+                rhs_scale=v_scale[a, half][:],
                 start=(a == 0),
                 stop=(a == PASSES - 1),
             )
 
         pick_words(0, 0)
-        order_w1()
+        pick_scales(0)
+        order_w1(w1_raw_first, 0, 1)
+        for j in range(TILES):
+            first_product(j, 0, 0)
+        pick_scales(1)
+        order_w1(w1_raw_rest, 1, PASSES)
+        pick_words(1, 0)
+        for j in range(TILES):
+            first_product(j, 0, 1)
         pick_words(0, 1)
-        for a, half in ((0, 0), (0, 1), (1, 0), (2, 0), (1, 1), (2, 1)):
-            if a > 0:
-                pick_words(a, half)
-            for j in range(SLOTS):
-                first_product(j, half, a)
+        pick_words(2, 0)
 
         w2_view = w2.rearrange("(b q t i) n -> b t q i n", b=GROUPS, t=SLOTS, i=8)
         w2_all = keep.tile([P, GROUPS, SLOTS, H], F32, name="w2_all", tag="staging")
-        w2_raw = [w2_all[:, b] for b in range(GROUPS)]
         for b in range(GROUPS):
             for t in range(SLOTS):
-                nc.sync.dma_start(w2_raw[b][:, t, :], w2_view[b, t])
+                nc.sync.dma_start(w2_all[:, b, t, :], w2_view[b, t])
 
         h_sb = [keep.tile([P, S], F32, name="h%d" % j) for j in range(TILES)]
         ref_group = [keep.tile([P, SLOTS, M], F32, name="ref%d" % b) for b in range(GROUPS)]
@@ -176,8 +183,8 @@ def tile_list_quilt_block_turn_kernel(tc, tab_words, tab_scales, offs, pos1, pos
         def bound(b, cut):
             bounded[b, cut] = ring3.tile([P, CW, SLOTS], F32, name="bounded")
             nc.scalar.activation(
-                bounded[b, cut][:],
-                ref_group[b][:, :, cut * CW : (cut + 1) * CW].rearrange("p t m -> p m t"),
+                bounded[b, cut][:].rearrange("p (c i) t -> p c t i", i=4),
+                ref_group[b][:, :, cut * CW : (cut + 1) * CW].rearrange("p t (c i) -> p c t i", i=4),
                 ACT.Tanh,
             )
 
@@ -204,8 +211,8 @@ def tile_list_quilt_block_turn_kernel(tc, tab_words, tab_scales, offs, pos1, pos
         def weave_w2(j):
             bn, tn = divmod(j, SLOTS)
             w2_woven[j] = ring3.tile([P, GROUPS, P, SLOTS], BF16, name="w2_woven", align_bytes=64)
-            src = w2_all[:].rearrange("p b s (g q t i) -> p g t b q i s", g=GROUPS, t=SLOTS, i=8)[:, bn, tn]
-            nc.scalar.copy(w2_woven[j][:].rearrange("p b (q i) s -> p b q i s", i=8), src)
+            src = w2_all[:].rearrange("p b s (g q t i) -> p g t b q s i", g=GROUPS, t=SLOTS, i=8)[:, bn, tn]
+            nc.scalar.copy(w2_woven[j][:].rearrange("p b (q i) s -> p b q s i", i=8), src)
 
         def quantize_w2(j):
             w2_codes[j] = keep.tile([P, GROUPS * P], U32, name="w2_codes%d" % j, align_bytes=64)
@@ -216,29 +223,40 @@ def tile_list_quilt_block_turn_kernel(tc, tab_words, tab_scales, offs, pos1, pos
                 in_=w2_woven[j][:].rearrange("p b n s -> p (b n s)"),
             )
 
-        def second_group_products(j):
-            for half in range(HALVES):
-                for a in range(PASSES):
-                    first_product(j, half, a)
+        gain_sb = keep.tile([P, TILES], F32, name="gain_sb")
 
-        for j in range(SLOTS):
+        def spread_gain():
+            gain_bank = psum.tile([P, BANK], F32, name="bank")
+            for b in range(GROUPS):
+                nc.tensor.transpose(gain_bank[:, b * P : (b + 1) * P], gain_rows[:, b * P : (b + 1) * P], ident[:])
+            nc.scalar.copy(
+                gain_sb[:].rearrange("p (b t) -> p b t", t=SLOTS),
+                gain_bank[:, 0 : GROUPS * P].rearrange("p (b c) -> p b c", b=GROUPS)[:, :, P - SLOTS : P],
+            )
+
+        def close_first_half(j):
+            first_product(j, 0, PASSES - 1)
             evacuate(j, 0)
-        for j in range(SLOTS):
+
+        AHEAD = 3
+        for j in range(AHEAD):
+            close_first_half(j)
+        pick_words(1, 1)
+        pick_words(2, 1)
+        for j in range(TILES):
+            for a in range(PASSES):
+                first_product(j, 1, a)
+            if j + AHEAD < TILES:
+                close_first_half(j + AHEAD)
             evacuate(j, 1)
-            pick_ref(j, 0, 2)
-        for j in range(SLOTS, TILES):
-            second_group_products(j)
-        for j in (4, 5):
-            evacuate(j, 0)
-            evacuate(j, 1)
-            pick_ref(j, 0, 2)
-        bound(0, 0)
-        evacuate(6, 0)
-        evacuate(6, 1)
-        pick_ref(6, 0, 2)
-        evacuate(7, 0)
-        evacuate(7, 1)
-        pick_ref(7, 0, 1)
+            if j == TILES - 1:
+                pick_ref(j, 0, 1)
+            else:
+                pick_ref(j, 0, 2)
+            if j == 5:
+                spread_gain()
+            if j == 6:
+                bound(0, 0)
         bound(0, 1)
         weigh(0, 0)
         bound(1, 0)

@@ -29,6 +29,7 @@ FLOPS = 2 * K * H * S + 2 * H * H * M
 EVAC_ON_VECTOR = ((0, 1),)
 PRE = 1
 CUTS = 2
+RUNS = ((0,), (1, 2), (3, 4), (5, 6), (7,))
 
 
 def tile_list_quilt_block_turn_kernel(tc, tab_words, tab_scales, offs, pos1, pos2, w1_words, w1_scales, gain, w2, out):
@@ -59,8 +60,8 @@ def tile_list_quilt_block_turn_kernel(tc, tab_words, tab_scales, offs, pos1, pos
         tab_view = tab_words.rearrange("a p t i -> p a (t i)").bitcast(I32)
         w1_view = w1_words.bitcast(I32).rearrange("a p c -> p a c")
         tab_sb = [keep.tile([P, T], I32, name="tab%d" % a) for a in range(PASSES)]
-        w1_raw_first = keep.tile([P, 1, H // 2], I32, name="w1_raw_first")
-        w1_raw_rest = keep.tile([P, PASSES - 1, H // 2], I32, name="w1_raw_rest", tag="staging")
+        w1_raw_first = keep.tile([P, 1, H // 2], I32, name="w1_raw_first", tag="staging0")
+        w1_raw_rest = keep.tile([P, PASSES - 1, H // 2], I32, name="w1_raw_rest", tag="staging1")
         nc.sync.dma_start(offs_sb[:], offs)
         nc.sync.dma_start(tab_sb[0][:], tab_view[:, 0, :])
         for quad in range(4):
@@ -153,11 +154,27 @@ def tile_list_quilt_block_turn_kernel(tc, tab_words, tab_scales, offs, pos1, pos
         pick_words(0, 1)
         pick_words(2, 0)
 
-        w2_view = w2.rearrange("(b q t i) n -> b t q i n", b=GROUPS, t=SLOTS, i=8)
-        w2_all = keep.tile([P, GROUPS, SLOTS, H], F32, name="w2_all", tag="staging")
-        for b in range(GROUPS):
-            for t in range(SLOTS):
-                nc.sync.dma_start(w2_all[:, b, t, :], w2_view[b, t])
+        w2_view = w2.rearrange("(b q s i) (g n) -> g s b q i n", b=GROUPS, s=SLOTS, i=8, g=GROUPS)
+        w2_columns = []
+        for g in range(GROUPS):
+            w2_raw = keep.tile([P, SLOTS, GROUPS, H // GROUPS], F32, name="w2_raw%d" % g, tag="staging%d" % g)
+            for s in range(SLOTS):
+                for b in range(GROUPS):
+                    nc.sync.dma_start(w2_raw[:, s, b, :], w2_view[g, s, b])
+            w2_columns.append(w2_raw[:].rearrange("p s b (q t i) -> p t (b q) s i", t=SLOTS, i=8))
+        w2_woven = [
+            keep.tile([P, 2, GROUPS * 16, 8, SLOTS], BF16, name="w2_woven%d" % pair, align_bytes=64)
+            for pair in range(TILES // 2)
+        ]
+        for j in range(SLOTS):
+            nc.gpsimd.tensor_scalar(
+                w2_woven[j // 2][:, j % 2],
+                w2_columns[0][:, j].rearrange("p c s i -> p c i s"),
+                1.0,
+                0.0,
+                ALU.mult,
+                ALU.add,
+            )
 
         h_sb = [keep.tile([P, S], F32, name="h%d" % j) for j in range(TILES)]
         ref_group = [keep.tile([P, SLOTS, M], F32, name="ref%d" % b) for b in range(GROUPS)]
@@ -206,22 +223,25 @@ def tile_list_quilt_block_turn_kernel(tc, tab_words, tab_scales, offs, pos1, pos
 
         w2_codes = {}
         w2_scale = {}
-        w2_woven = {}
 
-        def weave_w2(j):
-            bn, tn = divmod(j, SLOTS)
-            w2_woven[j] = ring3.tile([P, GROUPS, P, SLOTS], BF16, name="w2_woven", align_bytes=64)
-            src = w2_all[:].rearrange("p b s (g q t i) -> p g t b q s i", g=GROUPS, t=SLOTS, i=8)[:, bn, tn]
-            nc.scalar.copy(w2_woven[j][:].rearrange("p b (q i) s -> p b q s i", i=8), src)
-
-        def quantize_w2(j):
-            w2_codes[j] = keep.tile([P, GROUPS * P], U32, name="w2_codes%d" % j, align_bytes=64)
-            w2_scale[j] = keep.tile([P, GROUPS * P], U8, name="w2_scale%d" % j, align_bytes=64)
-            nc.vector.quantize_mx(
-                out=w2_codes[j][:].bitcast(FP8X4),
-                scales=w2_scale[j][:],
-                in_=w2_woven[j][:].rearrange("p b n s -> p (b n s)"),
+        def weave_w2(pair):
+            first = 2 * pair - SLOTS
+            nc.scalar.copy(
+                w2_woven[pair][:].rearrange("p k c i s -> p k c s i"), w2_columns[1][:, first : first + 2]
             )
+
+        def quantize_w2(pair):
+            width = 2 * GROUPS * P
+            codes = keep.tile([P, width], U32, name="w2_codes%d" % pair, align_bytes=64)
+            scale = keep.tile([P, width], U8, name="w2_scale%d" % pair, align_bytes=64)
+            nc.vector.quantize_mx(
+                out=codes[:].bitcast(FP8X4),
+                scales=scale[:],
+                in_=w2_woven[pair][:].rearrange("p k c i s -> p (k c i s)"),
+            )
+            for k in range(2):
+                w2_codes[2 * pair + k] = codes[:, k * GROUPS * P : (k + 1) * GROUPS * P]
+                w2_scale[2 * pair + k] = scale[:, k * GROUPS * P : (k + 1) * GROUPS * P]
 
         gain_sb = keep.tile([P, TILES], F32, name="gain_sb")
 
@@ -261,7 +281,6 @@ def tile_list_quilt_block_turn_kernel(tc, tab_words, tab_scales, offs, pos1, pos
         weigh(0, 0)
         bound(1, 0)
         pick_ref(7, 1, 2)
-        weave_w2(0)
         weigh(0, 1)
         bound(1, 1)
         quantize_z(0, 0)
@@ -271,6 +290,7 @@ def tile_list_quilt_block_turn_kernel(tc, tab_words, tab_scales, offs, pos1, pos
         weigh(1, 1)
         quantize_z(1, 0)
         quantize_z(1, 1)
+        quantize_w2(1)
         for j in range(PRE):
             nc.vector.tensor_copy(rot[j][:], h_sb[j][:].indirect(pos2_sb[:]))
 
@@ -282,61 +302,66 @@ def tile_list_quilt_block_turn_kernel(tc, tab_words, tab_scales, offs, pos1, pos
         lean = {}
         turned = {}
 
-        def second_product(j):
-            y_bank[j] = psum.tile([P, BANK], F32, name="bank")
-            for b in range(GROUPS):
-                nc.tensor.matmul_mx(
-                    out=y_bank[j][:],
-                    lhsT=w2_codes[j][:, b * P : (b + 1) * P].bitcast(FP8X4),
-                    lhsT_scale=w2_scale[j][:, b * P : (b + 1) * P],
-                    rhs=z_codes[b][:].bitcast(FP8X4),
-                    rhs_scale=z_scale[b][:],
-                    start=(b == 0),
-                    stop=(b == GROUPS - 1),
-                )
+        def run_tile(pool, u, dtype, name):
+            return pool.tile([P, len(RUNS[u]), M], dtype, name=name)
 
-        def count_turns(j):
-            turns[j] = ring3.tile([P, M], F32, name="turns")
-            whole[j] = ring.tile([P, M], I32, name="whole")
-            nc.scalar.activation(turns[j][:], y_bank[j][:], ACT.Abs, scale=1.0 / (2.0 * math.pi))
-            nc.scalar.activation(whole[j][:].bitcast(U32), turns[j][:], ACT.Copy, bias=-0.25)
+        def second_product(u):
+            for j in RUNS[u]:
+                y_bank[j] = psum.tile([P, BANK], F32, name="bank")
+                for b in range(GROUPS):
+                    nc.tensor.matmul_mx(
+                        out=y_bank[j][:],
+                        lhsT=w2_codes[j][:, b * P : (b + 1) * P].bitcast(FP8X4),
+                        lhsT_scale=w2_scale[j][:, b * P : (b + 1) * P],
+                        rhs=z_codes[b][:].bitcast(FP8X4),
+                        rhs_scale=z_scale[b][:],
+                        start=(b == 0),
+                        stop=(b == GROUPS - 1),
+                    )
 
-        def reduce_angle(j):
-            part = ring.tile([P, M], F32, name="part")
-            nc.vector.scalar_tensor_tensor(part[:], whole[j][:], 0.25, turns[j][:], ALU.add, ALU.subtract)
-            cosine[j] = ring3.tile([P, M], F32, name="cosine")
-            nc.scalar.activation(cosine[j][:], part[:], ACT.Sin, scale=2.0 * math.pi)
+        def count_turns(u):
+            turns[u] = run_tile(ring3, u, F32, "turns")
+            whole[u] = run_tile(ring, u, I32, "whole")
+            for k, j in enumerate(RUNS[u]):
+                nc.scalar.activation(turns[u][:, k, :], y_bank[j][:], ACT.Abs, scale=1.0 / (2.0 * math.pi))
+            nc.scalar.activation(whole[u][:].bitcast(U32), turns[u][:], ACT.Copy, bias=-0.25)
 
-        def lean_ref(j):
-            lean[j] = ring3.tile([P, M], F32, name="lean")
-            nc.vector.tensor_tensor(lean[j][:], y_bank[j][:], ref[j], ALU.mult)
+        def reduce_angle(u):
+            part = turns[u]
+            nc.vector.scalar_tensor_tensor(part[:], whole[u][:], 0.25, turns[u][:], ALU.add, ALU.subtract)
+            cosine[u] = run_tile(ring, u, F32, "cosine")
+            nc.scalar.activation(cosine[u][:], part[:], ACT.Sin, scale=2.0 * math.pi)
 
-        def turn_rot(j):
-            turned[j] = ring.tile([P, M], F32, name="turned")
-            if j < PRE:
-                nc.vector.tensor_tensor(turned[j][:], rot[j][:], cosine[j][:], ALU.mult)
-            else:
-                nc.vector.tensor_tensor(turned[j][:], h_sb[j][:].indirect(pos2_sb[:]), cosine[j][:], ALU.mult)
+        def lean_ref(u):
+            lean[u] = run_tile(ring3, u, F32, "lean")
+            for k, j in enumerate(RUNS[u]):
+                nc.vector.tensor_tensor(lean[u][:, k, :], y_bank[j][:], ref[j], ALU.mult)
 
-        def finish(j):
-            res = ring3.tile([P, M], F32, name="res")
-            nc.vector.tensor_tensor(res[:], turned[j][:], lean[j][:], ALU.add)
-            b, t = divmod(j, SLOTS)
-            nc.sync.dma_start(out_view[b, t], res[:])
+        def turn_rot(u):
+            turned[u] = run_tile(ring, u, F32, "turned")
+            for k, j in enumerate(RUNS[u]):
+                picked = rot[j][:] if j < PRE else h_sb[j][:].indirect(pos2_sb[:])
+                nc.vector.tensor_tensor(turned[u][:, k, :], picked, cosine[u][:, k, :], ALU.mult)
 
-        for step in range(TILES + 2):
-            if step < TILES:
+        def finish(u):
+            res = lean[u]
+            nc.vector.tensor_tensor(res[:], turned[u][:], lean[u][:], ALU.add)
+            for k, j in enumerate(RUNS[u]):
+                nc.sync.dma_start(out_view[j // SLOTS, j % SLOTS], res[:, k, :])
+
+        STEPS = len(RUNS)
+        for step in range(STEPS + 1):
+            if step < STEPS:
                 second_product(step)
                 count_turns(step)
-            if step + 1 < TILES:
-                weave_w2(step + 1)
-            if step >= 2:
-                turn_rot(step - 2)
-            if step < TILES:
                 reduce_angle(step)
-            if step + 1 < TILES:
+            if step < 2:
+                weave_w2(step + 2)
+            if step < STEPS:
+                lean_ref(step)
+            if step >= 1:
+                turn_rot(step - 1)
+            if 1 <= step <= 2:
                 quantize_w2(step + 1)
-            if 1 <= step <= TILES:
-                lean_ref(step - 1)
-            if step >= 2:
-                finish(step - 2)
+            if step >= 1:
+                finish(step - 1)

@@ -38,13 +38,14 @@ def tile_list_quilt_block_turn_kernel(tc, tab_words, tab_scales, offs, pos1, pos
         keep = ctx.enter_context(tc.tile_pool(name="keep", bufs=1))
         ring = ctx.enter_context(tc.tile_pool(name="ring", bufs=2))
         ring3 = ctx.enter_context(tc.tile_pool(name="ring3", bufs=3))
+        shared = ctx.enter_context(tc.tile_pool(name="shared", bufs=1))
         psum = ctx.enter_context(tc.psum_pool(name="psum", bufs=8))
 
         offs_sb = keep.tile([P, S // 16], U16, name="offs_sb")
         pos1_sb = keep.tile([P, M // 16], U16, name="pos1_sb")
         pos2_sb = keep.tile([P, M // 16], U16, name="pos2_sb")
         tab_scale = keep.tile([P, T], U8, name="tab_scale", align_bytes=64)
-        w1_scale_raw = keep.tile([P, PASSES * H // 4], I32, name="w1_scale_raw")
+        w1_scale_raw = shared.tile([P, PASSES * H // 4], I32, name="w1_scale_raw", offset=0, align_bytes=64)
         moved_scale = {}
         for half in range(HALVES):
             for a in range(1, PASSES):
@@ -60,8 +61,8 @@ def tile_list_quilt_block_turn_kernel(tc, tab_words, tab_scales, offs, pos1, pos
         tab_view = tab_words.rearrange("a p t i -> p a (t i)").bitcast(I32)
         w1_view = w1_words.bitcast(I32).rearrange("a p c -> p a c")
         tab_sb = [keep.tile([P, T], I32, name="tab%d" % a) for a in range(PASSES)]
-        w1_raw_first = keep.tile([P, 1, H // 2], I32, name="w1_raw_first", tag="staging0")
-        w1_raw_rest = keep.tile([P, PASSES - 1, H // 2], I32, name="w1_raw_rest", tag="staging1")
+        w1_raw_first = keep.tile([P, 1, H // 2], I32, name="w1_raw_first")
+        w1_raw_rest = keep.tile([P, PASSES - 1, H // 2], I32, name="w1_raw_rest")
         nc.sync.dma_start(offs_sb[:], offs)
         nc.sync.dma_start(tab_sb[0][:], tab_view[:, 0, :])
         for quad in range(4):
@@ -75,15 +76,8 @@ def tile_list_quilt_block_turn_kernel(tc, tab_words, tab_scales, offs, pos1, pos
                 w1_scale_raw[32 * quad : 32 * quad + 4, :].rearrange("r (a c) -> r a c", a=PASSES),
                 w1_scales[:, 4 * quad : 4 * quad + 4, :].bitcast(I32).rearrange("a r c -> r a c"),
             )
-        nc.sync.dma_start(tab_sb[1][:], tab_view[:, 1, :])
         nc.sync.dma_start(w1_raw_rest[:], w1_view[:, 1:PASSES, :])
-        nc.sync.dma_start(tab_sb[2][:], tab_view[:, 2, :])
-        nc.sync.dma_start(pos1_sb[:], pos1)
-        nc.sync.dma_start(pos2_sb[:], pos2)
-        nc.sync.dma_start(
-            gain_rows[P - SLOTS : P, :].rearrange("t (g i) -> t g i", i=8),
-            gain.rearrange("(g t i) -> t g i", t=SLOTS, i=8),
-        )
+        nc.sync.dma_start(tab_sb[1][:], tab_view[:, 1, :])
         make_identity(nc, ident[:])
         warm = keep.tile([P, 1], F32, name="warm")
         nc.scalar.activation(warm[0:64, :], gain_rows[0:64, 0:1], ACT.Silu)
@@ -93,18 +87,21 @@ def tile_list_quilt_block_turn_kernel(tc, tab_words, tab_scales, offs, pos1, pos
 
         def order_w1(raw, lo, hi):
             codes = keep.tile([P, (hi - lo) * 2 * H], U8, name="w1_codes%d" % lo, align_bytes=64)
-            scale = keep.tile([P, (hi - lo) * H], U8, name="w1_scale%d" % lo, align_bytes=64)
             nc.vector.tensor_copy(
                 codes[:].bitcast(I32).rearrange("p (g t q i) -> p g t q i", t=SLOTS, q=16, i=4),
                 raw[:].rearrange("p a (b q t i) -> p (a b) t q i", t=SLOTS, q=16, i=4),
             )
-            nc.vector.tensor_copy(
-                scale[:].bitcast(I32).rearrange("p (g t q i) -> p g t q i", t=SLOTS, q=16, i=2),
-                w1_scale_raw[:, lo * H // 4 : hi * H // 4].rearrange("p (g q t i) -> p g t q i", t=SLOTS, q=16, i=2),
-            )
             for a in range(lo, hi):
                 w1_codes[a] = codes[:, (a - lo) * 2 * H : (a - lo + 1) * 2 * H]
-                w1_scale[a] = scale[:, (a - lo) * H : (a - lo + 1) * H]
+
+        def order_w1_scales():
+            scale = keep.tile([P, PASSES * H], U8, name="w1_scale", align_bytes=64)
+            nc.vector.tensor_copy(
+                scale[:].bitcast(I32).rearrange("p (g t q i) -> p g t q i", t=SLOTS, q=16, i=2),
+                w1_scale_raw[:].rearrange("p (g q t i) -> p g t q i", t=SLOTS, q=16, i=2),
+            )
+            for a in range(PASSES):
+                w1_scale[a] = scale[:, a * H : (a + 1) * H]
 
         v_words = {}
         v_scale = {}
@@ -114,18 +111,24 @@ def tile_list_quilt_block_turn_kernel(tc, tab_words, tab_scales, offs, pos1, pos
             return offs_sb[:, half * BANK // 16 : (half + 1) * BANK // 16]
 
         def pick_scales(half):
-            picked = keep.tile([P, BANK], U8, name="picked_scale%d" % half, align_bytes=64)
+            if half == 0:
+                picked = keep.tile([P, BANK], U8, name="picked_scale0", align_bytes=64)
+            else:
+                picked = shared.tile([P, BANK], U8, name="picked_scale1", offset=4 * BANK, align_bytes=64)
             nc.vector.tensor_copy(picked[:], tab_scale[:].indirect(list_half(half)))
             v_scale[0, half] = picked
             for a in range(1, PASSES):
                 v_scale[a, half] = moved_scale[a, half]
-                nc.scalar.dma_start(
+                queue = nc.sync if (a, half) == (1, 0) else nc.scalar
+                queue.dma_start(
                     moved_scale[a, half][0:100, :].bitcast(I32), picked[4 * a : 4 * a + 100, :].bitcast(I32)
                 )
 
         def pick_words(a, half):
-            tag = "v%d" % a if a < PASSES - 1 else "v%d_%d" % (a, half)
-            v_words[a, half] = keep.tile([P, BANK], U32, name="v%d_%d" % (a, half), tag=tag, align_bytes=64)
+            if (a, half) == (0, 1):
+                v_words[a, half] = shared.tile([P, BANK], U32, name="v0_1", offset=0, align_bytes=64)
+            else:
+                v_words[a, half] = keep.tile([P, BANK], U32, name="v%d_%d" % (a, half), align_bytes=64)
             nc.vector.tensor_copy(v_words[a, half][:], tab_sb[a][:].bitcast(U32).indirect(list_half(half)))
 
         def first_product(j, half, a):
@@ -143,21 +146,30 @@ def tile_list_quilt_block_turn_kernel(tc, tab_words, tab_scales, offs, pos1, pos
 
         pick_words(0, 0)
         pick_scales(0)
+        nc.sync.dma_start(tab_sb[2][:], tab_view[:, 2, :])
+        nc.sync.dma_start(pos1_sb[:], pos1)
+        nc.sync.dma_start(pos2_sb[:], pos2)
+        nc.sync.dma_start(
+            gain_rows[P - SLOTS : P, :].rearrange("t (g i) -> t g i", i=8),
+            gain.rearrange("(g t i) -> t g i", t=SLOTS, i=8),
+        )
         order_w1(w1_raw_first, 0, 1)
+        order_w1_scales()
         for j in range(TILES):
             first_product(j, 0, 0)
         pick_scales(1)
         order_w1(w1_raw_rest, 1, PASSES)
+        pick_words(0, 1)
         pick_words(1, 0)
         for j in range(TILES):
             first_product(j, 0, 1)
-        pick_words(0, 1)
+        pick_words(1, 1)
         pick_words(2, 0)
 
         w2_view = w2.rearrange("(b q s i) (g n) -> g s b q i n", b=GROUPS, s=SLOTS, i=8, g=GROUPS)
         w2_columns = []
         for g in range(GROUPS):
-            w2_raw = keep.tile([P, SLOTS, GROUPS, H // GROUPS], F32, name="w2_raw%d" % g, tag="staging%d" % g)
+            w2_raw = keep.tile([P, SLOTS, GROUPS, H // GROUPS], F32, name="w2_raw%d" % g, tag="tab%d" % g)
             for s in range(SLOTS):
                 for b in range(GROUPS):
                     nc.sync.dma_start(w2_raw[:, s, b, :], w2_view[g, s, b])
@@ -261,7 +273,6 @@ def tile_list_quilt_block_turn_kernel(tc, tab_words, tab_scales, offs, pos1, pos
         AHEAD = 3
         for j in range(AHEAD):
             close_first_half(j)
-        pick_words(1, 1)
         pick_words(2, 1)
         for j in range(TILES):
             for a in range(PASSES):

@@ -29,6 +29,8 @@ FLOPS = 2 * K * H * S + 2 * H * H * M
 EVAC_ON_VECTOR = ((0, 1),)
 PRE = 1
 CUTS = 2
+PASS_ORDER = ((0, 1, 2), (0, 2, 1))
+W2_RUNS = ((0, 2), (2, 2), (4, 4))
 RUNS = ((0,), (1, 2), (3, 4), (5, 6), (7,))
 
 
@@ -60,7 +62,7 @@ def tile_list_quilt_block_turn_kernel(tc, tab_words, tab_scales, offs, pos1, pos
 
         tab_view = tab_words.rearrange("a p t i -> p a (t i)").bitcast(I32)
         w1_view = w1_words.bitcast(I32).rearrange("a p c -> p a c")
-        tab_sb = [keep.tile([P, T], I32, name="tab%d" % a) for a in range(PASSES)]
+        tab_sb = [keep.tile([P, T], I32, name="tab%d" % a, align_bytes=64) for a in range(PASSES)]
         w1_raw_first = keep.tile([P, 1, H // 2], I32, name="w1_raw_first")
         w1_raw_rest = keep.tile([P, PASSES - 1, H // 2], I32, name="w1_raw_rest")
         nc.sync.dma_start(offs_sb[:], offs)
@@ -72,12 +74,13 @@ def tile_list_quilt_block_turn_kernel(tc, tab_words, tab_scales, offs, pos1, pos
             )
         nc.sync.dma_start(w1_raw_first[:], w1_view[:, 0:1, :])
         for quad in range(4):
-            nc.sync.dma_start(
+            queue = nc.sync if quad < 2 else nc.scalar
+            queue.dma_start(
                 w1_scale_raw[32 * quad : 32 * quad + 4, :].rearrange("r (a c) -> r a c", a=PASSES),
                 w1_scales[:, 4 * quad : 4 * quad + 4, :].bitcast(I32).rearrange("a r c -> r a c"),
             )
-        nc.sync.dma_start(w1_raw_rest[:], w1_view[:, 1:PASSES, :])
         nc.sync.dma_start(tab_sb[1][:], tab_view[:, 1, :])
+        nc.sync.dma_start(w1_raw_rest[:], w1_view[:, 1:PASSES, :])
         make_identity(nc, ident[:])
         warm = keep.tile([P, 1], F32, name="warm")
         nc.scalar.activation(warm[0:64, :], gain_rows[0:64, 0:1], ACT.Silu)
@@ -119,20 +122,24 @@ def tile_list_quilt_block_turn_kernel(tc, tab_words, tab_scales, offs, pos1, pos
             v_scale[0, half] = picked
             for a in range(1, PASSES):
                 v_scale[a, half] = moved_scale[a, half]
-                queue = nc.sync if (a, half) == (1, 0) else nc.scalar
-                queue.dma_start(
+                nc.scalar.dma_start(
                     moved_scale[a, half][0:100, :].bitcast(I32), picked[4 * a : 4 * a + 100, :].bitcast(I32)
                 )
 
         def pick_words(a, half):
             if (a, half) == (0, 1):
                 v_words[a, half] = shared.tile([P, BANK], U32, name="v0_1", offset=0, align_bytes=64)
+            elif (a, half) == (1, 0):
+                v_words[a, half] = shared.tile([P, BANK], U32, name="v1_0", offset=5 * BANK, align_bytes=64)
+            elif (a, half) == (1, 1):
+                v_words[a, half] = keep.tile([P, BANK], U32, name="v1_1", tag="tab2", align_bytes=64)
             else:
                 v_words[a, half] = keep.tile([P, BANK], U32, name="v%d_%d" % (a, half), align_bytes=64)
             nc.vector.tensor_copy(v_words[a, half][:], tab_sb[a][:].bitcast(U32).indirect(list_half(half)))
 
         def first_product(j, half, a):
-            if a == 0:
+            order = PASS_ORDER[half]
+            if a == order[0]:
                 h_bank[j, half] = psum.tile([P, BANK], F32, name="bank")
             nc.tensor.matmul_mx(
                 out=h_bank[j, half][:],
@@ -140,8 +147,8 @@ def tile_list_quilt_block_turn_kernel(tc, tab_words, tab_scales, offs, pos1, pos
                 lhsT_scale=w1_scale[a][:, j * P : (j + 1) * P],
                 rhs=v_words[a, half][:].bitcast(FP8X4),
                 rhs_scale=v_scale[a, half][:],
-                start=(a == 0),
-                stop=(a == PASSES - 1),
+                start=(a == order[0]),
+                stop=(a == order[-1]),
             )
 
         pick_words(0, 0)
@@ -157,30 +164,27 @@ def tile_list_quilt_block_turn_kernel(tc, tab_words, tab_scales, offs, pos1, pos
         order_w1_scales()
         for j in range(TILES):
             first_product(j, 0, 0)
-        pick_scales(1)
-        order_w1(w1_raw_rest, 1, PASSES)
-        pick_words(0, 1)
         pick_words(1, 0)
-        for j in range(TILES):
-            first_product(j, 0, 1)
-        pick_words(1, 1)
+        order_w1(w1_raw_rest, 1, PASSES)
+        pick_scales(1)
+        pick_words(0, 1)
         pick_words(2, 0)
 
         w2_view = w2.rearrange("(b q s i) (g n) -> g s b q i n", b=GROUPS, s=SLOTS, i=8, g=GROUPS)
         w2_columns = []
         for g in range(GROUPS):
-            w2_raw = keep.tile([P, SLOTS, GROUPS, H // GROUPS], F32, name="w2_raw%d" % g, tag="tab%d" % g)
+            w2_raw = keep.tile([P, SLOTS, GROUPS, H // GROUPS], F32, name="w2_raw%d" % g, tag="tab%d" % g, align_bytes=64)
             for s in range(SLOTS):
                 for b in range(GROUPS):
                     nc.sync.dma_start(w2_raw[:, s, b, :], w2_view[g, s, b])
             w2_columns.append(w2_raw[:].rearrange("p s b (q t i) -> p t (b q) s i", t=SLOTS, i=8))
-        w2_woven = [
-            keep.tile([P, 2, GROUPS * 16, 8, SLOTS], BF16, name="w2_woven%d" % pair, align_bytes=64)
-            for pair in range(TILES // 2)
-        ]
-        for j in range(SLOTS):
+        w2_woven = {
+            first: keep.tile([P, count, GROUPS * 16, 8, SLOTS], BF16, name="w2_woven%d" % first, align_bytes=64)
+            for first, count in W2_RUNS
+        }
+        for j in range(2):
             nc.gpsimd.tensor_scalar(
-                w2_woven[j // 2][:, j % 2],
+                w2_woven[0][:, j],
                 w2_columns[0][:, j].rearrange("p c s i -> p c i s"),
                 1.0,
                 0.0,
@@ -204,7 +208,7 @@ def tile_list_quilt_block_turn_kernel(tc, tab_words, tab_scales, offs, pos1, pos
 
         CW = M // CUTS
         bounded = {}
-        z_woven = {}
+        z_woven = [keep.tile([P, M, SLOTS], BF16, name="z_woven%d" % b, align_bytes=64) for b in range(GROUPS)]
 
         def pick_ref(j, lo, hi):
             nc.vector.tensor_copy(ref[j][:, lo * CW : hi * CW], h_sb[j][:].indirect(pos1_sb[:, lo * CW // 16 : hi * CW // 16]))
@@ -217,43 +221,42 @@ def tile_list_quilt_block_turn_kernel(tc, tab_words, tab_scales, offs, pos1, pos
                 ACT.Tanh,
             )
 
-        def weigh(b, cut):
-            z_woven[b, cut] = ring3.tile([P, CW, SLOTS], BF16, name="z_woven", align_bytes=64)
-            nc.vector.tensor_tensor(
-                z_woven[b, cut][:],
+        def weigh(b, cut, engine):
+            engine.tensor_tensor(
+                z_woven[b][:, cut * CW : (cut + 1) * CW, :],
                 bounded[b, cut][:],
                 gain_sb[:, b * SLOTS : (b + 1) * SLOTS].unsqueeze(1).to_broadcast([P, CW, SLOTS]),
                 ALU.mult,
             )
 
-        def quantize_z(b, cut):
+        def quantize_z(b, lo, hi):
             nc.vector.quantize_mx(
-                out=z_codes[b][:, cut * CW : (cut + 1) * CW].bitcast(FP8X4),
-                scales=z_scale[b][:, cut * CW : (cut + 1) * CW],
-                in_=z_woven[b, cut][:].rearrange("p m t -> p (m t)"),
+                out=z_codes[b][:, lo * CW : hi * CW].bitcast(FP8X4),
+                scales=z_scale[b][:, lo * CW : hi * CW],
+                in_=z_woven[b][:, lo * CW : hi * CW, :].rearrange("p m t -> p (m t)"),
             )
 
         w2_codes = {}
         w2_scale = {}
 
         def weave_w2(pair):
-            first = 2 * pair - SLOTS
-            nc.scalar.copy(
-                w2_woven[pair][:].rearrange("p k c i s -> p k c s i"), w2_columns[1][:, first : first + 2]
-            )
+            g, t = divmod(2 * pair, SLOTS)
+            woven = w2_woven[2][:] if g == 0 else w2_woven[4][:, t : t + 2]
+            nc.scalar.copy(woven.rearrange("p k c i s -> p k c s i"), w2_columns[g][:, t : t + 2])
 
-        def quantize_w2(pair):
-            width = 2 * GROUPS * P
-            codes = keep.tile([P, width], U32, name="w2_codes%d" % pair, align_bytes=64)
-            scale = keep.tile([P, width], U8, name="w2_scale%d" % pair, align_bytes=64)
+        def quantize_w2(run):
+            first, count = W2_RUNS[run]
+            width = count * GROUPS * P
+            codes = keep.tile([P, width], U32, name="w2_codes%d" % run, align_bytes=64)
+            scale = keep.tile([P, width], U8, name="w2_scale%d" % run, align_bytes=64)
             nc.vector.quantize_mx(
                 out=codes[:].bitcast(FP8X4),
                 scales=scale[:],
-                in_=w2_woven[pair][:].rearrange("p k c i s -> p (k c i s)"),
+                in_=w2_woven[first][:].rearrange("p k c i s -> p (k c i s)"),
             )
-            for k in range(2):
-                w2_codes[2 * pair + k] = codes[:, k * GROUPS * P : (k + 1) * GROUPS * P]
-                w2_scale[2 * pair + k] = scale[:, k * GROUPS * P : (k + 1) * GROUPS * P]
+            for k in range(count):
+                w2_codes[first + k] = codes[:, k * GROUPS * P : (k + 1) * GROUPS * P]
+                w2_scale[first + k] = scale[:, k * GROUPS * P : (k + 1) * GROUPS * P]
 
         gain_sb = keep.tile([P, TILES], F32, name="gain_sb")
 
@@ -267,40 +270,43 @@ def tile_list_quilt_block_turn_kernel(tc, tab_words, tab_scales, offs, pos1, pos
             )
 
         def close_first_half(j):
-            first_product(j, 0, PASSES - 1)
+            for a in range(1, PASSES):
+                first_product(j, 0, a)
             evacuate(j, 0)
 
         AHEAD = 3
         for j in range(AHEAD):
             close_first_half(j)
         pick_words(2, 1)
+        pick_words(1, 1)
         for j in range(TILES):
-            for a in range(PASSES):
-                first_product(j, 1, a)
             if j + AHEAD < TILES:
                 close_first_half(j + AHEAD)
+            for a in PASS_ORDER[1]:
+                first_product(j, 1, a)
             evacuate(j, 1)
             if j == TILES - 1:
                 pick_ref(j, 0, 1)
             else:
                 pick_ref(j, 0, 2)
-            if j == 5:
+            if j == 3:
                 spread_gain()
-            if j == 6:
+            if j == 5:
                 bound(0, 0)
-        bound(0, 1)
-        weigh(0, 0)
+                weigh(0, 0, nc.gpsimd)
+            if j == 6:
+                bound(0, 1)
         bound(1, 0)
         pick_ref(7, 1, 2)
-        weigh(0, 1)
         bound(1, 1)
-        quantize_z(0, 0)
-        weigh(1, 0)
-        quantize_z(0, 1)
+        weigh(0, 1, nc.vector)
         quantize_w2(0)
-        weigh(1, 1)
-        quantize_z(1, 0)
-        quantize_z(1, 1)
+        quantize_z(0, 0, 2)
+        weigh(1, 0, nc.vector)
+        weigh(1, 1, nc.vector)
+        quantize_z(1, 0, 1)
+        quantize_z(1, 1, 2)
+        weave_w2(1)
         quantize_w2(1)
         for j in range(PRE):
             nc.vector.tensor_copy(rot[j][:], h_sb[j][:].indirect(pos2_sb[:]))
@@ -372,7 +378,7 @@ def tile_list_quilt_block_turn_kernel(tc, tab_words, tab_scales, offs, pos1, pos
                 lean_ref(step)
             if step >= 1:
                 turn_rot(step - 1)
-            if 1 <= step <= 2:
-                quantize_w2(step + 1)
+            if step == 1:
+                quantize_w2(2)
             if step >= 1:
                 finish(step - 1)

@@ -345,9 +345,9 @@ def tile_list_quilt_block_turn_kernel(tc, tab_words, tab_scales, offs, pos1, pos
 
         def reduce_angle(u):
             part = turns[u]
-            nc.vector.scalar_tensor_tensor(part[:], whole[u][:], 0.25, turns[u][:], ALU.add, ALU.subtract)
+            nc.vector.tensor_tensor(part[:], turns[u][:], whole[u][:], ALU.subtract)
             cosine[u] = run_tile(ring, u, F32, "cosine")
-            nc.scalar.activation(cosine[u][:], part[:], ACT.Sin, scale=2.0 * math.pi)
+            nc.scalar.activation(cosine[u][:], part[:], ACT.Sin, scale=-2.0 * math.pi, bias=0.5 * math.pi)
 
         def lean_ref(u):
             lean[u] = run_tile(ring3, u, F32, "lean")

@@ -23,15 +23,13 @@ SLOTS = 4
 TILES = GROUPS * SLOTS
 BANK = 512
 HALVES = S // BANK
+CUTS = 2
+CW = M // CUTS
+KIB = 1024
 
 FLOPS = 2 * K * H * S + 2 * H * H * M
 
-EVAC_ON_VECTOR = ((0, 1),)
-PRE = 1
-CUTS = 2
-PASS_ORDER = ((0, 1, 2), (0, 2, 1))
-W2_RUNS = ((0, 2), (2, 2), (4, 4))
-RUNS = ((0,), (1, 2), (3, 4), (5, 6), (7,))
+RUNS = ((0,), (1, 2), (3, 4, 5), (6, 7))
 
 
 def tile_list_quilt_block_turn_kernel(tc, tab_words, tab_scales, offs, pos1, pos2, w1_words, w1_scales, gain, w2, out):
@@ -46,25 +44,21 @@ def tile_list_quilt_block_turn_kernel(tc, tab_words, tab_scales, offs, pos1, pos
         offs_sb = keep.tile([P, S // 16], U16, name="offs_sb")
         pos1_sb = keep.tile([P, M // 16], U16, name="pos1_sb")
         pos2_sb = keep.tile([P, M // 16], U16, name="pos2_sb")
-        tab_scale = keep.tile([P, T], U8, name="tab_scale", align_bytes=64)
-        w1_scale_raw = shared.tile([P, PASSES * H // 4], I32, name="w1_scale_raw", offset=0, align_bytes=64)
-        moved_scale = {}
-        for half in range(HALVES):
-            for a in range(1, PASSES):
-                moved_scale[a, half] = keep.tile([P, BANK], U8, name="moved_scale%d_%d" % (a, half), align_bytes=64)
+        tab_scale = shared.tile([P, T], U8, name="tab_scale", offset=8 * KIB, align_bytes=64)
+        w1_scale_raw = keep.tile([P, PASSES, H // 4], U32, name="w1_scale_raw", align_bytes=64)
+        v_scale = [keep.tile([P, S], U8, name="v_scale%d" % a, align_bytes=64) for a in range(PASSES)]
         gain_rows = keep.tile([P, GROUPS * P], F32, name="gain_rows")
         ident = keep.tile([P, P], F32, name="ident")
         nc.gpsimd.memset(tab_scale[:].bitcast(I32), 0)
-        nc.vector.memset(w1_scale_raw[:], 0)
-        for plane in moved_scale.values():
-            nc.vector.memset(plane[96:P, :].bitcast(I32), 0)
+        nc.vector.memset(w1_scale_raw[:].bitcast(I32), 0)
+        for a in range(1, PASSES):
+            nc.vector.memset(v_scale[a][96:P, :].bitcast(I32), 0)
         nc.vector.memset(gain_rows[0 : P - SLOTS, :], 0.0)
 
         tab_view = tab_words.rearrange("a p t i -> p a (t i)").bitcast(I32)
-        w1_view = w1_words.bitcast(I32).rearrange("a p c -> p a c")
+        w1_view = w1_words.bitcast(I32).rearrange("a p (b c) -> b p a c", b=GROUPS)
         tab_sb = [keep.tile([P, T], I32, name="tab%d" % a, align_bytes=64) for a in range(PASSES)]
-        w1_raw_first = keep.tile([P, 1, H // 2], I32, name="w1_raw_first")
-        w1_raw_rest = keep.tile([P, PASSES - 1, H // 2], I32, name="w1_raw_rest")
+        w1_raw = [keep.tile([P, PASSES, H // 4], I32, name="w1_raw")]
         nc.sync.dma_start(offs_sb[:], offs)
         nc.sync.dma_start(tab_sb[0][:], tab_view[:, 0, :])
         for quad in range(4):
@@ -72,87 +66,13 @@ def tile_list_quilt_block_turn_kernel(tc, tab_words, tab_scales, offs, pos1, pos
                 tab_scale[32 * quad : 32 * quad + 4 * PASSES, :].bitcast(I32),
                 tab_scales[:, 4 * quad : 4 * quad + 4, :].bitcast(I32),
             )
-        nc.sync.dma_start(w1_raw_first[:], w1_view[:, 0:1, :])
+        nc.sync.dma_start(w1_raw[0][:], w1_view[0])
         for quad in range(4):
-            queue = nc.sync if quad < 2 else nc.scalar
-            queue.dma_start(
-                w1_scale_raw[32 * quad : 32 * quad + 4, :].rearrange("r (a c) -> r a c", a=PASSES),
+            (nc.sync if quad < 2 else nc.scalar).dma_start(
+                w1_scale_raw[32 * quad : 32 * quad + 4].bitcast(I32),
                 w1_scales[:, 4 * quad : 4 * quad + 4, :].bitcast(I32).rearrange("a r c -> r a c"),
             )
         nc.sync.dma_start(tab_sb[1][:], tab_view[:, 1, :])
-        nc.sync.dma_start(w1_raw_rest[:], w1_view[:, 1:PASSES, :])
-        make_identity(nc, ident[:])
-        warm = keep.tile([P, 1], F32, name="warm")
-        nc.scalar.activation(warm[0:64, :], gain_rows[0:64, 0:1], ACT.Silu)
-
-        w1_codes = {}
-        w1_scale = {}
-
-        def order_w1(raw, lo, hi):
-            codes = keep.tile([P, (hi - lo) * 2 * H], U8, name="w1_codes%d" % lo, align_bytes=64)
-            nc.vector.tensor_copy(
-                codes[:].bitcast(I32).rearrange("p (g t q i) -> p g t q i", t=SLOTS, q=16, i=4),
-                raw[:].rearrange("p a (b q t i) -> p (a b) t q i", t=SLOTS, q=16, i=4),
-            )
-            for a in range(lo, hi):
-                w1_codes[a] = codes[:, (a - lo) * 2 * H : (a - lo + 1) * 2 * H]
-
-        def order_w1_scales():
-            scale = keep.tile([P, PASSES * H], U8, name="w1_scale", align_bytes=64)
-            nc.vector.tensor_copy(
-                scale[:].bitcast(I32).rearrange("p (g t q i) -> p g t q i", t=SLOTS, q=16, i=2),
-                w1_scale_raw[:].rearrange("p (g q t i) -> p g t q i", t=SLOTS, q=16, i=2),
-            )
-            for a in range(PASSES):
-                w1_scale[a] = scale[:, a * H : (a + 1) * H]
-
-        v_words = {}
-        v_scale = {}
-        h_bank = {}
-
-        def list_half(half):
-            return offs_sb[:, half * BANK // 16 : (half + 1) * BANK // 16]
-
-        def pick_scales(half):
-            if half == 0:
-                picked = keep.tile([P, BANK], U8, name="picked_scale0", align_bytes=64)
-            else:
-                picked = shared.tile([P, BANK], U8, name="picked_scale1", offset=4 * BANK, align_bytes=64)
-            nc.vector.tensor_copy(picked[:], tab_scale[:].indirect(list_half(half)))
-            v_scale[0, half] = picked
-            for a in range(1, PASSES):
-                v_scale[a, half] = moved_scale[a, half]
-                nc.scalar.dma_start(
-                    moved_scale[a, half][0:100, :].bitcast(I32), picked[4 * a : 4 * a + 100, :].bitcast(I32)
-                )
-
-        def pick_words(a, half):
-            if (a, half) == (0, 1):
-                v_words[a, half] = shared.tile([P, BANK], U32, name="v0_1", offset=0, align_bytes=64)
-            elif (a, half) == (1, 0):
-                v_words[a, half] = shared.tile([P, BANK], U32, name="v1_0", offset=5 * BANK, align_bytes=64)
-            elif (a, half) == (1, 1):
-                v_words[a, half] = keep.tile([P, BANK], U32, name="v1_1", tag="tab2", align_bytes=64)
-            else:
-                v_words[a, half] = keep.tile([P, BANK], U32, name="v%d_%d" % (a, half), align_bytes=64)
-            nc.vector.tensor_copy(v_words[a, half][:], tab_sb[a][:].bitcast(U32).indirect(list_half(half)))
-
-        def first_product(j, half, a):
-            order = PASS_ORDER[half]
-            if a == order[0]:
-                h_bank[j, half] = psum.tile([P, BANK], F32, name="bank")
-            nc.tensor.matmul_mx(
-                out=h_bank[j, half][:],
-                lhsT=w1_codes[a][:, 2 * j * P : 2 * (j + 1) * P].bitcast(FP4X4),
-                lhsT_scale=w1_scale[a][:, j * P : (j + 1) * P],
-                rhs=v_words[a, half][:].bitcast(FP8X4),
-                rhs_scale=v_scale[a, half][:],
-                start=(a == order[0]),
-                stop=(a == order[-1]),
-            )
-
-        pick_words(0, 0)
-        pick_scales(0)
         nc.sync.dma_start(tab_sb[2][:], tab_view[:, 2, :])
         nc.sync.dma_start(pos1_sb[:], pos1)
         nc.sync.dma_start(pos2_sb[:], pos2)
@@ -160,15 +80,80 @@ def tile_list_quilt_block_turn_kernel(tc, tab_words, tab_scales, offs, pos1, pos
             gain_rows[P - SLOTS : P, :].rearrange("t (g i) -> t g i", i=8),
             gain.rearrange("(g t i) -> t g i", t=SLOTS, i=8),
         )
-        order_w1(w1_raw_first, 0, 1)
-        order_w1_scales()
-        for j in range(TILES):
-            first_product(j, 0, 0)
-        pick_words(1, 0)
-        order_w1(w1_raw_rest, 1, PASSES)
-        pick_scales(1)
+        make_identity(nc, ident[:])
+        warm = keep.tile([P, 1], F32, name="warm")
+        nc.scalar.activation(warm[0:64, :], gain_rows[0:64, 0:1], ACT.Silu)
+
+        w1_codes = {}
+        w1_scale = {}
+
+        def order_codes(copy, codes, b, passes, slots):
+            copy(
+                codes[:].rearrange("p a t (q i) -> p a t q i", i=4),
+                w1_raw[b][:].bitcast(U32).rearrange("p a (q t i) -> p a t q i", t=SLOTS, i=4)[:, passes, slots],
+            )
+            for a in range(passes.start, passes.stop):
+                for t in range(slots.start, slots.stop):
+                    w1_codes[a, SLOTS * b + t] = codes[:, a - passes.start, t - slots.start, :]
+
+        def order_scales(copy, scale, b):
+            copy(
+                scale[:].rearrange("p a t (q i) -> p a t q i", i=2),
+                w1_scale_raw[:].rearrange("p a (b q t i) -> p b a t q i", b=GROUPS, t=SLOTS, i=2)[:, b],
+            )
+            for a in range(PASSES):
+                for t in range(SLOTS):
+                    w1_scale[a, SLOTS * b + t] = scale[:, a, t, :]
+
+        codes_head = keep.tile([P, PASSES, SLOTS, P // 2], U32, name="w1_codes_head", align_bytes=64)
+        order_codes(nc.scalar.copy, codes_head, 0, slice(0, PASSES), slice(0, SLOTS))
+        scale_head = keep.tile([P, PASSES, SLOTS, P // 4], U32, name="w1_scale_head", align_bytes=64)
+        order_scales(nc.gpsimd.tensor_copy, scale_head, 0)
+        w1_raw.append(keep.tile([P, PASSES, H // 4], I32, name="w1_raw"))
+        nc.sync.dma_start(w1_raw[1][:], w1_view[1])
+
+        v_words = {}
+        h_bank = {}
+
+        def pick_words(a, half):
+            if (a, half) == (0, 1):
+                v_words[a, half] = shared.tile([P, BANK], U32, name="v0_1", offset=8 * KIB, align_bytes=64)
+            else:
+                v_words[a, half] = keep.tile([P, BANK], U32, name="v%d_%d" % (a, half), align_bytes=64)
+            nc.vector.tensor_copy(
+                v_words[a, half][:], tab_sb[a][:].bitcast(U32).indirect(offs_sb[:, half * BANK // 16 : (half + 1) * BANK // 16])
+            )
+
+        def first_product(j, half, a):
+            if a == 0:
+                h_bank[j, half] = psum.tile([P, BANK], F32, name="bank")
+            nc.tensor.matmul_mx(
+                out=h_bank[j, half][:],
+                lhsT=w1_codes[a, j].bitcast(U8).bitcast(FP4X4),
+                lhsT_scale=w1_scale[a, j].bitcast(U8),
+                rhs=v_words[a, half][:].bitcast(FP8X4),
+                rhs_scale=v_scale[a][:, half * BANK : (half + 1) * BANK],
+                start=(a == 0),
+                stop=(a == PASSES - 1),
+            )
+
+        pick_words(0, 0)
+        for half in range(HALVES):
+            nc.vector.tensor_copy(
+                v_scale[0][:, half * BANK : (half + 1) * BANK],
+                tab_scale[:].indirect(offs_sb[:, half * BANK // 16 : (half + 1) * BANK // 16]),
+            )
+        for a in range(1, PASSES):
+            nc.scalar.dma_start(v_scale[a][0:100, :].bitcast(I32), v_scale[0][4 * a : 4 * a + 100, :].bitcast(I32))
         pick_words(0, 1)
-        pick_words(2, 0)
+        for a in range(1, PASSES):
+            for half in range(HALVES):
+                pick_words(a, half)
+
+        scale_rest = shared.tile([P, PASSES, SLOTS, P // 4], U32, name="w1_scale_rest", offset=4 * KIB, align_bytes=64)
+        order_scales(nc.scalar.copy, scale_rest, 1)
+        codes_rest = shared.tile([P, PASSES, SLOTS, P // 2], U32, name="w1_codes_rest", offset=0, align_bytes=64)
+        order_codes(nc.scalar.copy, codes_rest, 1, slice(0, PASSES), slice(0, SLOTS))
 
         w2_view = w2.rearrange("(b q s i) (g n) -> g s b q i n", b=GROUPS, s=SLOTS, i=8, g=GROUPS)
         w2_columns = []
@@ -178,51 +163,40 @@ def tile_list_quilt_block_turn_kernel(tc, tab_words, tab_scales, offs, pos1, pos
                 for b in range(GROUPS):
                     nc.sync.dma_start(w2_raw[:, s, b, :], w2_view[g, s, b])
             w2_columns.append(w2_raw[:].rearrange("p s b (q t i) -> p t (b q) s i", t=SLOTS, i=8))
-        w2_woven = {
-            first: keep.tile([P, count, GROUPS * 16, 8, SLOTS], BF16, name="w2_woven%d" % first, align_bytes=64)
-            for first, count in W2_RUNS
-        }
-        for j in range(2):
+        woven_first = keep.tile([P, SLOTS, GROUPS * 16, 8, SLOTS], BF16, name="w2_woven_first", align_bytes=64)
+        for t in range(SLOTS):
             nc.gpsimd.tensor_scalar(
-                w2_woven[0][:, j],
-                w2_columns[0][:, j].rearrange("p c s i -> p c i s"),
-                1.0,
-                0.0,
-                ALU.mult,
-                ALU.add,
+                woven_first[:, t], w2_columns[0][:, t].rearrange("p c s i -> p c i s"), 1.0, 0.0, ALU.mult, ALU.add
             )
 
         h_sb = [keep.tile([P, S], F32, name="h%d" % j) for j in range(TILES)]
         ref_group = [keep.tile([P, SLOTS, M], F32, name="ref%d" % b) for b in range(GROUPS)]
         ref = [ref_group[j // SLOTS][:, j % SLOTS, :] for j in range(TILES)]
-        rot = [keep.tile([P, M], F32, name="rot%d" % j) for j in range(PRE)]
         z_codes = [keep.tile([P, M], U32, name="z_codes%d" % b, align_bytes=64) for b in range(GROUPS)]
         z_scale = [keep.tile([P, M], U8, name="z_scale%d" % b, align_bytes=64) for b in range(GROUPS)]
+        z_woven = [keep.tile([P, M, SLOTS], BF16, name="z_woven%d" % b, align_bytes=64) for b in range(GROUPS)]
+        bounded = {}
 
         def evacuate(j, half):
-            dst = h_sb[j][:, half * BANK : (half + 1) * BANK]
-            if (j, half) in EVAC_ON_VECTOR:
-                nc.vector.tensor_copy(dst, h_bank[j, half][:])
-            else:
-                nc.scalar.copy(dst, h_bank[j, half][:])
+            copy = nc.vector.tensor_copy if (j, half) == (0, 1) else nc.scalar.copy
+            copy(h_sb[j][:, half * BANK : (half + 1) * BANK], h_bank[j, half][:])
 
-        CW = M // CUTS
-        bounded = {}
-        z_woven = [keep.tile([P, M, SLOTS], BF16, name="z_woven%d" % b, align_bytes=64) for b in range(GROUPS)]
-
-        def pick_ref(j, lo, hi):
-            nc.vector.tensor_copy(ref[j][:, lo * CW : hi * CW], h_sb[j][:].indirect(pos1_sb[:, lo * CW // 16 : hi * CW // 16]))
+        def pick_ref(j):
+            nc.vector.tensor_copy(ref[j], h_sb[j][:].indirect(pos1_sb[:]))
 
         def bound(b, cut):
-            bounded[b, cut] = ring3.tile([P, CW, SLOTS], F32, name="bounded")
+            if b == 0:
+                bounded[b, cut] = shared.tile([P, CW, SLOTS], F32, name="bounded0_%d" % cut, offset=4 * KIB * cut, align_bytes=64)
+            else:
+                bounded[b, cut] = keep.tile([P, CW, SLOTS], F32, name="bounded1_%d" % cut)
             nc.scalar.activation(
                 bounded[b, cut][:].rearrange("p (c i) t -> p c t i", i=4),
                 ref_group[b][:, :, cut * CW : (cut + 1) * CW].rearrange("p t (c i) -> p c t i", i=4),
                 ACT.Tanh,
             )
 
-        def weigh(b, cut, engine):
-            engine.tensor_tensor(
+        def weigh(b, cut):
+            nc.vector.tensor_tensor(
                 z_woven[b][:, cut * CW : (cut + 1) * CW, :],
                 bounded[b, cut][:],
                 gain_sb[:, b * SLOTS : (b + 1) * SLOTS].unsqueeze(1).to_broadcast([P, CW, SLOTS]),
@@ -239,88 +213,72 @@ def tile_list_quilt_block_turn_kernel(tc, tab_words, tab_scales, offs, pos1, pos
         w2_codes = {}
         w2_scale = {}
 
-        def weave_w2(pair):
-            g, t = divmod(2 * pair, SLOTS)
-            woven = w2_woven[2][:] if g == 0 else w2_woven[4][:, t : t + 2]
-            nc.scalar.copy(woven.rearrange("p k c i s -> p k c s i"), w2_columns[g][:, t : t + 2])
-
-        def quantize_w2(run):
-            first, count = W2_RUNS[run]
-            width = count * GROUPS * P
-            codes = keep.tile([P, width], U32, name="w2_codes%d" % run, align_bytes=64)
-            scale = keep.tile([P, width], U8, name="w2_scale%d" % run, align_bytes=64)
+        def quantize_w2(woven, codes, first, count):
+            scale = keep.tile([P, count * GROUPS * P], U8, name="w2_scale%d" % first, align_bytes=64)
             nc.vector.quantize_mx(
                 out=codes[:].bitcast(FP8X4),
                 scales=scale[:],
-                in_=w2_woven[first][:].rearrange("p k c i s -> p (k c i s)"),
+                in_=woven[:].rearrange("p k c i s -> p (k c i s)"),
             )
             for k in range(count):
                 w2_codes[first + k] = codes[:, k * GROUPS * P : (k + 1) * GROUPS * P]
                 w2_scale[first + k] = scale[:, k * GROUPS * P : (k + 1) * GROUPS * P]
 
+        for a in range(PASSES):
+            for half in range(HALVES):
+                for j in range(SLOTS):
+                    first_product(j, half, a)
+        for j in range(SLOTS + 1):
+            if j < SLOTS:
+                evacuate(j, 0)
+            if j >= 2:
+                evacuate(j - 1, 1)
+            if j == 0:
+                evacuate(0, 1)
+        for j in range(SLOTS):
+            pick_ref(j)
+        for j in range(SLOTS, TILES):
+            for half in range(HALVES):
+                for a in range(PASSES):
+                    first_product(j, half, a)
+                evacuate(j, half)
+            pick_ref(j)
         gain_sb = keep.tile([P, TILES], F32, name="gain_sb")
+        gain_bank = psum.tile([P, BANK], F32, name="bank")
+        for b in range(GROUPS):
+            nc.tensor.transpose(gain_bank[:, b * P : (b + 1) * P], gain_rows[:, b * P : (b + 1) * P], ident[:])
+        nc.scalar.copy(
+            gain_sb[:].rearrange("p (b t) -> p b t", t=SLOTS),
+            gain_bank[:, 0 : GROUPS * P].rearrange("p (b c) -> p b c", b=GROUPS)[:, :, P - SLOTS : P],
+        )
 
-        def spread_gain():
-            gain_bank = psum.tile([P, BANK], F32, name="bank")
-            for b in range(GROUPS):
-                nc.tensor.transpose(gain_bank[:, b * P : (b + 1) * P], gain_rows[:, b * P : (b + 1) * P], ident[:])
-            nc.scalar.copy(
-                gain_sb[:].rearrange("p (b t) -> p b t", t=SLOTS),
-                gain_bank[:, 0 : GROUPS * P].rearrange("p (b c) -> p b c", b=GROUPS)[:, :, P - SLOTS : P],
-            )
-
-        def close_first_half(j):
-            for a in range(1, PASSES):
-                first_product(j, 0, a)
-            evacuate(j, 0)
-
-        AHEAD = 3
-        for j in range(AHEAD):
-            close_first_half(j)
-        pick_words(2, 1)
-        pick_words(1, 1)
-        for j in range(TILES):
-            if j + AHEAD < TILES:
-                close_first_half(j + AHEAD)
-            for a in PASS_ORDER[1]:
-                first_product(j, 1, a)
-            evacuate(j, 1)
-            if j == TILES - 1:
-                pick_ref(j, 0, 1)
-            else:
-                pick_ref(j, 0, 2)
-            if j == 3:
-                spread_gain()
-            if j == 5:
-                bound(0, 0)
-                weigh(0, 0, nc.gpsimd)
-            if j == 6:
-                bound(0, 1)
-        bound(1, 0)
-        pick_ref(7, 1, 2)
-        bound(1, 1)
-        weigh(0, 1, nc.vector)
-        quantize_w2(0)
+        for b in range(GROUPS):
+            for cut in range(CUTS):
+                bound(b, cut)
+        weigh(0, 0)
+        weigh(0, 1)
+        codes_first = shared.tile([P, SLOTS * GROUPS * P], U32, name="w2_codes_first", offset=0, align_bytes=64)
+        quantize_w2(woven_first, codes_first, 0, SLOTS)
         quantize_z(0, 0, 2)
-        weigh(1, 0, nc.vector)
-        weigh(1, 1, nc.vector)
+        weigh(1, 0)
+        weigh(1, 1)
         quantize_z(1, 0, 1)
         quantize_z(1, 1, 2)
-        weave_w2(1)
-        quantize_w2(1)
-        for j in range(PRE):
-            nc.vector.tensor_copy(rot[j][:], h_sb[j][:].indirect(pos2_sb[:]))
+
+        def weave_pair(first, offset):
+            woven = shared.tile([P, 2, GROUPS * 16, 8, SLOTS], BF16, name="w2_woven%d" % first, offset=offset, align_bytes=64)
+            nc.scalar.copy(woven[:].rearrange("p k c i s -> p k c s i"), w2_columns[1][:, first - SLOTS : first - SLOTS + 2])
+            codes = keep.tile([P, 2 * GROUPS * P], U32, name="w2_codes%d" % first, align_bytes=64)
+            quantize_w2(woven, codes, first, 2)
+
+        weave_pair(4, 4 * KIB)
 
         out_view = out.rearrange("(b q t i) m -> b t q i m", b=GROUPS, t=SLOTS, i=8)
         y_bank = {}
         turns = {}
         whole = {}
         cosine = {}
-        lean = {}
         turned = {}
-
-        def run_tile(pool, u, dtype, name):
-            return pool.tile([P, len(RUNS[u]), M], dtype, name=name)
 
         def second_product(u):
             for j in RUNS[u]:
@@ -337,48 +295,47 @@ def tile_list_quilt_block_turn_kernel(tc, tab_words, tab_scales, offs, pos1, pos
                     )
 
         def count_turns(u):
-            turns[u] = run_tile(ring3, u, F32, "turns")
-            whole[u] = run_tile(ring, u, I32, "whole")
+            shape = [P, len(RUNS[u]), M]
+            if u == 1:
+                turns[u] = shared.tile(shape, F32, name="turns_second", offset=12 * KIB, align_bytes=64)
+            else:
+                turns[u] = ring.tile(shape, F32, name="turns")
+            whole[u] = ring.tile(shape, I32, name="whole")
             for k, j in enumerate(RUNS[u]):
                 nc.scalar.activation(turns[u][:, k, :], y_bank[j][:], ACT.Abs, scale=1.0 / (2.0 * math.pi))
             nc.scalar.activation(whole[u][:].bitcast(U32), turns[u][:], ACT.Copy, bias=-0.25)
-
-        def reduce_angle(u):
-            part = turns[u]
-            nc.vector.tensor_tensor(part[:], turns[u][:], whole[u][:], ALU.subtract)
-            cosine[u] = run_tile(ring, u, F32, "cosine")
-            nc.scalar.activation(cosine[u][:], part[:], ACT.Sin, scale=-2.0 * math.pi, bias=0.5 * math.pi)
-
-        def lean_ref(u):
-            lean[u] = run_tile(ring3, u, F32, "lean")
-            for k, j in enumerate(RUNS[u]):
-                nc.vector.tensor_tensor(lean[u][:, k, :], y_bank[j][:], ref[j], ALU.mult)
+            nc.vector.tensor_tensor(turns[u][:], turns[u][:], whole[u][:], ALU.subtract)
 
         def turn_rot(u):
-            turned[u] = run_tile(ring, u, F32, "turned")
+            cosine[u] = ring.tile([P, len(RUNS[u]), M], F32, name="cosine")
+            nc.scalar.activation(cosine[u][:], turns[u][:], ACT.Sin, scale=-2.0 * math.pi, bias=0.5 * math.pi)
+            turned[u] = ring3.tile([P, len(RUNS[u]), M], F32, name="turned")
             for k, j in enumerate(RUNS[u]):
-                picked = rot[j][:] if j < PRE else h_sb[j][:].indirect(pos2_sb[:])
-                nc.vector.tensor_tensor(turned[u][:, k, :], picked, cosine[u][:, k, :], ALU.mult)
+                nc.vector.tensor_tensor(turned[u][:, k, :], h_sb[j][:].indirect(pos2_sb[:]), cosine[u][:, k, :], ALU.mult)
+
+        def lean_ref(u):
+            for j in RUNS[u]:
+                nc.vector.tensor_tensor(ref[j], y_bank[j][:], ref[j], ALU.mult)
 
         def finish(u):
-            res = lean[u]
-            nc.vector.tensor_tensor(res[:], turned[u][:], lean[u][:], ALU.add)
             for k, j in enumerate(RUNS[u]):
-                nc.sync.dma_start(out_view[j // SLOTS, j % SLOTS], res[:, k, :])
+                nc.vector.tensor_tensor(ref[j], turned[u][:, k, :], ref[j], ALU.add)
+                nc.sync.dma_start(out_view[j // SLOTS, j % SLOTS], ref[j])
 
-        STEPS = len(RUNS)
-        for step in range(STEPS + 1):
-            if step < STEPS:
-                second_product(step)
-                count_turns(step)
-                reduce_angle(step)
-            if step < 2:
-                weave_w2(step + 2)
-            if step < STEPS:
-                lean_ref(step)
-            if step >= 1:
-                turn_rot(step - 1)
-            if step == 1:
-                quantize_w2(2)
-            if step >= 1:
-                finish(step - 1)
+        steps = len(RUNS)
+        for u in range(steps - 1):
+            second_product(u)
+        count_turns(0)
+        lean_ref(0)
+        for u in range(steps):
+            if u == steps - 2:
+                weave_pair(6, 12 * KIB)
+                second_product(steps - 1)
+            if u + 1 < steps:
+                count_turns(u + 1)
+            turn_rot(u)
+            if u + 1 < steps:
+                lean_ref(u + 1)
+            if u >= 1:
+                finish(u - 1)
+        finish(steps - 1)

@@ -46,20 +46,20 @@ def tile_list_quilt_block_turn_kernel(tc, tab_words, tab_scales, offs, pos1, pos
         pos2_sb = keep.tile([P, M // 16], U16, name="pos2_sb")
         tab_scale = shared.tile([P, T], U8, name="tab_scale", offset=8 * KIB, align_bytes=64)
         w1_scale_raw = keep.tile([P, PASSES, H // 4], U32, name="w1_scale_raw", align_bytes=64)
-        v_scale = [keep.tile([P, S], U8, name="v_scale%d" % a, align_bytes=64) for a in range(PASSES)]
+        v_scale = [keep.tile([P, S], U8, name="v_scale0", align_bytes=64)]
         gain_rows = keep.tile([P, GROUPS * P], F32, name="gain_rows")
         ident = keep.tile([P, P], F32, name="ident")
         nc.gpsimd.memset(tab_scale[:].bitcast(I32), 0)
         nc.vector.memset(w1_scale_raw[:].bitcast(I32), 0)
-        for a in range(1, PASSES):
-            nc.vector.memset(v_scale[a][96:P, :].bitcast(I32), 0)
         nc.vector.memset(gain_rows[0 : P - SLOTS, :], 0.0)
 
         tab_view = tab_words.rearrange("a p t i -> p a (t i)").bitcast(I32)
         w1_view = w1_words.bitcast(I32).rearrange("a p (b c) -> b p a c", b=GROUPS)
         tab_sb = [keep.tile([P, T], I32, name="tab%d" % a, align_bytes=64) for a in range(PASSES)]
-        w1_raw = [keep.tile([P, PASSES, H // 4], I32, name="w1_raw")]
+        w1_raw = [keep.tile([P, PASSES, H // 4], I32, name="w1_raw%d" % b, align_bytes=64) for b in range(GROUPS)]
         nc.sync.dma_start(offs_sb[:], offs)
+        nc.sync.dma_start(pos1_sb[:], pos1)
+        nc.sync.dma_start(pos2_sb[:], pos2)
         nc.sync.dma_start(tab_sb[0][:], tab_view[:, 0, :])
         for quad in range(4):
             nc.scalar.dma_start(
@@ -68,14 +68,13 @@ def tile_list_quilt_block_turn_kernel(tc, tab_words, tab_scales, offs, pos1, pos
             )
         nc.sync.dma_start(w1_raw[0][:], w1_view[0])
         for quad in range(4):
-            (nc.sync if quad < 2 else nc.scalar).dma_start(
+            nc.sync.dma_start(
                 w1_scale_raw[32 * quad : 32 * quad + 4].bitcast(I32),
                 w1_scales[:, 4 * quad : 4 * quad + 4, :].bitcast(I32).rearrange("a r c -> r a c"),
             )
         nc.sync.dma_start(tab_sb[1][:], tab_view[:, 1, :])
         nc.sync.dma_start(tab_sb[2][:], tab_view[:, 2, :])
-        nc.sync.dma_start(pos1_sb[:], pos1)
-        nc.sync.dma_start(pos2_sb[:], pos2)
+        nc.sync.dma_start(w1_raw[1][:], w1_view[1])
         nc.sync.dma_start(
             gain_rows[P - SLOTS : P, :].rearrange("t (g i) -> t g i", i=8),
             gain.rearrange("(g t i) -> t g i", t=SLOTS, i=8),
@@ -109,8 +108,6 @@ def tile_list_quilt_block_turn_kernel(tc, tab_words, tab_scales, offs, pos1, pos
         order_codes(nc.scalar.copy, codes_head, 0, slice(0, PASSES), slice(0, SLOTS))
         scale_head = keep.tile([P, PASSES, SLOTS, P // 4], U32, name="w1_scale_head", align_bytes=64)
         order_scales(nc.gpsimd.tensor_copy, scale_head, 0)
-        w1_raw.append(keep.tile([P, PASSES, H // 4], I32, name="w1_raw"))
-        nc.sync.dma_start(w1_raw[1][:], w1_view[1])
 
         v_words = {}
         h_bank = {}
@@ -143,17 +140,21 @@ def tile_list_quilt_block_turn_kernel(tc, tab_words, tab_scales, offs, pos1, pos
                 v_scale[0][:, half * BANK : (half + 1) * BANK],
                 tab_scale[:].indirect(offs_sb[:, half * BANK // 16 : (half + 1) * BANK // 16]),
             )
+        moved = keep.tile([P, (PASSES - 1) * S], U8, name="moved_scale", tag="w1_raw0", align_bytes=64)
+        nc.gpsimd.memset(moved[96:P, :].bitcast(I32), 0)
         for a in range(1, PASSES):
+            v_scale.append(moved[:, (a - 1) * S : a * S])
             nc.scalar.dma_start(v_scale[a][0:100, :].bitcast(I32), v_scale[0][4 * a : 4 * a + 100, :].bitcast(I32))
         pick_words(0, 1)
         for a in range(1, PASSES):
             for half in range(HALVES):
                 pick_words(a, half)
 
-        scale_rest = shared.tile([P, PASSES, SLOTS, P // 4], U32, name="w1_scale_rest", offset=4 * KIB, align_bytes=64)
+        scale_rest = shared.tile([P, PASSES, SLOTS, P // 4], U32, name="w1_scale_rest", offset=16 * KIB, align_bytes=64)
         order_scales(nc.scalar.copy, scale_rest, 1)
-        codes_rest = shared.tile([P, PASSES, SLOTS, P // 2], U32, name="w1_codes_rest", offset=0, align_bytes=64)
-        order_codes(nc.scalar.copy, codes_rest, 1, slice(0, PASSES), slice(0, SLOTS))
+        for first, last, offset in ((0, 2, 0), (2, 3, 4 * KIB), (3, 4, 18 * KIB)):
+            codes_rest = shared.tile([P, PASSES, last - first, P // 2], U32, name="w1_codes_rest%d" % first, offset=offset, align_bytes=64)
+            order_codes(nc.scalar.copy, codes_rest, 1, slice(0, PASSES), slice(first, last))
 
         w2_view = w2.rearrange("(b q s i) (g n) -> g s b q i n", b=GROUPS, s=SLOTS, i=8, g=GROUPS)
         w2_columns = []
@@ -170,11 +171,13 @@ def tile_list_quilt_block_turn_kernel(tc, tab_words, tab_scales, offs, pos1, pos
             )
 
         h_sb = [keep.tile([P, S], F32, name="h%d" % j) for j in range(TILES)]
-        ref_group = [keep.tile([P, SLOTS, M], F32, name="ref%d" % b) for b in range(GROUPS)]
-        ref = [ref_group[j // SLOTS][:, j % SLOTS, :] for j in range(TILES)]
-        z_codes = [keep.tile([P, M], U32, name="z_codes%d" % b, align_bytes=64) for b in range(GROUPS)]
+        ref_all = keep.tile([P, TILES, M], F32, name="ref_all")
+        ref_group = [ref_all[:, b * SLOTS : (b + 1) * SLOTS, :] for b in range(GROUPS)]
+        ref = [ref_all[:, j, :] for j in range(TILES)]
+        z_codes = {}
         z_scale = [keep.tile([P, M], U8, name="z_scale%d" % b, align_bytes=64) for b in range(GROUPS)]
-        z_woven = [keep.tile([P, M, SLOTS], BF16, name="z_woven%d" % b, align_bytes=64) for b in range(GROUPS)]
+        z_woven = [keep.tile([P, M * SLOTS // 2], U32, name="z_woven%d" % b, align_bytes=64) for b in range(GROUPS)]
+        z_woven = [woven[:].bitcast(BF16).rearrange("p (m t) -> p m t", t=SLOTS) for woven in z_woven]
         bounded = {}
 
         def evacuate(j, half):
@@ -187,8 +190,10 @@ def tile_list_quilt_block_turn_kernel(tc, tab_words, tab_scales, offs, pos1, pos
         def bound(b, cut):
             if b == 0:
                 bounded[b, cut] = shared.tile([P, CW, SLOTS], F32, name="bounded0_%d" % cut, offset=4 * KIB * cut, align_bytes=64)
+            elif cut == 0:
+                bounded[b, cut] = shared.tile([P, CW, SLOTS], F32, name="bounded1_0", offset=20 * KIB, align_bytes=64)
             else:
-                bounded[b, cut] = keep.tile([P, CW, SLOTS], F32, name="bounded1_%d" % cut)
+                bounded[b, cut] = keep.tile([P, CW, SLOTS], F32, name="bounded1_1")
             nc.scalar.activation(
                 bounded[b, cut][:].rearrange("p (c i) t -> p c t i", i=4),
                 ref_group[b][:, :, cut * CW : (cut + 1) * CW].rearrange("p t (c i) -> p c t i", i=4),
@@ -224,46 +229,47 @@ def tile_list_quilt_block_turn_kernel(tc, tab_words, tab_scales, offs, pos1, pos
                 w2_codes[first + k] = codes[:, k * GROUPS * P : (k + 1) * GROUPS * P]
                 w2_scale[first + k] = scale[:, k * GROUPS * P : (k + 1) * GROUPS * P]
 
-        for a in range(PASSES):
-            for half in range(HALVES):
-                for j in range(SLOTS):
+        steps = [(a, half) for a in range(PASSES) for half in range(HALVES)]
+        for a, half in steps[:3]:
+            for j in range(SLOTS):
+                first_product(j, half, a)
+        for pair in range(SLOTS // 2):
+            for a, half in steps[3:]:
+                for j in (2 * pair, 2 * pair + 1):
                     first_product(j, half, a)
-        for j in range(SLOTS + 1):
-            if j < SLOTS:
-                evacuate(j, 0)
-            if j >= 2:
-                evacuate(j - 1, 1)
-            if j == 0:
-                evacuate(0, 1)
-        for j in range(SLOTS):
-            pick_ref(j)
+                    if a == PASSES - 1:
+                        evacuate(j, half)
+            for j in (2 * pair, 2 * pair + 1):
+                pick_ref(j)
         for j in range(SLOTS, TILES):
             for half in range(HALVES):
                 for a in range(PASSES):
                     first_product(j, half, a)
                 evacuate(j, half)
+            if j == SLOTS:
+                gain_sb = keep.tile([P, TILES], F32, name="gain_sb")
+                gain_bank = psum.tile([P, BANK], F32, name="bank")
+                for b in range(GROUPS):
+                    nc.tensor.transpose(gain_bank[:, b * P : (b + 1) * P], gain_rows[:, b * P : (b + 1) * P], ident[:])
+                nc.scalar.copy(
+                    gain_sb[:].rearrange("p (b t) -> p b t", t=SLOTS),
+                    gain_bank[:, 0 : GROUPS * P].rearrange("p (b c) -> p b c", b=GROUPS)[:, :, P - SLOTS : P],
+                )
+            if j == TILES - 1:
+                z_codes[0] = shared.tile([P, M], U32, name="z_codes0", offset=16 * KIB, align_bytes=64)
+                quantize_z(0, 0, 2)
             pick_ref(j)
-        gain_sb = keep.tile([P, TILES], F32, name="gain_sb")
-        gain_bank = psum.tile([P, BANK], F32, name="bank")
-        for b in range(GROUPS):
-            nc.tensor.transpose(gain_bank[:, b * P : (b + 1) * P], gain_rows[:, b * P : (b + 1) * P], ident[:])
-        nc.scalar.copy(
-            gain_sb[:].rearrange("p (b t) -> p b t", t=SLOTS),
-            gain_bank[:, 0 : GROUPS * P].rearrange("p (b c) -> p b c", b=GROUPS)[:, :, P - SLOTS : P],
-        )
-
-        for b in range(GROUPS):
-            for cut in range(CUTS):
-                bound(b, cut)
-        weigh(0, 0)
-        weigh(0, 1)
-        codes_first = shared.tile([P, SLOTS * GROUPS * P], U32, name="w2_codes_first", offset=0, align_bytes=64)
+            if j in (5, 6):
+                bound(0, j - 5)
+                weigh(0, j - 5)
+        codes_first = keep.tile([P, SLOTS * GROUPS * P], U32, name="w2_codes_first", tag="z_woven0", align_bytes=64)
         quantize_w2(woven_first, codes_first, 0, SLOTS)
-        quantize_z(0, 0, 2)
-        weigh(1, 0)
-        weigh(1, 1)
-        quantize_z(1, 0, 1)
-        quantize_z(1, 1, 2)
+        z_codes[1] = keep.tile([P, M], U32, name="z_codes1", align_bytes=64)
+        for cut in range(CUTS):
+            bound(1, cut)
+            weigh(1, cut)
+        for cut in range(CUTS):
+            quantize_z(1, cut, cut + 1)
 
         def weave_pair(first, offset):
             woven = shared.tile([P, 2, GROUPS * 16, 8, SLOTS], BF16, name="w2_woven%d" % first, offset=offset, align_bytes=64)
@@ -271,7 +277,7 @@ def tile_list_quilt_block_turn_kernel(tc, tab_words, tab_scales, offs, pos1, pos
             codes = keep.tile([P, 2 * GROUPS * P], U32, name="w2_codes%d" % first, align_bytes=64)
             quantize_w2(woven, codes, first, 2)
 
-        weave_pair(4, 4 * KIB)
+        weave_pair(4, 20 * KIB)
 
         out_view = out.rearrange("(b q t i) m -> b t q i m", b=GROUPS, t=SLOTS, i=8)
         y_bank = {}
@@ -318,24 +324,28 @@ def tile_list_quilt_block_turn_kernel(tc, tab_words, tab_scales, offs, pos1, pos
                 nc.vector.tensor_tensor(ref[j], y_bank[j][:], ref[j], ALU.mult)
 
         def finish(u):
+            if len(RUNS[u]) > 2:
+                rows = ref_all[:, RUNS[u][0] : RUNS[u][-1] + 1, :]
+                nc.vector.tensor_tensor(rows, turned[u][:], rows, ALU.add)
             for k, j in enumerate(RUNS[u]):
-                nc.vector.tensor_tensor(ref[j], turned[u][:, k, :], ref[j], ALU.add)
+                if len(RUNS[u]) <= 2:
+                    nc.vector.tensor_tensor(ref[j], turned[u][:, k, :], ref[j], ALU.add)
                 nc.sync.dma_start(out_view[j // SLOTS, j % SLOTS], ref[j])
 
-        steps = len(RUNS)
-        for u in range(steps - 1):
+        runs = len(RUNS)
+        for u in range(runs - 1):
             second_product(u)
         count_turns(0)
         lean_ref(0)
-        for u in range(steps):
-            if u == steps - 2:
+        for u in range(runs):
+            if u == runs - 2:
                 weave_pair(6, 12 * KIB)
-                second_product(steps - 1)
-            if u + 1 < steps:
+                second_product(runs - 1)
+            if u + 1 < runs:
                 count_turns(u + 1)
             turn_rot(u)
-            if u + 1 < steps:
+            if u + 1 < runs:
                 lean_ref(u + 1)
             if u >= 1:
                 finish(u - 1)
-        finish(steps - 1)
+        finish(runs - 1)

@@ -39,27 +39,27 @@ def tile_list_quilt_block_turn_kernel(tc, tab_words, tab_scales, offs, pos1, pos
         ring = ctx.enter_context(tc.tile_pool(name="ring", bufs=2))
         ring3 = ctx.enter_context(tc.tile_pool(name="ring3", bufs=3))
         shared = ctx.enter_context(tc.tile_pool(name="shared", bufs=1))
+        head = ctx.enter_context(tc.tile_pool(name="head", bufs=1))
         psum = ctx.enter_context(tc.psum_pool(name="psum", bufs=8))
 
         offs_sb = keep.tile([P, S // 16], U16, name="offs_sb")
         pos1_sb = keep.tile([P, M // 16], U16, name="pos1_sb")
         pos2_sb = keep.tile([P, M // 16], U16, name="pos2_sb")
-        tab_scale = shared.tile([P, T], U8, name="tab_scale", offset=8 * KIB, align_bytes=64)
+        tab_scale = shared.tile([P, T], U8, name="tab_scale", offset=25 * KIB, align_bytes=64)
         w1_scale_raw = keep.tile([P, PASSES, H // 4], U32, name="w1_scale_raw", align_bytes=64)
         v_scale = [keep.tile([P, S], U8, name="v_scale0", align_bytes=64)]
-        gain_rows = keep.tile([P, GROUPS * P], F32, name="gain_rows")
+        warm = keep.tile([P, 2], F32, name="warm")
         ident = keep.tile([P, P], F32, name="ident")
         nc.gpsimd.memset(tab_scale[:].bitcast(I32), 0)
         nc.vector.memset(w1_scale_raw[:].bitcast(I32), 0)
-        nc.vector.memset(gain_rows[0 : P - SLOTS, :], 0.0)
+        nc.vector.memset(warm[:, 0:1], 0.0)
 
         tab_view = tab_words.rearrange("a p t i -> p a (t i)").bitcast(I32)
         w1_view = w1_words.bitcast(I32).rearrange("a p (b c) -> b p a c", b=GROUPS)
-        tab_sb = [keep.tile([P, T], I32, name="tab%d" % a, align_bytes=64) for a in range(PASSES)]
-        w1_raw = [keep.tile([P, PASSES, H // 4], I32, name="w1_raw%d" % b, align_bytes=64) for b in range(GROUPS)]
+        tab_sb = [head.tile([P, T], I32, name="tab0", offset=0, align_bytes=64)]
+        tab_sb.extend(keep.tile([P, T], I32, name="tab%d" % a, align_bytes=64) for a in range(1, PASSES))
+        w1_raw = [keep.tile([P, PASSES, H // 4], I32, name="w1_raw0", align_bytes=64)]
         nc.sync.dma_start(offs_sb[:], offs)
-        nc.sync.dma_start(pos1_sb[:], pos1)
-        nc.sync.dma_start(pos2_sb[:], pos2)
         nc.sync.dma_start(tab_sb[0][:], tab_view[:, 0, :])
         for quad in range(4):
             nc.scalar.dma_start(
@@ -68,20 +68,16 @@ def tile_list_quilt_block_turn_kernel(tc, tab_words, tab_scales, offs, pos1, pos
             )
         nc.sync.dma_start(w1_raw[0][:], w1_view[0])
         for quad in range(4):
-            nc.sync.dma_start(
+            (nc.sync if quad < 2 else nc.scalar).dma_start(
                 w1_scale_raw[32 * quad : 32 * quad + 4].bitcast(I32),
                 w1_scales[:, 4 * quad : 4 * quad + 4, :].bitcast(I32).rearrange("a r c -> r a c"),
             )
         nc.sync.dma_start(tab_sb[1][:], tab_view[:, 1, :])
         nc.sync.dma_start(tab_sb[2][:], tab_view[:, 2, :])
-        nc.sync.dma_start(w1_raw[1][:], w1_view[1])
-        nc.sync.dma_start(
-            gain_rows[P - SLOTS : P, :].rearrange("t (g i) -> t g i", i=8),
-            gain.rearrange("(g t i) -> t g i", t=SLOTS, i=8),
-        )
+        nc.sync.dma_start(pos1_sb[:], pos1)
+        nc.sync.dma_start(pos2_sb[:], pos2)
         make_identity(nc, ident[:])
-        warm = keep.tile([P, 1], F32, name="warm")
-        nc.scalar.activation(warm[0:64, :], gain_rows[0:64, 0:1], ACT.Silu)
+        nc.scalar.activation(warm[:, 1:2], warm[:, 0:1], ACT.Silu)
 
         w1_codes = {}
         w1_scale = {}
@@ -114,7 +110,7 @@ def tile_list_quilt_block_turn_kernel(tc, tab_words, tab_scales, offs, pos1, pos
 
         def pick_words(a, half):
             if (a, half) == (0, 1):
-                v_words[a, half] = shared.tile([P, BANK], U32, name="v0_1", offset=8 * KIB, align_bytes=64)
+                v_words[a, half] = shared.tile([P, BANK], U32, name="v0_1", offset=24 * KIB, align_bytes=64)
             else:
                 v_words[a, half] = keep.tile([P, BANK], U32, name="v%d_%d" % (a, half), align_bytes=64)
             nc.vector.tensor_copy(
@@ -146,6 +142,14 @@ def tile_list_quilt_block_turn_kernel(tc, tab_words, tab_scales, offs, pos1, pos
             v_scale.append(moved[:, (a - 1) * S : a * S])
             nc.scalar.dma_start(v_scale[a][0:100, :].bitcast(I32), v_scale[0][4 * a : 4 * a + 100, :].bitcast(I32))
         pick_words(0, 1)
+        w1_raw.append(head.tile([P, PASSES, H // 4], I32, name="w1_raw1", offset=0, align_bytes=64))
+        nc.sync.dma_start(w1_raw[1][:], w1_view[1])
+        gain_rows = head.tile([P, GROUPS * P], F32, name="gain_rows", offset=3 * KIB, align_bytes=64)
+        nc.gpsimd.memset(gain_rows[0 : P - SLOTS, :], 0.0)
+        nc.sync.dma_start(
+            gain_rows[P - SLOTS : P, :].rearrange("t (g i) -> t g i", i=8),
+            gain.rearrange("(g t i) -> t g i", t=SLOTS, i=8),
+        )
         for a in range(1, PASSES):
             for half in range(HALVES):
                 pick_words(a, half)
@@ -159,7 +163,10 @@ def tile_list_quilt_block_turn_kernel(tc, tab_words, tab_scales, offs, pos1, pos
         w2_view = w2.rearrange("(b q s i) (g n) -> g s b q i n", b=GROUPS, s=SLOTS, i=8, g=GROUPS)
         w2_columns = []
         for g in range(GROUPS):
-            w2_raw = keep.tile([P, SLOTS, GROUPS, H // GROUPS], F32, name="w2_raw%d" % g, tag="tab%d" % g, align_bytes=64)
+            if g == 0:
+                w2_raw = head.tile([P, SLOTS, GROUPS, H // GROUPS], F32, name="w2_raw0", offset=4 * KIB, align_bytes=64)
+            else:
+                w2_raw = keep.tile([P, SLOTS, GROUPS, H // GROUPS], F32, name="w2_raw1", tag="tab1", align_bytes=64)
             for s in range(SLOTS):
                 for b in range(GROUPS):
                     nc.sync.dma_start(w2_raw[:, s, b, :], w2_view[g, s, b])
@@ -229,23 +236,21 @@ def tile_list_quilt_block_turn_kernel(tc, tab_words, tab_scales, offs, pos1, pos
                 w2_codes[first + k] = codes[:, k * GROUPS * P : (k + 1) * GROUPS * P]
                 w2_scale[first + k] = scale[:, k * GROUPS * P : (k + 1) * GROUPS * P]
 
-        steps = [(a, half) for a in range(PASSES) for half in range(HALVES)]
-        for a, half in steps[:3]:
+        for half in range(HALVES):
             for j in range(SLOTS):
-                first_product(j, half, a)
-        for pair in range(SLOTS // 2):
-            for a, half in steps[3:]:
-                for j in (2 * pair, 2 * pair + 1):
-                    first_product(j, half, a)
-                    if a == PASSES - 1:
-                        evacuate(j, half)
-            for j in (2 * pair, 2 * pair + 1):
-                pick_ref(j)
-        for j in range(SLOTS, TILES):
-            for half in range(HALVES):
-                for a in range(PASSES):
-                    first_product(j, half, a)
-                evacuate(j, half)
+                first_product(j, half, 0)
+        for j in range(TILES):
+            if j < SLOTS:
+                for a in range(1, PASSES):
+                    for half in range(HALVES):
+                        first_product(j, half, a)
+                        if a == PASSES - 1:
+                            evacuate(j, half)
+            else:
+                for half in range(HALVES):
+                    for a in range(PASSES):
+                        first_product(j, half, a)
+                    evacuate(j, half)
             if j == SLOTS:
                 gain_sb = keep.tile([P, TILES], F32, name="gain_sb")
                 gain_bank = psum.tile([P, BANK], F32, name="bank")
@@ -282,8 +287,6 @@ def tile_list_quilt_block_turn_kernel(tc, tab_words, tab_scales, offs, pos1, pos
         out_view = out.rearrange("(b q t i) m -> b t q i m", b=GROUPS, t=SLOTS, i=8)
         y_bank = {}
         turns = {}
-        whole = {}
-        cosine = {}
         turned = {}
 
         def second_product(u):
@@ -300,24 +303,26 @@ def tile_list_quilt_block_turn_kernel(tc, tab_words, tab_scales, offs, pos1, pos
                         stop=(b == GROUPS - 1),
                     )
 
-        def count_turns(u):
-            shape = [P, len(RUNS[u]), M]
-            if u == 1:
-                turns[u] = shared.tile(shape, F32, name="turns_second", offset=12 * KIB, align_bytes=64)
-            else:
-                turns[u] = ring.tile(shape, F32, name="turns")
-            whole[u] = ring.tile(shape, I32, name="whole")
+        def measure(u):
+            turns[u] = ring3.tile([P, len(RUNS[u]), M], F32, name="turns")
             for k, j in enumerate(RUNS[u]):
                 nc.scalar.activation(turns[u][:, k, :], y_bank[j][:], ACT.Abs, scale=1.0 / (2.0 * math.pi))
-            nc.scalar.activation(whole[u][:].bitcast(U32), turns[u][:], ACT.Copy, bias=-0.25)
-            nc.vector.tensor_tensor(turns[u][:], turns[u][:], whole[u][:], ALU.subtract)
+
+        def reduce_angle(u):
+            shape = [P, len(RUNS[u]), M]
+            if u == 1:
+                whole = shared.tile(shape, I32, name="whole_second", offset=12 * KIB, align_bytes=64)
+            else:
+                whole = ring.tile(shape, I32, name="whole")
+            nc.scalar.activation(whole[:].bitcast(U32), turns[u][:], ACT.Copy, bias=-0.25)
+            nc.vector.tensor_tensor(turns[u][:], turns[u][:], whole[:], ALU.subtract)
 
         def turn_rot(u):
-            cosine[u] = ring.tile([P, len(RUNS[u]), M], F32, name="cosine")
-            nc.scalar.activation(cosine[u][:], turns[u][:], ACT.Sin, scale=-2.0 * math.pi, bias=0.5 * math.pi)
+            cosine = ring.tile([P, len(RUNS[u]), M], F32, name="cosine")
+            nc.scalar.activation(cosine[:], turns[u][:], ACT.Sin, scale=-2.0 * math.pi, bias=0.5 * math.pi)
             turned[u] = ring3.tile([P, len(RUNS[u]), M], F32, name="turned")
             for k, j in enumerate(RUNS[u]):
-                nc.vector.tensor_tensor(turned[u][:, k, :], h_sb[j][:].indirect(pos2_sb[:]), cosine[u][:, k, :], ALU.mult)
+                nc.vector.tensor_tensor(turned[u][:, k, :], h_sb[j][:].indirect(pos2_sb[:]), cosine[:, k, :], ALU.mult)
 
         def lean_ref(u):
             for j in RUNS[u]:
@@ -335,16 +340,18 @@ def tile_list_quilt_block_turn_kernel(tc, tab_words, tab_scales, offs, pos1, pos
         runs = len(RUNS)
         for u in range(runs - 1):
             second_product(u)
-        count_turns(0)
+        measure(0)
+        reduce_angle(0)
         lean_ref(0)
         for u in range(runs):
             if u == runs - 2:
                 weave_pair(6, 12 * KIB)
                 second_product(runs - 1)
             if u + 1 < runs:
-                count_turns(u + 1)
+                measure(u + 1)
             turn_rot(u)
             if u + 1 < runs:
+                reduce_angle(u + 1)
                 lean_ref(u + 1)
             if u >= 1:
                 finish(u - 1)

@@ -156,7 +156,7 @@ def tile_list_quilt_block_turn_kernel(tc, tab_words, tab_scales, offs, pos1, pos
 
         scale_rest = shared.tile([P, PASSES, SLOTS, P // 4], U32, name="w1_scale_rest", offset=16 * KIB, align_bytes=64)
         order_scales(nc.scalar.copy, scale_rest, 1)
-        for first, last, offset in ((0, 2, 0), (2, 3, 4 * KIB), (3, 4, 18 * KIB)):
+        for first, last, offset in ((0, 2, 0), (2, 3, 4 * KIB), (3, 4, 28 * KIB)):
             codes_rest = shared.tile([P, PASSES, last - first, P // 2], U32, name="w1_codes_rest%d" % first, offset=offset, align_bytes=64)
             order_codes(nc.scalar.copy, codes_rest, 1, slice(0, PASSES), slice(first, last))
 
@@ -236,21 +236,23 @@ def tile_list_quilt_block_turn_kernel(tc, tab_words, tab_scales, offs, pos1, pos
                 w2_codes[first + k] = codes[:, k * GROUPS * P : (k + 1) * GROUPS * P]
                 w2_scale[first + k] = scale[:, k * GROUPS * P : (k + 1) * GROUPS * P]
 
-        for half in range(HALVES):
+        steps = [(a, half) for a in range(PASSES) for half in range(HALVES)]
+        for a, half in steps[:3]:
             for j in range(SLOTS):
-                first_product(j, half, 0)
-        for j in range(TILES):
-            if j < SLOTS:
-                for a in range(1, PASSES):
-                    for half in range(HALVES):
-                        first_product(j, half, a)
-                        if a == PASSES - 1:
-                            evacuate(j, half)
-            else:
-                for half in range(HALVES):
-                    for a in range(PASSES):
-                        first_product(j, half, a)
-                    evacuate(j, half)
+                first_product(j, half, a)
+        for pair in range(SLOTS // 2):
+            for a, half in steps[3:]:
+                for j in (2 * pair, 2 * pair + 1):
+                    first_product(j, half, a)
+                    if a == PASSES - 1:
+                        evacuate(j, half)
+            for j in (2 * pair, 2 * pair + 1):
+                pick_ref(j)
+        for j in range(SLOTS, TILES):
+            for half in range(HALVES):
+                for a in range(PASSES):
+                    first_product(j, half, a)
+                evacuate(j, half)
             if j == SLOTS:
                 gain_sb = keep.tile([P, TILES], F32, name="gain_sb")
                 gain_bank = psum.tile([P, BANK], F32, name="bank")
@@ -267,6 +269,12 @@ def tile_list_quilt_block_turn_kernel(tc, tab_words, tab_scales, offs, pos1, pos
             if j in (5, 6):
                 bound(0, j - 5)
                 weigh(0, j - 5)
+        woven_rest = shared.tile([P, SLOTS, GROUPS * 16, 8, SLOTS], BF16, name="w2_woven_rest", offset=28 * KIB, align_bytes=64)
+
+        def weave_pair(pair):
+            slots = slice(2 * pair, 2 * pair + 2)
+            nc.scalar.copy(woven_rest[:, slots].rearrange("p k c i s -> p k c s i"), w2_columns[1][:, slots])
+
         codes_first = keep.tile([P, SLOTS * GROUPS * P], U32, name="w2_codes_first", tag="z_woven0", align_bytes=64)
         quantize_w2(woven_first, codes_first, 0, SLOTS)
         z_codes[1] = keep.tile([P, M], U32, name="z_codes1", align_bytes=64)
@@ -275,14 +283,10 @@ def tile_list_quilt_block_turn_kernel(tc, tab_words, tab_scales, offs, pos1, pos
             weigh(1, cut)
         for cut in range(CUTS):
             quantize_z(1, cut, cut + 1)
-
-        def weave_pair(first, offset):
-            woven = shared.tile([P, 2, GROUPS * 16, 8, SLOTS], BF16, name="w2_woven%d" % first, offset=offset, align_bytes=64)
-            nc.scalar.copy(woven[:].rearrange("p k c i s -> p k c s i"), w2_columns[1][:, first - SLOTS : first - SLOTS + 2])
-            codes = keep.tile([P, 2 * GROUPS * P], U32, name="w2_codes%d" % first, align_bytes=64)
-            quantize_w2(woven, codes, first, 2)
-
-        weave_pair(4, 20 * KIB)
+        for pair in range(2):
+            weave_pair(pair)
+        codes_rest = keep.tile([P, SLOTS * GROUPS * P], U32, name="w2_codes_rest", align_bytes=64)
+        quantize_w2(woven_rest, codes_rest, SLOTS, SLOTS)
 
         out_view = out.rearrange("(b q t i) m -> b t q i m", b=GROUPS, t=SLOTS, i=8)
         y_bank = {}
@@ -304,7 +308,10 @@ def tile_list_quilt_block_turn_kernel(tc, tab_words, tab_scales, offs, pos1, pos
                     )
 
         def measure(u):
-            turns[u] = ring3.tile([P, len(RUNS[u]), M], F32, name="turns")
+            if u == 0:
+                turns[u] = shared.tile([P, 1, M], F32, name="turns_first", offset=12 * KIB, align_bytes=64)
+            else:
+                turns[u] = ring3.tile([P, len(RUNS[u]), M], F32, name="turns")
             for k, j in enumerate(RUNS[u]):
                 nc.scalar.activation(turns[u][:, k, :], y_bank[j][:], ACT.Abs, scale=1.0 / (2.0 * math.pi))
 
@@ -320,7 +327,7 @@ def tile_list_quilt_block_turn_kernel(tc, tab_words, tab_scales, offs, pos1, pos
         def turn_rot(u):
             cosine = ring.tile([P, len(RUNS[u]), M], F32, name="cosine")
             nc.scalar.activation(cosine[:], turns[u][:], ACT.Sin, scale=-2.0 * math.pi, bias=0.5 * math.pi)
-            turned[u] = ring3.tile([P, len(RUNS[u]), M], F32, name="turned")
+            turned[u] = ring.tile([P, len(RUNS[u]), M], F32, name="turned")
             for k, j in enumerate(RUNS[u]):
                 nc.vector.tensor_tensor(turned[u][:, k, :], h_sb[j][:].indirect(pos2_sb[:]), cosine[:, k, :], ALU.mult)
 
@@ -338,15 +345,12 @@ def tile_list_quilt_block_turn_kernel(tc, tab_words, tab_scales, offs, pos1, pos
                 nc.sync.dma_start(out_view[j // SLOTS, j % SLOTS], ref[j])
 
         runs = len(RUNS)
-        for u in range(runs - 1):
+        for u in range(runs):
             second_product(u)
         measure(0)
         reduce_angle(0)
         lean_ref(0)
         for u in range(runs):
-            if u == runs - 2:
-                weave_pair(6, 12 * KIB)
-                second_product(runs - 1)
             if u + 1 < runs:
                 measure(u + 1)
             turn_rot(u)

@@ -56,7 +56,7 @@ def tile_list_quilt_block_turn_kernel(tc, tab_words, tab_scales, offs, pos1, pos
 
         tab_view = tab_words.rearrange("a p t i -> p a (t i)").bitcast(I32)
         w1_view = w1_words.bitcast(I32).rearrange("a p (b c) -> b p a c", b=GROUPS)
-        tab_sb = [head.tile([P, T], I32, name="tab0", offset=0, align_bytes=64)]
+        tab_sb = [head.tile([P, T], I32, name="tab0", offset=8 * KIB, align_bytes=64)]
         tab_sb.extend(keep.tile([P, T], I32, name="tab%d" % a, align_bytes=64) for a in range(1, PASSES))
         w1_raw = [keep.tile([P, PASSES, H // 4], I32, name="w1_raw0", align_bytes=64)]
         nc.sync.dma_start(offs_sb[:], offs)
@@ -111,6 +111,8 @@ def tile_list_quilt_block_turn_kernel(tc, tab_words, tab_scales, offs, pos1, pos
         def pick_words(a, half):
             if (a, half) == (0, 1):
                 v_words[a, half] = shared.tile([P, BANK], U32, name="v0_1", offset=24 * KIB, align_bytes=64)
+            elif (a, half) == (PASSES - 1, 0):
+                v_words[a, half] = keep.tile([P, BANK], U32, name="v2_0", tag="z_woven0", align_bytes=64)
             else:
                 v_words[a, half] = keep.tile([P, BANK], U32, name="v%d_%d" % (a, half), align_bytes=64)
             nc.vector.tensor_copy(
@@ -142,9 +144,9 @@ def tile_list_quilt_block_turn_kernel(tc, tab_words, tab_scales, offs, pos1, pos
             v_scale.append(moved[:, (a - 1) * S : a * S])
             nc.scalar.dma_start(v_scale[a][0:100, :].bitcast(I32), v_scale[0][4 * a : 4 * a + 100, :].bitcast(I32))
         pick_words(0, 1)
-        w1_raw.append(head.tile([P, PASSES, H // 4], I32, name="w1_raw1", offset=0, align_bytes=64))
+        w1_raw.append(head.tile([P, PASSES, H // 4], I32, name="w1_raw1", offset=10 * KIB, align_bytes=64))
         nc.sync.dma_start(w1_raw[1][:], w1_view[1])
-        gain_rows = head.tile([P, GROUPS * P], F32, name="gain_rows", offset=3 * KIB, align_bytes=64)
+        gain_rows = head.tile([P, GROUPS * P], F32, name="gain_rows", offset=13 * KIB, align_bytes=64)
         nc.gpsimd.memset(gain_rows[0 : P - SLOTS, :], 0.0)
         nc.sync.dma_start(
             gain_rows[P - SLOTS : P, :].rearrange("t (g i) -> t g i", i=8),
@@ -160,22 +162,20 @@ def tile_list_quilt_block_turn_kernel(tc, tab_words, tab_scales, offs, pos1, pos
             codes_rest = shared.tile([P, PASSES, last - first, P // 2], U32, name="w1_codes_rest%d" % first, offset=offset, align_bytes=64)
             order_codes(nc.scalar.copy, codes_rest, 1, slice(0, PASSES), slice(first, last))
 
-        w2_view = w2.rearrange("(b q s i) (g n) -> g s b q i n", b=GROUPS, s=SLOTS, i=8, g=GROUPS)
-        w2_columns = []
-        for g in range(GROUPS):
-            if g == 0:
-                w2_raw = head.tile([P, SLOTS, GROUPS, H // GROUPS], F32, name="w2_raw0", offset=4 * KIB, align_bytes=64)
-            else:
-                w2_raw = keep.tile([P, SLOTS, GROUPS, H // GROUPS], F32, name="w2_raw1", tag="tab1", align_bytes=64)
+        w2_view = w2.rearrange("(b q s i) (g n) -> g b s q i n", b=GROUPS, s=SLOTS, i=8, g=GROUPS)
+        woven_first = keep.tile([P, SLOTS, GROUPS, 16, 8, SLOTS], BF16, name="w2_woven_first", align_bytes=64)
+        for b in range(GROUPS):
+            raw_first = head.tile([P, SLOTS, H // GROUPS], F32, name="w2_raw_first%d" % b, offset=(2 + 12 * b) * KIB, align_bytes=64)
             for s in range(SLOTS):
-                for b in range(GROUPS):
-                    nc.sync.dma_start(w2_raw[:, s, b, :], w2_view[g, s, b])
-            w2_columns.append(w2_raw[:].rearrange("p s b (q t i) -> p t (b q) s i", t=SLOTS, i=8))
-        woven_first = keep.tile([P, SLOTS, GROUPS * 16, 8, SLOTS], BF16, name="w2_woven_first", align_bytes=64)
-        for t in range(SLOTS):
-            nc.gpsimd.tensor_scalar(
-                woven_first[:, t], w2_columns[0][:, t].rearrange("p c s i -> p c i s"), 1.0, 0.0, ALU.mult, ALU.add
-            )
+                nc.sync.dma_start(raw_first[:, s, :], w2_view[0, b, s])
+            columns = raw_first[:].rearrange("p s (q t i) -> p t q i s", t=SLOTS, i=8)
+            for t in range(SLOTS):
+                nc.gpsimd.tensor_scalar(woven_first[:, t, b], columns[:, t], 1.0, 0.0, ALU.mult, ALU.add)
+        raw_rest = keep.tile([P, SLOTS, GROUPS, H // GROUPS], F32, name="w2_raw_rest", tag="tab1", align_bytes=64)
+        for b in range(GROUPS):
+            for s in range(SLOTS):
+                nc.sync.dma_start(raw_rest[:, s, b, :], w2_view[1, b, s])
+        rest_columns = raw_rest[:].rearrange("p s b (q t i) -> p t (b q) s i", t=SLOTS, i=8)
 
         h_sb = [keep.tile([P, S], F32, name="h%d" % j) for j in range(TILES)]
         ref_all = keep.tile([P, TILES, M], F32, name="ref_all")
@@ -230,7 +230,7 @@ def tile_list_quilt_block_turn_kernel(tc, tab_words, tab_scales, offs, pos1, pos
             nc.vector.quantize_mx(
                 out=codes[:].bitcast(FP8X4),
                 scales=scale[:],
-                in_=woven[:].rearrange("p k c i s -> p (k c i s)"),
+                in_=woven,
             )
             for k in range(count):
                 w2_codes[first + k] = codes[:, k * GROUPS * P : (k + 1) * GROUPS * P]
@@ -262,21 +262,21 @@ def tile_list_quilt_block_turn_kernel(tc, tab_words, tab_scales, offs, pos1, pos
                     gain_sb[:].rearrange("p (b t) -> p b t", t=SLOTS),
                     gain_bank[:, 0 : GROUPS * P].rearrange("p (b c) -> p b c", b=GROUPS)[:, :, P - SLOTS : P],
                 )
-            if j == TILES - 1:
-                z_codes[0] = shared.tile([P, M], U32, name="z_codes0", offset=16 * KIB, align_bytes=64)
-                quantize_z(0, 0, 2)
             pick_ref(j)
             if j in (5, 6):
                 bound(0, j - 5)
-                weigh(0, j - 5)
+        for cut in range(CUTS):
+            weigh(0, cut)
+        z_codes[0] = keep.tile([P, M], U32, name="z_codes0", align_bytes=64)
+        quantize_z(0, 0, 2)
         woven_rest = shared.tile([P, SLOTS, GROUPS * 16, 8, SLOTS], BF16, name="w2_woven_rest", offset=28 * KIB, align_bytes=64)
 
         def weave_pair(pair):
             slots = slice(2 * pair, 2 * pair + 2)
-            nc.scalar.copy(woven_rest[:, slots].rearrange("p k c i s -> p k c s i"), w2_columns[1][:, slots])
+            nc.scalar.copy(woven_rest[:, slots].rearrange("p k c i s -> p k c s i"), rest_columns[:, slots])
 
         codes_first = keep.tile([P, SLOTS * GROUPS * P], U32, name="w2_codes_first", tag="z_woven0", align_bytes=64)
-        quantize_w2(woven_first, codes_first, 0, SLOTS)
+        quantize_w2(woven_first[:].rearrange("p t b q i s -> p (t b q i s)"), codes_first, 0, SLOTS)
         z_codes[1] = keep.tile([P, M], U32, name="z_codes1", align_bytes=64)
         for cut in range(CUTS):
             bound(1, cut)
@@ -286,7 +286,7 @@ def tile_list_quilt_block_turn_kernel(tc, tab_words, tab_scales, offs, pos1, pos
         for pair in range(2):
             weave_pair(pair)
         codes_rest = keep.tile([P, SLOTS * GROUPS * P], U32, name="w2_codes_rest", align_bytes=64)
-        quantize_w2(woven_rest, codes_rest, SLOTS, SLOTS)
+        quantize_w2(woven_rest[:].rearrange("p t c i s -> p (t c i s)"), codes_rest, SLOTS, SLOTS)
 
         out_view = out.rearrange("(b q t i) m -> b t q i m", b=GROUPS, t=SLOTS, i=8)
         y_bank = {}

@@ -45,13 +45,15 @@ def tile_list_quilt_block_turn_kernel(tc, tab_words, tab_scales, offs, pos1, pos
         offs_sb = keep.tile([P, S // 16], U16, name="offs_sb")
         pos1_sb = keep.tile([P, M // 16], U16, name="pos1_sb")
         pos2_sb = keep.tile([P, M // 16], U16, name="pos2_sb")
-        tab_scale = shared.tile([P, T], U8, name="tab_scale", offset=25 * KIB, align_bytes=64)
+        tab_scale = shared.tile([P, T], U8, name="tab_scale", offset=24 * KIB, align_bytes=64)
         w1_scale_raw = keep.tile([P, PASSES, H // 4], U32, name="w1_scale_raw", align_bytes=64)
         v_scale = [keep.tile([P, S], U8, name="v_scale0", align_bytes=64)]
         warm = keep.tile([P, 2], F32, name="warm")
         ident = keep.tile([P, P], F32, name="ident")
         nc.gpsimd.memset(tab_scale[:].bitcast(I32), 0)
         nc.vector.memset(w1_scale_raw[:].bitcast(I32), 0)
+        moved = shared.tile([P, (PASSES - 1) * S], U8, name="moved_scale", offset=26 * KIB, align_bytes=64)
+        nc.vector.memset(moved[96:P, :].bitcast(I32), 0)
         nc.vector.memset(warm[:, 0:1], 0.0)
 
         tab_view = tab_words.rearrange("a p t i -> p a (t i)").bitcast(I32)
@@ -60,21 +62,21 @@ def tile_list_quilt_block_turn_kernel(tc, tab_words, tab_scales, offs, pos1, pos
         tab_sb.extend(keep.tile([P, T], I32, name="tab%d" % a, align_bytes=64) for a in range(1, PASSES))
         w1_raw = [keep.tile([P, PASSES, H // 4], I32, name="w1_raw0", align_bytes=64)]
         nc.sync.dma_start(offs_sb[:], offs)
-        nc.sync.dma_start(tab_sb[0][:], tab_view[:, 0, :])
+        nc.sync.dma_start(pos1_sb[:], pos1)
         for quad in range(4):
-            nc.scalar.dma_start(
+            (nc.scalar if quad < 2 else nc.sync).dma_start(
                 tab_scale[32 * quad : 32 * quad + 4 * PASSES, :].bitcast(I32),
                 tab_scales[:, 4 * quad : 4 * quad + 4, :].bitcast(I32),
             )
-        nc.sync.dma_start(w1_raw[0][:], w1_view[0])
         for quad in range(4):
-            (nc.sync if quad < 2 else nc.scalar).dma_start(
+            (nc.scalar if quad < 2 else nc.sync).dma_start(
                 w1_scale_raw[32 * quad : 32 * quad + 4].bitcast(I32),
                 w1_scales[:, 4 * quad : 4 * quad + 4, :].bitcast(I32).rearrange("a r c -> r a c"),
             )
-        nc.sync.dma_start(tab_sb[1][:], tab_view[:, 1, :])
-        nc.sync.dma_start(tab_sb[2][:], tab_view[:, 2, :])
-        nc.sync.dma_start(pos1_sb[:], pos1)
+        nc.sync.dma_start(tab_sb[0][:], tab_view[:, 0, :])
+        nc.sync.dma_start(w1_raw[0][:], w1_view[0])
+        for a in range(1, PASSES):
+            nc.sync.dma_start(tab_sb[a][:], tab_view[:, a, :])
         nc.sync.dma_start(pos2_sb[:], pos2)
         make_identity(nc, ident[:])
         nc.scalar.activation(warm[:, 1:2], warm[:, 0:1], ACT.Silu)
@@ -103,18 +105,16 @@ def tile_list_quilt_block_turn_kernel(tc, tab_words, tab_scales, offs, pos1, pos
         codes_head = keep.tile([P, PASSES, SLOTS, P // 2], U32, name="w1_codes_head", align_bytes=64)
         order_codes(nc.scalar.copy, codes_head, 0, slice(0, PASSES), slice(0, SLOTS))
         scale_head = keep.tile([P, PASSES, SLOTS, P // 4], U32, name="w1_scale_head", align_bytes=64)
-        order_scales(nc.gpsimd.tensor_copy, scale_head, 0)
+        order_scales(nc.scalar.copy, scale_head, 0)
 
         v_words = {}
         h_bank = {}
 
         def pick_words(a, half):
-            if (a, half) == (0, 1):
-                v_words[a, half] = shared.tile([P, BANK], U32, name="v0_1", offset=24 * KIB, align_bytes=64)
-            elif (a, half) == (PASSES - 1, 0):
+            if (a, half) == (PASSES - 1, 0):
                 v_words[a, half] = keep.tile([P, BANK], U32, name="v2_0", tag="z_woven0", align_bytes=64)
             else:
-                v_words[a, half] = keep.tile([P, BANK], U32, name="v%d_%d" % (a, half), align_bytes=64)
+                v_words[a, half] = keep.tile([P, BANK], U32, name="v%d_%d" % (a, half), tag="v%d_%d" % (a, half), align_bytes=64)
             nc.vector.tensor_copy(
                 v_words[a, half][:], tab_sb[a][:].bitcast(U32).indirect(offs_sb[:, half * BANK // 16 : (half + 1) * BANK // 16])
             )
@@ -132,14 +132,8 @@ def tile_list_quilt_block_turn_kernel(tc, tab_words, tab_scales, offs, pos1, pos
                 stop=(a == PASSES - 1),
             )
 
+        nc.vector.tensor_copy(v_scale[0][:], tab_scale[:].indirect(offs_sb[:]))
         pick_words(0, 0)
-        for half in range(HALVES):
-            nc.vector.tensor_copy(
-                v_scale[0][:, half * BANK : (half + 1) * BANK],
-                tab_scale[:].indirect(offs_sb[:, half * BANK // 16 : (half + 1) * BANK // 16]),
-            )
-        moved = keep.tile([P, (PASSES - 1) * S], U8, name="moved_scale", tag="w1_raw0", align_bytes=64)
-        nc.gpsimd.memset(moved[96:P, :].bitcast(I32), 0)
         for a in range(1, PASSES):
             v_scale.append(moved[:, (a - 1) * S : a * S])
             nc.scalar.dma_start(v_scale[a][0:100, :].bitcast(I32), v_scale[0][4 * a : 4 * a + 100, :].bitcast(I32))
@@ -181,7 +175,7 @@ def tile_list_quilt_block_turn_kernel(tc, tab_words, tab_scales, offs, pos1, pos
         ref_all = keep.tile([P, TILES, M], F32, name="ref_all")
         ref_group = [ref_all[:, b * SLOTS : (b + 1) * SLOTS, :] for b in range(GROUPS)]
         ref = [ref_all[:, j, :] for j in range(TILES)]
-        z_codes = {}
+        z_codes = [keep.tile([P, M], U32, name="z_codes%d" % b, tag="v%d_0" % b, align_bytes=64) for b in range(GROUPS)]
         z_scale = [keep.tile([P, M], U8, name="z_scale%d" % b, align_bytes=64) for b in range(GROUPS)]
         z_woven = [keep.tile([P, M * SLOTS // 2], U32, name="z_woven%d" % b, align_bytes=64) for b in range(GROUPS)]
         z_woven = [woven[:].bitcast(BF16).rearrange("p (m t) -> p m t", t=SLOTS) for woven in z_woven]
@@ -267,17 +261,15 @@ def tile_list_quilt_block_turn_kernel(tc, tab_words, tab_scales, offs, pos1, pos
                 bound(0, j - 5)
         for cut in range(CUTS):
             weigh(0, cut)
-        z_codes[0] = keep.tile([P, M], U32, name="z_codes0", align_bytes=64)
-        quantize_z(0, 0, 2)
         woven_rest = shared.tile([P, SLOTS, GROUPS * 16, 8, SLOTS], BF16, name="w2_woven_rest", offset=28 * KIB, align_bytes=64)
 
         def weave_pair(pair):
             slots = slice(2 * pair, 2 * pair + 2)
             nc.scalar.copy(woven_rest[:, slots].rearrange("p k c i s -> p k c s i"), rest_columns[:, slots])
 
-        codes_first = keep.tile([P, SLOTS * GROUPS * P], U32, name="w2_codes_first", tag="z_woven0", align_bytes=64)
+        codes_first = shared.tile([P, SLOTS * GROUPS * P], U32, name="w2_codes_first", offset=4 * KIB, align_bytes=64)
         quantize_w2(woven_first[:].rearrange("p t b q i s -> p (t b q i s)"), codes_first, 0, SLOTS)
-        z_codes[1] = keep.tile([P, M], U32, name="z_codes1", align_bytes=64)
+        quantize_z(0, 0, 2)
         for cut in range(CUTS):
             bound(1, cut)
             weigh(1, cut)

@@ -62,14 +62,13 @@ def tile_list_quilt_block_turn_kernel(tc, tab_words, tab_scales, offs, pos1, pos
         tab_sb.extend(keep.tile([P, T], I32, name="tab%d" % a, align_bytes=64) for a in range(1, PASSES))
         w1_raw = [keep.tile([P, PASSES, H // 4], I32, name="w1_raw0", align_bytes=64)]
         nc.sync.dma_start(offs_sb[:], offs)
-        nc.sync.dma_start(pos1_sb[:], pos1)
         for quad in range(4):
             (nc.scalar if quad < 2 else nc.sync).dma_start(
                 tab_scale[32 * quad : 32 * quad + 4 * PASSES, :].bitcast(I32),
                 tab_scales[:, 4 * quad : 4 * quad + 4, :].bitcast(I32),
             )
         for quad in range(4):
-            (nc.scalar if quad < 2 else nc.sync).dma_start(
+            nc.scalar.dma_start(
                 w1_scale_raw[32 * quad : 32 * quad + 4].bitcast(I32),
                 w1_scales[:, 4 * quad : 4 * quad + 4, :].bitcast(I32).rearrange("a r c -> r a c"),
             )
@@ -77,6 +76,7 @@ def tile_list_quilt_block_turn_kernel(tc, tab_words, tab_scales, offs, pos1, pos
         nc.sync.dma_start(w1_raw[0][:], w1_view[0])
         for a in range(1, PASSES):
             nc.sync.dma_start(tab_sb[a][:], tab_view[:, a, :])
+        nc.sync.dma_start(pos1_sb[:], pos1)
         nc.sync.dma_start(pos2_sb[:], pos2)
         make_identity(nc, ident[:])
         nc.scalar.activation(warm[:, 1:2], warm[:, 0:1], ACT.Silu)
@@ -86,7 +86,7 @@ def tile_list_quilt_block_turn_kernel(tc, tab_words, tab_scales, offs, pos1, pos
 
         def order_codes(copy, codes, b, passes, slots):
             copy(
-                codes[:].rearrange("p a t (q i) -> p a t q i", i=4),
+                codes.rearrange("p a t (q i) -> p a t q i", i=4),
                 w1_raw[b][:].bitcast(U32).rearrange("p a (q t i) -> p a t q i", t=SLOTS, i=4)[:, passes, slots],
             )
             for a in range(passes.start, passes.stop):
@@ -103,9 +103,10 @@ def tile_list_quilt_block_turn_kernel(tc, tab_words, tab_scales, offs, pos1, pos
                     w1_scale[a, SLOTS * b + t] = scale[:, a, t, :]
 
         codes_head = keep.tile([P, PASSES, SLOTS, P // 2], U32, name="w1_codes_head", align_bytes=64)
-        order_codes(nc.scalar.copy, codes_head, 0, slice(0, PASSES), slice(0, SLOTS))
         scale_head = keep.tile([P, PASSES, SLOTS, P // 4], U32, name="w1_scale_head", align_bytes=64)
         order_scales(nc.scalar.copy, scale_head, 0)
+        for passes in (slice(0, 1), slice(1, PASSES)):
+            order_codes(nc.scalar.copy, codes_head[:, passes], 0, passes, slice(0, SLOTS))
 
         v_words = {}
         h_bank = {}
@@ -136,7 +137,7 @@ def tile_list_quilt_block_turn_kernel(tc, tab_words, tab_scales, offs, pos1, pos
         pick_words(0, 0)
         for a in range(1, PASSES):
             v_scale.append(moved[:, (a - 1) * S : a * S])
-            nc.scalar.dma_start(v_scale[a][0:100, :].bitcast(I32), v_scale[0][4 * a : 4 * a + 100, :].bitcast(I32))
+            nc.sync.dma_start(v_scale[a][0:100, :].bitcast(I32), v_scale[0][4 * a : 4 * a + 100, :].bitcast(I32))
         pick_words(0, 1)
         w1_raw.append(head.tile([P, PASSES, H // 4], I32, name="w1_raw1", offset=10 * KIB, align_bytes=64))
         nc.sync.dma_start(w1_raw[1][:], w1_view[1])
@@ -154,7 +155,7 @@ def tile_list_quilt_block_turn_kernel(tc, tab_words, tab_scales, offs, pos1, pos
         order_scales(nc.scalar.copy, scale_rest, 1)
         for first, last, offset in ((0, 2, 0), (2, 3, 4 * KIB), (3, 4, 28 * KIB)):
             codes_rest = shared.tile([P, PASSES, last - first, P // 2], U32, name="w1_codes_rest%d" % first, offset=offset, align_bytes=64)
-            order_codes(nc.scalar.copy, codes_rest, 1, slice(0, PASSES), slice(first, last))
+            order_codes(nc.scalar.copy, codes_rest[:], 1, slice(0, PASSES), slice(first, last))
 
         w2_view = w2.rearrange("(b q s i) (g n) -> g b s q i n", b=GROUPS, s=SLOTS, i=8, g=GROUPS)
         woven_first = keep.tile([P, SLOTS, GROUPS, 16, 8, SLOTS], BF16, name="w2_woven_first", align_bytes=64)

@@ -62,6 +62,7 @@ def tile_list_quilt_block_turn_kernel(tc, tab_words, tab_scales, offs, pos1, pos
         tab_sb.extend(keep.tile([P, T], I32, name="tab%d" % a, align_bytes=64) for a in range(1, PASSES))
         w1_raw = [keep.tile([P, PASSES, H // 4], I32, name="w1_raw0", align_bytes=64)]
         nc.sync.dma_start(offs_sb[:], offs)
+        nc.sync.dma_start(pos1_sb[:], pos1)
         for quad in range(4):
             (nc.scalar if quad < 2 else nc.sync).dma_start(
                 tab_scale[32 * quad : 32 * quad + 4 * PASSES, :].bitcast(I32),
@@ -76,7 +77,6 @@ def tile_list_quilt_block_turn_kernel(tc, tab_words, tab_scales, offs, pos1, pos
         nc.sync.dma_start(w1_raw[0][:], w1_view[0])
         for a in range(1, PASSES):
             nc.sync.dma_start(tab_sb[a][:], tab_view[:, a, :])
-        nc.sync.dma_start(pos1_sb[:], pos1)
         nc.sync.dma_start(pos2_sb[:], pos2)
         make_identity(nc, ident[:])
         nc.scalar.activation(warm[:, 1:2], warm[:, 0:1], ACT.Silu)

@@ -30,6 +30,7 @@ KIB = 1024
 FLOPS = 2 * K * H * S + 2 * H * H * M
 
 RUNS = ((0,), (1, 2), (3, 4, 5), (6, 7))
+TENSOR_SUMS = 4
 
 
 def tile_list_quilt_block_turn_kernel(tc, tab_words, tab_scales, offs, pos1, pos2, w1_words, w1_scales, gain, w2, out):
@@ -37,7 +38,6 @@ def tile_list_quilt_block_turn_kernel(tc, tab_words, tab_scales, offs, pos1, pos
     with ExitStack() as ctx:
         keep = ctx.enter_context(tc.tile_pool(name="keep", bufs=1))
         ring = ctx.enter_context(tc.tile_pool(name="ring", bufs=2))
-        ring3 = ctx.enter_context(tc.tile_pool(name="ring3", bufs=3))
         shared = ctx.enter_context(tc.tile_pool(name="shared", bufs=1))
         head = ctx.enter_context(tc.tile_pool(name="head", bufs=1))
         psum = ctx.enter_context(tc.psum_pool(name="psum", bufs=8))
@@ -62,7 +62,6 @@ def tile_list_quilt_block_turn_kernel(tc, tab_words, tab_scales, offs, pos1, pos
         tab_sb.extend(keep.tile([P, T], I32, name="tab%d" % a, align_bytes=64) for a in range(1, PASSES))
         w1_raw = [keep.tile([P, PASSES, H // 4], I32, name="w1_raw0", align_bytes=64)]
         nc.sync.dma_start(offs_sb[:], offs)
-        nc.sync.dma_start(pos1_sb[:], pos1)
         for quad in range(4):
             (nc.scalar if quad < 2 else nc.sync).dma_start(
                 tab_scale[32 * quad : 32 * quad + 4 * PASSES, :].bitcast(I32),
@@ -77,6 +76,7 @@ def tile_list_quilt_block_turn_kernel(tc, tab_words, tab_scales, offs, pos1, pos
         nc.sync.dma_start(w1_raw[0][:], w1_view[0])
         for a in range(1, PASSES):
             nc.sync.dma_start(tab_sb[a][:], tab_view[:, a, :])
+        nc.sync.dma_start(pos1_sb[:], pos1)
         nc.sync.dma_start(pos2_sb[:], pos2)
         make_identity(nc, ident[:])
         nc.scalar.activation(warm[:, 1:2], warm[:, 0:1], ACT.Silu)
@@ -285,6 +285,7 @@ def tile_list_quilt_block_turn_kernel(tc, tab_words, tab_scales, offs, pos1, pos
         y_bank = {}
         turns = {}
         turned = {}
+        cosine = {}
 
         def second_product(u):
             for j in RUNS[u]:
@@ -304,7 +305,7 @@ def tile_list_quilt_block_turn_kernel(tc, tab_words, tab_scales, offs, pos1, pos
             if u == 0:
                 turns[u] = shared.tile([P, 1, M], F32, name="turns_first", offset=12 * KIB, align_bytes=64)
             else:
-                turns[u] = ring3.tile([P, len(RUNS[u]), M], F32, name="turns")
+                turns[u] = head.tile([P, len(RUNS[u]), M], F32, name="turns%d" % u, offset=(14 + 2 * RUNS[u][0]) * KIB, align_bytes=64)
             for k, j in enumerate(RUNS[u]):
                 nc.scalar.activation(turns[u][:, k, :], y_bank[j][:], ACT.Abs, scale=1.0 / (2.0 * math.pi))
 
@@ -317,25 +318,44 @@ def tile_list_quilt_block_turn_kernel(tc, tab_words, tab_scales, offs, pos1, pos
             nc.scalar.activation(whole[:].bitcast(U32), turns[u][:], ACT.Copy, bias=-0.25)
             nc.vector.tensor_tensor(turns[u][:], turns[u][:], whole[:], ALU.subtract)
 
+        def sine(u):
+            cosine[u] = ring.tile([P, len(RUNS[u]), M], F32, name="cosine")
+            nc.scalar.activation(cosine[u][:], turns[u][:], ACT.Sin, scale=-2.0 * math.pi, bias=0.5 * math.pi)
+
+        def turn_tile(u, k):
+            j = RUNS[u][k]
+            turned[j] = head.tile([P, M], F32, name="turned%d" % j, offset=2 * j * KIB, align_bytes=64)
+            nc.vector.tensor_tensor(turned[j][:], h_sb[j][:].indirect(pos2_sb[:]), cosine[u][:, k, :], ALU.mult)
+
         def turn_rot(u):
-            cosine = ring.tile([P, len(RUNS[u]), M], F32, name="cosine")
-            nc.scalar.activation(cosine[:], turns[u][:], ACT.Sin, scale=-2.0 * math.pi, bias=0.5 * math.pi)
-            turned[u] = ring.tile([P, len(RUNS[u]), M], F32, name="turned")
-            for k, j in enumerate(RUNS[u]):
-                nc.vector.tensor_tensor(turned[u][:, k, :], h_sb[j][:].indirect(pos2_sb[:]), cosine[:, k, :], ALU.mult)
+            for k in range(len(RUNS[u])):
+                turn_tile(u, k)
 
         def lean_ref(u):
             for j in RUNS[u]:
                 nc.vector.tensor_tensor(ref[j], y_bank[j][:], ref[j], ALU.mult)
 
-        def finish(u):
-            if len(RUNS[u]) > 2:
-                rows = ref_all[:, RUNS[u][0] : RUNS[u][-1] + 1, :]
-                nc.vector.tensor_tensor(rows, turned[u][:], rows, ALU.add)
-            for k, j in enumerate(RUNS[u]):
-                if len(RUNS[u]) <= 2:
-                    nc.vector.tensor_tensor(ref[j], turned[u][:, k, :], ref[j], ALU.add)
-                nc.sync.dma_start(out_view[j // SLOTS, j % SLOTS], ref[j])
+        across = {}
+        flipped = {}
+        blocks = [slice(c * P, (c + 1) * P) for c in range(M // P)]
+
+        def add_across(j):
+            across[j] = psum.tile([P, BANK], F32, name="bank")
+            for block in blocks:
+                nc.tensor.matmul(across[j][:, block], lhsT=turned[j][:, block], rhs=ident[:], is_transpose=True, start=True, stop=False)
+                nc.tensor.matmul(across[j][:, block], lhsT=ref[j][:, block], rhs=ident[:], is_transpose=True, start=False, stop=True)
+            flipped[j] = head.tile([P, BANK], F32, name="flipped%d" % j, offset=(16, 26, 28, 20, 22)[j] * KIB, align_bytes=64)
+            nc.scalar.copy(flipped[j][:], across[j][:])
+
+        def turn_back(j):
+            back = psum.tile([P, BANK], F32, name="bank")
+            for block in blocks:
+                nc.tensor.transpose(back[:, block], flipped[j][:, block], ident[:])
+            nc.scalar.copy(ref[j], back[:])
+            store(nc.scalar, j)
+
+        def store(queue, j):
+            queue.dma_start(out_view[j // SLOTS, j % SLOTS], ref[j])
 
         runs = len(RUNS)
         for u in range(runs):
@@ -343,13 +363,27 @@ def tile_list_quilt_block_turn_kernel(tc, tab_words, tab_scales, offs, pos1, pos
         measure(0)
         reduce_angle(0)
         lean_ref(0)
-        for u in range(runs):
-            if u + 1 < runs:
-                measure(u + 1)
+        for u in range(runs - 2):
+            measure(u + 1)
+            sine(u)
             turn_rot(u)
-            if u + 1 < runs:
-                reduce_angle(u + 1)
-                lean_ref(u + 1)
-            if u >= 1:
-                finish(u - 1)
-        finish(runs - 1)
+            reduce_angle(u + 1)
+            lean_ref(u + 1)
+        measure(runs - 1)
+        reduce_angle(runs - 1)
+        lean_ref(runs - 1)
+        add_across(0)
+        sine(runs - 2)
+        turn_back(0)
+        sine(runs - 1)
+        turn_rot(runs - 2)
+        add_across(1)
+        for j in range(2, TENSOR_SUMS):
+            add_across(j)
+            turn_back(j - 1)
+        turn_back(TENSOR_SUMS - 1)
+        for j in range(TENSOR_SUMS, TILES):
+            nc.vector.tensor_tensor(ref[j], turned[j][:], ref[j], ALU.add)
+            store(nc.sync, j)
+            if j - TENSOR_SUMS < len(RUNS[-1]):
+                turn_tile(runs - 1, j - TENSOR_SUMS)

@@ -114,6 +114,8 @@ def tile_list_quilt_block_turn_kernel(tc, tab_words, tab_scales, offs, pos1, pos
         def pick_words(a, half):
             if (a, half) == (PASSES - 1, 0):
                 v_words[a, half] = keep.tile([P, BANK], U32, name="v2_0", tag="z_woven0", align_bytes=64)
+            elif (a, half) == (0, 1):
+                v_words[a, half] = shared.tile([P, BANK], U32, name="v0_1", offset=24 * KIB, align_bytes=64)
             else:
                 v_words[a, half] = keep.tile([P, BANK], U32, name="v%d_%d" % (a, half), tag="v%d_%d" % (a, half), align_bytes=64)
             nc.vector.tensor_copy(
@@ -133,8 +135,8 @@ def tile_list_quilt_block_turn_kernel(tc, tab_words, tab_scales, offs, pos1, pos
                 stop=(a == PASSES - 1),
             )
 
-        nc.vector.tensor_copy(v_scale[0][:], tab_scale[:].indirect(offs_sb[:]))
         pick_words(0, 0)
+        nc.vector.tensor_copy(v_scale[0][:], tab_scale[:].indirect(offs_sb[:]))
         for a in range(1, PASSES):
             v_scale.append(moved[:, (a - 1) * S : a * S])
             nc.sync.dma_start(v_scale[a][0:100, :].bitcast(I32), v_scale[0][4 * a : 4 * a + 100, :].bitcast(I32))
@@ -232,11 +234,11 @@ def tile_list_quilt_block_turn_kernel(tc, tab_words, tab_scales, offs, pos1, pos
                 w2_scale[first + k] = scale[:, k * GROUPS * P : (k + 1) * GROUPS * P]
 
         steps = [(a, half) for a in range(PASSES) for half in range(HALVES)]
-        for a, half in steps[:3]:
+        for a, half in steps[:HALVES]:
             for j in range(SLOTS):
                 first_product(j, half, a)
         for pair in range(SLOTS // 2):
-            for a, half in steps[3:]:
+            for a, half in steps[HALVES:]:
                 for j in (2 * pair, 2 * pair + 1):
                     first_product(j, half, a)
                     if a == PASSES - 1:

@@ -53,7 +53,8 @@ def tile_list_quilt_block_turn_kernel(tc, tab_words, tab_scales, offs, pos1, pos
         nc.gpsimd.memset(tab_scale[:].bitcast(I32), 0)
         nc.vector.memset(w1_scale_raw[:].bitcast(I32), 0)
         moved = shared.tile([P, (PASSES - 1) * S], U8, name="moved_scale", offset=26 * KIB, align_bytes=64)
-        nc.vector.memset(moved[96:P, :].bitcast(I32), 0)
+        for upper in (32, 96):
+            nc.vector.memset(moved[upper : upper + 32, :].bitcast(I32), 0)
         nc.vector.memset(warm[:, 0:1], 0.0)
 
         tab_view = tab_words.rearrange("a p t i -> p a (t i)").bitcast(I32)
@@ -139,7 +140,10 @@ def tile_list_quilt_block_turn_kernel(tc, tab_words, tab_scales, offs, pos1, pos
         nc.vector.tensor_copy(v_scale[0][:], tab_scale[:].indirect(offs_sb[:]))
         for a in range(1, PASSES):
             v_scale.append(moved[:, (a - 1) * S : a * S])
-            nc.sync.dma_start(v_scale[a][0:100, :].bitcast(I32), v_scale[0][4 * a : 4 * a + 100, :].bitcast(I32))
+            for first in (0, 64):
+                nc.sync.dma_start(
+                    v_scale[a][first : first + 36, :].bitcast(I32), v_scale[0][first + 4 * a : first + 4 * a + 36, :].bitcast(I32)
+                )
         pick_words(0, 1)
         w1_raw.append(head.tile([P, PASSES, H // 4], I32, name="w1_raw1", offset=10 * KIB, align_bytes=64))
         nc.sync.dma_start(w1_raw[1][:], w1_view[1])

import math
from contextlib import ExitStack

import concourse.mybir as mybir
from concourse.masks import make_identity

F32 = mybir.dt.float32
BF16 = mybir.dt.bfloat16
I32 = mybir.dt.int32
U32 = mybir.dt.uint32
U16 = mybir.dt.uint16
U8 = mybir.dt.uint8
FP8X4 = mybir.dt.float8_e4m3fn_x4
FP4X4 = mybir.dt.float4_e2m1fn_x4
ALU = mybir.AluOpType
ACT = mybir.ActivationFunctionType

K, T, S, M, H = 1536, 2048, 1024, 512, 1024
P = 128
PASSES = K // 512
GROUPS = H // 512
SLOTS = 4
TILES = GROUPS * SLOTS
BANK = 512
HALVES = S // BANK
CUTS = 2
CW = M // CUTS
KIB = 1024

FLOPS = 2 * K * H * S + 2 * H * H * M

RUNS = ((0,), (1, 2), (3, 4, 5), (6, 7))
TENSOR_SUMS = 4


def tile_list_quilt_block_turn_kernel(tc, tab_words, tab_scales, offs, pos1, pos2, w1_words, w1_scales, gain, w2, out):
    nc = tc.nc
    with ExitStack() as ctx:
        keep = ctx.enter_context(tc.tile_pool(name="keep", bufs=1))
        ring = ctx.enter_context(tc.tile_pool(name="ring", bufs=2))
        shared = ctx.enter_context(tc.tile_pool(name="shared", bufs=1))
        head = ctx.enter_context(tc.tile_pool(name="head", bufs=1))
        psum = ctx.enter_context(tc.psum_pool(name="psum", bufs=8))

        offs_sb = keep.tile([P, S // 16], U16, name="offs_sb")
        pos1_sb = keep.tile([P, M // 16], U16, name="pos1_sb")
        pos2_sb = keep.tile([P, M // 16], U16, name="pos2_sb")
        tab_scale = shared.tile([P, T], U8, name="tab_scale", offset=24 * KIB, align_bytes=64)
        w1_scale_raw = keep.tile([P, PASSES, H // 4], U32, name="w1_scale_raw", align_bytes=64)
        v_scale = [keep.tile([P, S], U8, name="v_scale0", align_bytes=64)]
        warm = keep.tile([P, 2], F32, name="warm")
        ident = keep.tile([P, P], F32, name="ident")
        nc.gpsimd.memset(tab_scale[:].bitcast(I32), 0)
        nc.vector.memset(w1_scale_raw[:].bitcast(I32), 0)
        moved = shared.tile([P, (PASSES - 1) * S], U8, name="moved_scale", offset=26 * KIB, align_bytes=64)
        for upper in (32, 96):
            nc.vector.memset(moved[upper : upper + 32, :].bitcast(I32), 0)
        nc.vector.memset(warm[:, 0:1], 0.0)

        tab_view = tab_words.rearrange("a p t i -> p a (t i)").bitcast(I32)
        w1_view = w1_words.bitcast(I32).rearrange("a p (b c) -> b p a c", b=GROUPS)
        tab_sb = [head.tile([P, T], I32, name="tab0", offset=8 * KIB, align_bytes=64)]
        tab_sb.extend(keep.tile([P, T], I32, name="tab%d" % a, align_bytes=64) for a in range(1, PASSES))
        w1_raw = [keep.tile([P, PASSES, H // 4], I32, name="w1_raw0", align_bytes=64)]
        nc.sync.dma_start(offs_sb[:], offs)
        for quad in range(4):
            (nc.scalar if quad < 2 else nc.sync).dma_start(
                tab_scale[32 * quad : 32 * quad + 4 * PASSES, :].bitcast(I32),
                tab_scales[:, 4 * quad : 4 * quad + 4, :].bitcast(I32),
            )
        for quad in range(4):
            nc.scalar.dma_start(
                w1_scale_raw[32 * quad : 32 * quad + 4].bitcast(I32),
                w1_scales[:, 4 * quad : 4 * quad + 4, :].bitcast(I32).rearrange("a r c -> r a c"),
            )
        nc.sync.dma_start(tab_sb[0][:], tab_view[:, 0, :])
        nc.sync.dma_start(w1_raw[0][:], w1_view[0])
        for a in range(1, PASSES):
            nc.sync.dma_start(tab_sb[a][:], tab_view[:, a, :])
        nc.sync.dma_start(pos1_sb[:], pos1)
        nc.sync.dma_start(pos2_sb[:], pos2)
        make_identity(nc, ident[:])
        nc.scalar.activation(warm[:, 1:2], warm[:, 0:1], ACT.Silu)

        w1_codes = {}
        w1_scale = {}

        def order_codes(copy, codes, b, passes, slots):
            copy(
                codes.rearrange("p a t (q i) -> p a t q i", i=4),
                w1_raw[b][:].bitcast(U32).rearrange("p a (q t i) -> p a t q i", t=SLOTS, i=4)[:, passes, slots],
            )
            for a in range(passes.start, passes.stop):
                for t in range(slots.start, slots.stop):
                    w1_codes[a, SLOTS * b + t] = codes[:, a - passes.start, t - slots.start, :]

        def order_scales(copy, scale, b):
            copy(
                scale[:].rearrange("p a t (q i) -> p a t q i", i=2),
                w1_scale_raw[:].rearrange("p a (b q t i) -> p b a t q i", b=GROUPS, t=SLOTS, i=2)[:, b],
            )
            for a in range(PASSES):
                for t in range(SLOTS):
                    w1_scale[a, SLOTS * b + t] = scale[:, a, t, :]

        codes_head = keep.tile([P, PASSES, SLOTS, P // 2], U32, name="w1_codes_head", align_bytes=64)
        scale_head = keep.tile([P, PASSES, SLOTS, P // 4], U32, name="w1_scale_head", align_bytes=64)
        order_scales(nc.scalar.copy, scale_head, 0)
        for passes in (slice(0, 1), slice(1, PASSES)):
            order_codes(nc.scalar.copy, codes_head[:, passes], 0, passes, slice(0, SLOTS))

        v_words = {}
        h_bank = {}

        def pick_words(a, half):
            if (a, half) == (PASSES - 1, 0):
                v_words[a, half] = keep.tile([P, BANK], U32, name="v2_0", tag="z_woven0", align_bytes=64)
            elif (a, half) == (0, 1):
                v_words[a, half] = shared.tile([P, BANK], U32, name="v0_1", offset=24 * KIB, align_bytes=64)
            else:
                v_words[a, half] = keep.tile([P, BANK], U32, name="v%d_%d" % (a, half), tag="v%d_%d" % (a, half), align_bytes=64)
            nc.vector.tensor_copy(
                v_words[a, half][:], tab_sb[a][:].bitcast(U32).indirect(offs_sb[:, half * BANK // 16 : (half + 1) * BANK // 16])
            )

        def first_product(j, half, a):
            if a == 0:
                h_bank[j, half] = psum.tile([P, BANK], F32, name="bank")
            nc.tensor.matmul_mx(
                out=h_bank[j, half][:],
                lhsT=w1_codes[a, j].bitcast(U8).bitcast(FP4X4),
                lhsT_scale=w1_scale[a, j].bitcast(U8),
                rhs=v_words[a, half][:].bitcast(FP8X4),
                rhs_scale=v_scale[a][:, half * BANK : (half + 1) * BANK],
                start=(a == 0),
                stop=(a == PASSES - 1),
            )

        pick_words(0, 0)
        nc.vector.tensor_copy(v_scale[0][:], tab_scale[:].indirect(offs_sb[:]))
        for a in range(1, PASSES):
            v_scale.append(moved[:, (a - 1) * S : a * S])
            for first in (0, 64):
                nc.sync.dma_start(
                    v_scale[a][first : first + 36, :].bitcast(I32), v_scale[0][first + 4 * a : first + 4 * a + 36, :].bitcast(I32)
                )
        pick_words(0, 1)
        w1_raw.append(head.tile([P, PASSES, H // 4], I32, name="w1_raw1", offset=10 * KIB, align_bytes=64))
        nc.sync.dma_start(w1_raw[1][:], w1_view[1])
        gain_rows = head.tile([P, GROUPS * P], F32, name="gain_rows", offset=13 * KIB, align_bytes=64)
        nc.gpsimd.memset(gain_rows[0 : P - SLOTS, :], 0.0)
        nc.sync.dma_start(
            gain_rows[P - SLOTS : P, :].rearrange("t (g i) -> t g i", i=8),
            gain.rearrange("(g t i) -> t g i", t=SLOTS, i=8),
        )
        for a in range(1, PASSES):
            for half in range(HALVES):
                pick_words(a, half)

        scale_rest = shared.tile([P, PASSES, SLOTS, P // 4], U32, name="w1_scale_rest", offset=16 * KIB, align_bytes=64)
        order_scales(nc.scalar.copy, scale_rest, 1)
        for first, last, offset in ((0, 2, 0), (2, 3, 4 * KIB), (3, 4, 28 * KIB)):
            codes_rest = shared.tile([P, PASSES, last - first, P // 2], U32, name="w1_codes_rest%d" % first, offset=offset, align_bytes=64)
            order_codes(nc.scalar.copy, codes_rest[:], 1, slice(0, PASSES), slice(first, last))

        w2_view = w2.rearrange("(b q s i) (g n) -> g b s q i n", b=GROUPS, s=SLOTS, i=8, g=GROUPS)
        woven_first = keep.tile([P, SLOTS, GROUPS, 16, 8, SLOTS], BF16, name="w2_woven_first", align_bytes=64)
        for b in range(GROUPS):
            raw_first = head.tile([P, SLOTS, H // GROUPS], F32, name="w2_raw_first%d" % b, offset=(2 + 12 * b) * KIB, align_bytes=64)
            for s in range(SLOTS):
                nc.sync.dma_start(raw_first[:, s, :], w2_view[0, b, s])
            columns = raw_first[:].rearrange("p s (q t i) -> p t q i s", t=SLOTS, i=8)
            for t in range(SLOTS):
                nc.gpsimd.tensor_scalar(woven_first[:, t, b], columns[:, t], 1.0, 0.0, ALU.mult, ALU.add)
        raw_rest = keep.tile([P, SLOTS, GROUPS, H // GROUPS], F32, name="w2_raw_rest", tag="tab1", align_bytes=64)
        for b in range(GROUPS):
            for s in range(SLOTS):
                nc.sync.dma_start(raw_rest[:, s, b, :], w2_view[1, b, s])
        rest_columns = raw_rest[:].rearrange("p s b (q t i) -> p t (b q) s i", t=SLOTS, i=8)

        h_sb = [keep.tile([P, S], F32, name="h%d" % j) for j in range(TILES)]
        ref_all = keep.tile([P, TILES, M], F32, name="ref_all")
        ref_group = [ref_all[:, b * SLOTS : (b + 1) * SLOTS, :] for b in range(GROUPS)]
        ref = [ref_all[:, j, :] for j in range(TILES)]
        z_codes = [keep.tile([P, M], U32, name="z_codes%d" % b, tag="v%d_0" % b, align_bytes=64) for b in range(GROUPS)]
        z_scale = [keep.tile([P, M], U8, name="z_scale%d" % b, align_bytes=64) for b in range(GROUPS)]
        z_woven = [keep.tile([P, M * SLOTS // 2], U32, name="z_woven%d" % b, align_bytes=64) for b in range(GROUPS)]
        z_woven = [woven[:].bitcast(BF16).rearrange("p (m t) -> p m t", t=SLOTS) for woven in z_woven]
        bounded = {}

        def evacuate(j, half):
            copy = nc.vector.tensor_copy if (j, half) == (0, 1) else nc.scalar.copy
            copy(h_sb[j][:, half * BANK : (half + 1) * BANK], h_bank[j, half][:])

        def pick_ref(j):
            nc.vector.tensor_copy(ref[j], h_sb[j][:].indirect(pos1_sb[:]))

        def bound(b, cut):
            if b == 0:
                bounded[b, cut] = shared.tile([P, CW, SLOTS], F32, name="bounded0_%d" % cut, offset=4 * KIB * cut, align_bytes=64)
            elif cut == 0:
                bounded[b, cut] = shared.tile([P, CW, SLOTS], F32, name="bounded1_0", offset=20 * KIB, align_bytes=64)
            else:
                bounded[b, cut] = keep.tile([P, CW, SLOTS], F32, name="bounded1_1")
            nc.scalar.activation(
                bounded[b, cut][:].rearrange("p (c i) t -> p c t i", i=4),
                ref_group[b][:, :, cut * CW : (cut + 1) * CW].rearrange("p t (c i) -> p c t i", i=4),
                ACT.Tanh,
            )

        def weigh(b, cut):
            nc.vector.tensor_tensor(
                z_woven[b][:, cut * CW : (cut + 1) * CW, :],
                bounded[b, cut][:],
                gain_sb[:, b * SLOTS : (b + 1) * SLOTS].unsqueeze(1).to_broadcast([P, CW, SLOTS]),
                ALU.mult,
            )

        def quantize_z(b, lo, hi):
            nc.vector.quantize_mx(
                out=z_codes[b][:, lo * CW : hi * CW].bitcast(FP8X4),
                scales=z_scale[b][:, lo * CW : hi * CW],
                in_=z_woven[b][:, lo * CW : hi * CW, :].rearrange("p m t -> p (m t)"),
            )

        w2_codes = {}
        w2_scale = {}

        def quantize_w2(woven, codes, first, count):
            scale = keep.tile([P, count * GROUPS * P], U8, name="w2_scale%d" % first, align_bytes=64)
            nc.vector.quantize_mx(
                out=codes[:].bitcast(FP8X4),
                scales=scale[:],
                in_=woven,
            )
            for k in range(count):
                w2_codes[first + k] = codes[:, k * GROUPS * P : (k + 1) * GROUPS * P]
                w2_scale[first + k] = scale[:, k * GROUPS * P : (k + 1) * GROUPS * P]

        steps = [(a, half) for a in range(PASSES) for half in range(HALVES)]
        for a, half in steps[:HALVES]:
            for j in range(SLOTS):
                first_product(j, half, a)
        for pair in range(SLOTS // 2):
            for a, half in steps[HALVES:]:
                for j in (2 * pair, 2 * pair + 1):
                    first_product(j, half, a)
                    if a == PASSES - 1:
                        evacuate(j, half)
            for j in (2 * pair, 2 * pair + 1):
                pick_ref(j)
        for j in range(SLOTS, TILES):
            for half in range(HALVES):
                for a in range(PASSES):
                    first_product(j, half, a)
                evacuate(j, half)
            if j == SLOTS:
                gain_sb = keep.tile([P, TILES], F32, name="gain_sb")
                gain_bank = psum.tile([P, BANK], F32, name="bank")
                for b in range(GROUPS):
                    nc.tensor.transpose(gain_bank[:, b * P : (b + 1) * P], gain_rows[:, b * P : (b + 1) * P], ident[:])
                nc.scalar.copy(
                    gain_sb[:].rearrange("p (b t) -> p b t", t=SLOTS),
                    gain_bank[:, 0 : GROUPS * P].rearrange("p (b c) -> p b c", b=GROUPS)[:, :, P - SLOTS : P],
                )
            pick_ref(j)
            if j in (5, 6):
                bound(0, j - 5)
        for cut in range(CUTS):
            weigh(0, cut)
        woven_rest = shared.tile([P, SLOTS, GROUPS * 16, 8, SLOTS], BF16, name="w2_woven_rest", offset=28 * KIB, align_bytes=64)

        def weave_pair(pair):
            slots = slice(2 * pair, 2 * pair + 2)
            nc.scalar.copy(woven_rest[:, slots].rearrange("p k c i s -> p k c s i"), rest_columns[:, slots])

        codes_first = shared.tile([P, SLOTS * GROUPS * P], U32, name="w2_codes_first", offset=4 * KIB, align_bytes=64)
        quantize_w2(woven_first[:].rearrange("p t b q i s -> p (t b q i s)"), codes_first, 0, SLOTS)
        quantize_z(0, 0, 2)
        for cut in range(CUTS):
            bound(1, cut)
            weigh(1, cut)
        for cut in range(CUTS):
            quantize_z(1, cut, cut + 1)
        for pair in range(2):
            weave_pair(pair)
        codes_rest = keep.tile([P, SLOTS * GROUPS * P], U32, name="w2_codes_rest", align_bytes=64)
        quantize_w2(woven_rest[:].rearrange("p t c i s -> p (t c i s)"), codes_rest, SLOTS, SLOTS)

        out_view = out.rearrange("(b q t i) m -> b t q i m", b=GROUPS, t=SLOTS, i=8)
        y_bank = {}
        turns = {}
        turned = {}
        cosine = {}

        def second_product(u):
            for j in RUNS[u]:
                y_bank[j] = psum.tile([P, BANK], F32, name="bank")
                for b in range(GROUPS):
                    nc.tensor.matmul_mx(
                        out=y_bank[j][:],
                        lhsT=w2_codes[j][:, b * P : (b + 1) * P].bitcast(FP8X4),
                        lhsT_scale=w2_scale[j][:, b * P : (b + 1) * P],
                        rhs=z_codes[b][:].bitcast(FP8X4),
                        rhs_scale=z_scale[b][:],
                        start=(b == 0),
                        stop=(b == GROUPS - 1),
                    )

        def measure(u):
            if u == 0:
                turns[u] = shared.tile([P, 1, M], F32, name="turns_first", offset=12 * KIB, align_bytes=64)
            else:
                turns[u] = head.tile([P, len(RUNS[u]), M], F32, name="turns%d" % u, offset=(14 + 2 * RUNS[u][0]) * KIB, align_bytes=64)
            for k, j in enumerate(RUNS[u]):
                nc.scalar.activation(turns[u][:, k, :], y_bank[j][:], ACT.Abs, scale=1.0 / (2.0 * math.pi))

        def reduce_angle(u):
            shape = [P, len(RUNS[u]), M]
            if u == 1:
                whole = shared.tile(shape, I32, name="whole_second", offset=12 * KIB, align_bytes=64)
            else:
                whole = ring.tile(shape, I32, name="whole")
            nc.scalar.activation(whole[:].bitcast(U32), turns[u][:], ACT.Copy, bias=-0.25)
            nc.vector.tensor_tensor(turns[u][:], turns[u][:], whole[:], ALU.subtract)

        def sine(u):
            cosine[u] = ring.tile([P, len(RUNS[u]), M], F32, name="cosine")
            nc.scalar.activation(cosine[u][:], turns[u][:], ACT.Sin, scale=-2.0 * math.pi, bias=0.5 * math.pi)

        def turn_tile(u, k):
            j = RUNS[u][k]
            turned[j] = head.tile([P, M], F32, name="turned%d" % j, offset=2 * j * KIB, align_bytes=64)
            nc.vector.tensor_tensor(turned[j][:], h_sb[j][:].indirect(pos2_sb[:]), cosine[u][:, k, :], ALU.mult)

        def turn_rot(u):
            for k in range(len(RUNS[u])):
                turn_tile(u, k)

        def lean_ref(u):
            for j in RUNS[u]:
                nc.vector.tensor_tensor(ref[j], y_bank[j][:], ref[j], ALU.mult)

        across = {}
        flipped = {}
        blocks = [slice(c * P, (c + 1) * P) for c in range(M // P)]

        def add_across(j):
            across[j] = psum.tile([P, BANK], F32, name="bank")
            for block in blocks:
                nc.tensor.matmul(across[j][:, block], lhsT=turned[j][:, block], rhs=ident[:], is_transpose=True, start=True, stop=False)
                nc.tensor.matmul(across[j][:, block], lhsT=ref[j][:, block], rhs=ident[:], is_transpose=True, start=False, stop=True)
            flipped[j] = head.tile([P, BANK], F32, name="flipped%d" % j, offset=(16, 26, 28, 20, 22)[j] * KIB, align_bytes=64)
            nc.scalar.copy(flipped[j][:], across[j][:])

        def turn_back(j):
            back = psum.tile([P, BANK], F32, name="bank")
            for block in blocks:
                nc.tensor.transpose(back[:, block], flipped[j][:, block], ident[:])
            nc.scalar.copy(ref[j], back[:])
            store(nc.scalar, j)

        def store(queue, j):
            queue.dma_start(out_view[j // SLOTS, j % SLOTS], ref[j])

        runs = len(RUNS)
        for u in range(runs):
            second_product(u)
        measure(0)
        reduce_angle(0)
        lean_ref(0)
        for u in range(runs - 2):
            measure(u + 1)
            sine(u)
            turn_rot(u)
            reduce_angle(u + 1)
            lean_ref(u + 1)
        measure(runs - 1)
        reduce_angle(runs - 1)
        lean_ref(runs - 1)
        add_across(0)
        sine(runs - 2)
        turn_back(0)
        sine(runs - 1)
        turn_rot(runs - 2)
        add_across(1)
        for j in range(2, TENSOR_SUMS):
            add_across(j)
            turn_back(j - 1)
        turn_back(TENSOR_SUMS - 1)
        for j in range(TENSOR_SUMS, TILES):
            nc.vector.tensor_tensor(ref[j], turned[j][:], ref[j], ALU.add)
            store(nc.sync, j)
            if j - TENSOR_SUMS < len(RUNS[-1]):
                turn_tile(runs - 1, j - TENSOR_SUMS)
